import numpy as np, ml_dtypes
CORES = [13,21,141,149]
N = 4
BF = ml_dtypes.bfloat16
def gentries(a):
    return np.ascontiguousarray(a.reshape(8, 16, -1).transpose(0, 2, 1)).reshape(8, -1)
def gtable(e):
    e = np.asarray(e); return np.ascontiguousarray(e.reshape(8, -1, 16).transpose(0, 2, 1)).reshape(128, -1).astype(np.int32)
V, L, A, S, C, RO = 4096, 1280, 256, 128, 4, 3
def ringed(o, s):
    n = np.empty(V, np.int64); f = np.roll(o, -1); f[np.append(s[1:], V) - 1] = o[s]; n[o] = f
    return n
def longrings(rng):
    n = np.empty((N, 8, V), np.int64)
    for q in range(N):
        for g in range(8):
            m = int(rng.integers(1, 7)); s = (1 + rng.permutation(15)[:m - 1]) * (V // 16) + rng.integers(0, V // 32, m - 1)
            n[q, g] = ringed(rng.permutation(V), np.sort(np.concatenate([np.zeros(1, np.int64), s])))
    return n
def parts(rng):
    lev = np.array([64, 128, 256], np.float32)
    x = (rng.random((N, 8, 16, V), dtype=np.float32) * rng.choice(lev, (N, 8, 1, V))).astype(np.int32)
    z = (rng.random((N, 8, 16, L), dtype=np.float32) * rng.choice(lev, (N, 8, 1, L))).astype(np.int32)
    w = rng.integers(0, 256, (N, 8, 16, 1)); w[:, :, 0] |= 1
    return x, z, w
def turns(z, w):
    return 1 + (np.sum(w * z, axis=2) & (C - 1))
def stand(n, u, c):
    back = np.argsort(n, axis=-1)
    for i in range(C): u = np.where(i < c, np.take_along_axis(back, u, 2), u)
    return u
def pack(x, z, w, n, c):
    return {"cards": x.reshape(N, 128, V).astype(np.float32).astype(BF), "z0": z.reshape(N, 128, L).astype(np.float32).astype(BF), "wt": np.ascontiguousarray(w.reshape(N, 128, 1)).astype(np.int32),
            "cur": np.stack([gtable(a) for a in c]), "nx": n.astype(np.int32)}
def setup_inputs(rng):
    x, z, w = parts(rng); size = rng.permutation(np.tile(np.array([V, 2 * A, A // 2, A // 4]), 2 * N)).reshape(N, 8, 1)
    pool = np.argsort(rng.random((N, 8, V)), axis=-1)
    return pack(x, z, w, longrings(rng), np.take_along_axis(pool, (rng.random((N, 8, L)) * size).astype(np.int64), 2))
def setup_inputs_room(rng):
    x, z, w = parts(rng); n = longrings(rng); u = np.empty((N, 8, L), np.int64)
    many = rng.choice(np.array([0, 2, S - 2, S, S + 2, A]), (N, 8)); many[0] = (S, S + 2, A, S - 2, 2, 0, S, S + 2)
    for g, m in enumerate((S, S, S - 2, S + 2, A, A, 0, 2)): many[1 + g % (N - 1), (g + 1) % 8] = m
    w[0, 2] = 0
    for q in range(N):
        for g in range(8):
            p = rng.permutation(V); k = p[:A].reshape(A // 2, 2).copy(); rest = rng.permutation(A // 2)[int(many[q, g]) // 2:]
            if (q, g) == (0, 5):
                k[np.arange(A // 2), rng.integers(0, 2, A // 2)] = p[A]; k[int(rng.integers(0, A // 2))] = p[A]
            else:
                b = int(rng.integers(0, len(rest) // 2 + 1)); k[rest[b:2 * b], 0] = k[rest[:b], 1]; k[rest[2 * b:], 1] = k[rest[2 * b:], 0]
            u[q, g] = np.concatenate([k.reshape(-1), p[rng.integers(0, 2 * A, L - A)]])
    return pack(x, z, w, n, stand(n, u, turns(z, w)))
def setup_inputs_ties(rng):
    x, z, w = parts(rng); i = np.arange(16).reshape(1, 1, 16, 1)
    h = ((5 * i + rng.integers(0, 16, (N, 8, 1, V))) & 15) < rng.integers(7, 11, (N, 8, 1, V))
    x[:, ::2] = np.where(h, 255, 0)[:, ::2]; z[:, ::2] = np.minimum(z[:, ::2], 254)
    base = rng.choice(np.array([0, 100, 253]), (N, 4, 1, 1)); base[0, :, 0, 0] = (0, 100, 253, 0)
    x[:, 1::2] = base + rng.integers(0, 3, (N, 4, 16, V)); z[:, 1::2] = base + rng.integers(0, 2, (N, 4, 16, L))
    w[:, 2] = 0; w[:, 3] = 255; w[:, 4] = C * rng.integers(0, 256 // C, (N, 16, 1)); w[:, 5, 1:] = 0
    w[:, 7] = 0; w[:, 7, 0] = 1; z[:, 7, 0] |= C - 1
    return pack(x, z, w, longrings(rng), rng.integers(0, V, (N, 8, L)))
def setup_inputs_close(rng):
    x, z, w = parts(rng); n = np.empty((N, 8, V), np.int64); u = np.empty((N, 8, L), np.int64)
    w[:, 3::4, 0] = 1; w[:, 3::4, 1:] = C * rng.integers(0, 256 // C, (N, 2, 15, 1)); z[:, 3::4, :8, :A] = 255
    for q in range(N):
        for g in range(8):
            o = rng.permutation(V); a = int(rng.integers(0, V)); k = rng.permutation(A)
            if g % 4 == 0:
                o = np.arange(V); a = 1024 * int(rng.integers(0, V // 1024)) + int(rng.integers(240, 273))
            if g % 4 == 1: k = np.arange(A)
            if g % 4 == 3:
                t = 2 * rng.permutation(A // 2).reshape(2, A // 4); k = np.stack([t[0], t[1], t[0] + 1, t[1] + 1], axis=1).reshape(-1)
                i = o[(a + t[0] + 1) % V]; x[q, g, 0, i] = (x[q, g, 0, i] | (C - 1)) - 1
                i = o[(a + t[1] + 2) % V]; x[q, g, 0, i] = x[q, g, 0, i] | (C - 1)
            n[q, g] = ringed(o, np.zeros(1, np.int64))
            u[q, g] = o[(a + np.concatenate([k, rng.integers(-2 * C, A, L - A)])) % V]
    return pack(x, z, w, n, stand(n, u, turns(z, w)))
def setup_inputs_rings(rng):
    x, z, w = parts(rng); n = np.empty((N, 8, V), np.int64); c = rng.integers(0, V, (N, 8, L))
    for q in range(N):
        for g in range(8):
            m = (1, 2, 3, C, C + 1, 0, V, 7)[(q + g) % 8]; o = np.arange(V) if m == V else rng.permutation(V)
            n[q, g] = ringed(o, np.arange(0, V, m) if m > 0 else np.unique(np.concatenate([np.zeros(1, np.int64), rng.integers(0, V, V // 8)])))
    c[:, :, :8] = rng.choice(np.array([0, V - 1]), (N, 8, 8)); c[:, :, A - 2] = 0; c[:, :, A - 1] = V - 1; c[:, :, A] = 0; c[:, :, L - 1] = V - 1
    return pack(x, z, w, n, c)
def setup_inputs_spread(rng):
    x, z, w = parts(rng)
    def uneven(k):
        a = np.minimum((np.exp2(8 * rng.random((N, 8, 1, k))) * rng.random((N, 8, 16, k), dtype=np.float32)).astype(np.int32), 255); e = rng.random((N, 8, 1, k))
        return np.where(e < 0.04, 0, np.where(e > 0.96, 255, a))
    x = uneven(V); z = uneven(L); w = np.minimum(np.exp2(8 * rng.random((N, 8, 16, 1))).astype(np.int64), 255)
    return pack(x, z, w, longrings(rng), (V * rng.random((N, 8, L)) ** 3).astype(np.int64))
def check_inputs(d):
    bad = []
    for k in ("cards", "z0"):
        a = d[k].astype(np.float32)
        if not (np.min(a) >= 0 and np.max(a) <= 255 and np.all(np.floor(a) == a)): bad.append("whole numbers of " + k)
    for k, hi in (("wt", 255), ("cur", V - 1)):
        if np.min(d[k]) < 0 or np.max(d[k]) > hi: bad.append("range of " + k)
    if not np.all(np.sort(d["nx"], axis=-1) == np.arange(V)): bad.append("each row of nx holds every card once")
    return bad
def reference(cards, z0, wt, cur, nx):
    x = cards.astype(np.float32).astype(np.int32).reshape(N, 8, 16, V); z = z0.astype(np.float32).astype(np.int32).reshape(N, 8, 16, L)
    w = wt.astype(np.int32).reshape(N, 8, 16, 1); nxt = nx.astype(np.int64); v = np.stack([gentries(a) for a in cur]).astype(np.int64)
    for rnd in range(RO):
        c = 1 + (np.sum(w * z, axis=2) & (C - 1))
        for s in range(C):
            go = s < c
            v = np.where(go, np.take_along_axis(nxt, v, 2), v)
            cd = np.take_along_axis(x, v[:, :, None, :], 3)
            up = go & (np.add.reduce((cd > z).astype(np.int32), axis=2) >= 9)
            z = np.where(up[:, :, None, :], (z + cd) >> 1, z)
        u = v; v = np.take_along_axis(nxt, u, 2)
        z = np.abs(z - np.take_along_axis(x, v[:, :, None, :], 3))
        a = u[:, :, :A]; b = v[:, :, :A]
        key = np.arange(N * 8).reshape(N, 8, 1) * V + a
        cnt = np.bincount(key.reshape(-1), minlength=N * 8 * V).reshape(N, 8, V)
        alone = (np.take_along_axis(cnt, a, 2) == 1).reshape(N, 8, A // 2, 2)
        cut = np.repeat(np.all(alone, axis=3), 2, axis=2)
        i, g, j = np.nonzero(cut)
        nxt[i, g, a[i, g, j]] = b[i, g, j ^ 1]
        if rnd < RO - 1:
            top = [[b[q, h][cut[q, h]][:S] for h in range(8)] for q in range(N)]
            sent = [[x[q, h][:, top[q][h]] for h in range(8)] for q in range(N)]
            for q in range(N):
                for h in range(8):
                    r = (q + 1 + (h + rnd) % (N - 1)) % N; k = (h + 1) % 8; m = min(len(top[q][h]), len(top[r][k]))
                    x[r, k][:, top[r][k][:m]] = sent[q][h][:, :m]
    return {"yz": z.reshape(N, 128, L).astype(np.float32).astype(BF), "yc": v.astype(np.float32), "yn": nxt.astype(np.float32)}

@@ -1,0 +1,628 @@
+import numpy as np
+from concourse.bass import DstId, RemoteDMATransfer
+from concourse.mybir import dt, AluOpType, AxisListType, ActivationFunctionType
+
+ALU = AluOpType
+ACT = ActivationFunctionType
+V, L, A, RO = 4096, 1280, 256, 3
+PW = 144
+BIG = float(2 ** 33)
+M1 = 1.5 * 2 ** 23
+CH = ((0, 256), (256, 768), (768, 1280))
+CFG = {"iters": 1500, "polish": 5000, "seed": 2, "look": 0.01}
+PLANS = (((1.0, 1.0, 1.56, 3.8, 0.5), 90.0, 1.0), ((1.0, 1.0, 1.15, 2.0, 0.5), 60.0, 1.2), ((1.0, 1.0, 2.0, 5.5, 0.5), 120.0, 0.9))
+
+_bf, _f, _i, _u = "bfloat16", "float32", "int32", "uint16"
+_SB = {
+    _bf: {"crd": V, "pat": V, "bn0": V, "bn1": V + A, "bn2": V + A, "bn3": V + A, "w0": V, "w1": V + A, "w2": V + A, "r256": 16, "pc": 128,
+          "ih": 128, "ione": 128, "ipen": 128, "gm": 720, "bkp": 1024, "bkn": 1024, "bo": 128, "bw": 128, "sh": 384, "z": L, "dh": L,
+          "pb": 10 * L, "sg": L, "ml": 192, "pen": 576, "eq": 4096, "cutp": 128, "cutq": 128, "cutr": 128, "cum": 128, "rr": 128,
+          "pay0": 528, "pay1": 528, "jt": 528, "vnew": 256, "land": 6 * PW},
+    _f: {"curf": 80, "curg": 80, "col": 32, "rsel": 16, "gsel": 8, "ca": 16, "two": 16, "pw": 16, "pw2": 16, "iom": 128, "iog": 128, "jl": 32,
+         "sw": 128, "idf": 128, "cm": 320, "xf": 320, "vl": 16, "kf": 16, "kg": 16, "k1": 16, "k2": 16, "k3": 16, "k4": 16, "k5": 16, "k6": 16,
+         "ycs": 80, "yns": 256},
+    _i: {"nxi": 256, "curi": 80, "cura": 80, "curb": 80, "wti": 8, "ip": 8, "iq": 8, "ci": 192, "cj": 192, "li": 80, "lj": 80},
+    _u: {"nxl": 256, "xa": 192, "xb": 768, "ipay": 16, "itg": 32, "ijn": 16},
+    "float16": {"vw": 256},
+}
+SCRATCH = {k: ("sbuf", [128, n], d) for d, b in _SB.items() for k, n in b.items()}
+SCRATCH.update({k: ("psum", [128, 512], _f) for k in ("d0", "d1", "d2", "c0", "c1", "c2", "lb", "xk")})
+SEMAPHORES = ["nv", "ns", "nt", "ng", "arr0", "arr1", "hin0", "hin1", "sent0", "sent1"] + ["dq%d" % k for k in range(20)]
+HE = 4
+
+
+def routes(T, topo):
+    out = []
+    n = len(T.cores)
+    for q, c in enumerate(T.cores):
+        used, row = [], []
+        for e in range(n - 1):
+            r = (q + 1 + e) % n
+            d = T.cores[r]
+            if topo.may_write(c, d):
+                row.append((r, None))
+                continue
+            able = [h for h in topo.cores_of(c) if h not in T.cores and topo.may_write(h, d) and h not in used]
+            able.sort(key=lambda h: topo.die(h) != topo.die(c))
+            used.append(able[0])
+            row.append((r, able[0]))
+        out.append(row)
+    return out
+
+
+def as_mask(engs):
+    return sum(1 << e for e in engs)
+
+
+def helper_program(g, core, T, topo, e, r):
+    d = T.cores[r]
+    engs = topo.engines(core, d)
+    rid, pid = topo.addr(d, core)
+    for t in range(RO - 1):
+        g.wait_ge(T.sem["hin%d" % t], HE)
+        s = (3 * t + e) * PW
+        g.remote_dma(T.land[:, s:s + PW], T.land[:, s:s + PW], T.sem["arr%d" % t], T.sem["sent%d" % t], pid, rid, as_mask(engs))
+    for t in range(RO - 1):
+        g.wait_ge(T.sem["sent%d" % t], len(engs))
+
+
+def build(T, topo, core, rank):
+    ops, last_w, readers = [], {}, {}
+
+    def add(name, alts, r=(), w=(), bank=None, lat=0.0, dma=False, after=(), ext=None):
+        i = len(ops)
+        deps = set(after)
+        for k in list(r) + list(w):
+            if k in last_w:
+                deps.add(last_w[k])
+        for k in w:
+            deps.update(readers.get(k, ()))
+        for k in r:
+            readers.setdefault(k, []).append(i)
+        for k in w:
+            last_w[k] = i
+            readers[k] = []
+        deps.discard(i)
+        ops.append({"n": name, "alts": alts, "deps": sorted(deps), "bank": bank, "lat": lat, "dma": dma, "ext": ext, "i": i})
+        return i
+
+    def cv(n, f=1.0):
+        return (30.0, max(64.0, n * f), 0, 0, 0)
+
+    def ts(name, out, in0, s1, s2, op0, op1, n, r, w, bank=None, f=1.0):
+        if op1 is None:
+            fn = lambda g: g.vector.tensor_scalar(out, in0, s1, None, op0)
+        else:
+            fn = lambda g: g.vector.tensor_scalar(out, in0, s1, s2, op0, op1)
+        return add(name, {"v": (cv(n, f), fn)}, r, w, bank)
+
+    def tt(name, out, in0, in1, op, n, r, w, bank=None):
+        return add(name, {"v": (cv(n, 1.0 if bank else 2.0), lambda g: g.vector.tensor_tensor(out, in0, in1, op))}, r, w, bank)
+
+    def cp(name, out, in_, n, r, w, bank=None, both=False):
+        alts = {"v": (cv(n), lambda g: g.vector.tensor_copy(out, in_))}
+        if both:
+            alts["s"] = (cv(n), lambda g: g.scalar.activation(out, in_, ACT.Copy))
+        return add(name, alts, r, w, bank)
+
+    def lin(name, out, in_, sc, bi, n, r, w, bank=None, f=1.0):
+        alts = {"v": (cv(n, f), lambda g: g.vector.tensor_scalar(out, in_, sc, bi, ALU.mult, ALU.add)),
+                "s": (cv(n), lambda g: g.scalar.activation(out, in_, ACT.Identity, bias=bi, scale=sc))}
+        return add(name, alts, r, w, bank)
+
+    def ms(name, ap, c, n, w):
+        return add(name, {"v": (cv(n, 0.5), lambda g: g.vector.memset(ap, c))}, (), w)
+
+    def red(name, out, in_, r, w):
+        return add(name, {"v": (cv(16), lambda g: g.vector.tensor_reduce(out, in_, AxisListType.X, ALU.add))}, r, w)
+
+    def scan(name, out, a, b, init, op0, op1, r, w):
+        return add(name, {"v": (cv(64), lambda g: g.vector.tensor_tensor_scan(out, a, b, init, op0, op1))}, r, w)
+
+    def gather(name, out, win, off, n, r, w):
+        alts = {"v": ((55, 0, n, 0, 0), lambda g: g.vector.tensor_copy(out, win.indirect(off))),
+                "s": ((70, 0, n, 0, 0), lambda g: g.scalar.activation(out, win.indirect(off), ACT.Copy))}
+        return add(name, alts, r, w)
+
+    def gather_tt(name, out, win, off, in1, op, n, r, w):
+        return add(name, {"v": ((55, 0, n, 0, 0), lambda g: g.vector.tensor_tensor(out, win.indirect(off), in1, op))}, r, w)
+
+    def scatter(name, win, off, in_, n, r, w):
+        return add(name, {"v": ((55, 0, 0, n, 0), lambda g: g.vector.tensor_copy(win.indirect(off), in_))}, r, w)
+
+    def mm(name, items, r, w, bank, after=(), x=1):
+        def fn(g):
+            for o, a, b, s0, s1, _n in items:
+                ins = g.tensor.matmul(o, a, b, s0, s1)
+            return ins
+        return add(name, {"t": ((20, 0, 0, 0, x * sum(max(64, it[5]) for it in items)), fn)}, r, w, bank, after=after)
+
+    def dma(name, q, out, in_, nbytes, r, w):
+        fn = (lambda g: g.sync.dma_start(out, in_)) if q == "y" else (lambda g: g.scalar.dma_start(out, in_))
+        return add(name, {q: ((100.0, 0, 0, 0, 0), fn)}, r, w, lat=1800 + nbytes / 200.0, dma=True)
+
+    def iota(name, out, pattern, base, cm, n, w, integer=False):
+        if integer:
+            fn = lambda g: g.iota(out, pattern, base, cm)
+        else:
+            fn = lambda g: g.iota(out, pattern, base, cm, allow_small_or_imprecise_dtypes=True)
+        return add(name, {"g": ((150, 2.0 * n, 0, 0, 0), fn)}, (), w)
+
+    col = lambda k: T.col[:, k:k + 1]
+    GF, RF, PF, SHF, PARF, WT, WP, W4, SWF, KB, OFF, M3, TMP = 0, 1, 2, 3, 4, 5, 6, 7, 8, 9, 10, 14, 17
+    NM1, NQ, KC = col(TMP + 7), col(TMP + 8), col(TMP + 9)
+    gm = lambda fam, a: T.gm[:, fam * 144 + 15 - a: fam * 144 + 15 - a + 128]
+    GP, GT, GC, GW, G8 = 0, 1, 2, 3, 4
+
+    dma("ld_nx", "y", T.nxi[:, :], T.nx[:], 131072, (), ["nxi"])
+    dma("ld_cur", "y", T.curi[:, :], T.cur[:], 40960, (), ["curi"])
+    dma("ld_c0", "s", T.crd[:, 0:2048], T.cards[:, 0:2048], 1000000, (), ["crd0"])
+    dma("ld_c1", "s", T.crd[:, 2048:V], T.cards[:, 2048:V], 1000000, (), ["crd1"])
+    dma("ld_wt", "y", T.wti[:, 0:1], T.wt[:], 10000, (), ["wti"])
+    dma("ld_z", "y", T.z[:, :], T.z0[:], 600000, (), ["z0", "z1", "z2"])
+
+    iota("ip", T.ip[:, 0:2], [[16, 2]], 0, 1, 2, ["ip"], True)
+    iota("iom", T.iom[:, :], [[1, 128]], 0, 0, 128, ["iom"])
+    iota("iog", T.iog[:, :], [[1, 8], [0, 16]], 0, 0, 128, ["iog"])
+    iota("jl", T.jl[:, :], [[3824, 2], [16, 16]], 272, 0, 32, ["jl"])
+    iota("pc", T.pc[:, :], [[1, 128]], 129, 0, 128, ["pc"])
+    ts("ir", T.iq[:, 1:2], T.ip[:, 0:1], 15, None, ALU.bitwise_and, None, 1, ["ip"], ["iq1"])
+    cp("rf", col(RF), T.iq[:, 1:2], 1, ["iq1"], ["rf"])
+    ts("r256", T.r256[:, :], T.iom[:, 0:16], col(RF), 256.0, ALU.is_equal, ALU.mult, 16, ["iom", "rf"], ["r256"])
+    ms("pat0", T.pat[:, 0:1], 0.0, 1, ["pat"])
+    for k in range(11):
+        n = 1 << k
+        ts("pat%d" % k, T.pat[:, n:2 * n], T.pat[:, 0:n], T.r256[:, k:k + 1], None, ALU.add, None, n, ["pat", "r256"], ["pat"], f=0.5)
+    lin("patA", T.pat[:, 2048:3392], T.pat[:, 0:1344], 1.0, T.r256[:, 11:12], 1344, ["pat", "r256"], ["patA"], f=0.5)
+    lin("patB", T.pat[:, 3392:V], T.pat[:, 1344:2048], 1.0, T.r256[:, 11:12], 704, ["pat", "r256"], ["patB"], f=0.5)
+    ts("ig", T.iq[:, 0:1], T.ip[:, 0:1], 4, None, ALU.arith_shift_right, None, 1, ["ip"], ["iq0"])
+    ts("ish", T.iq[:, 3:4], T.ip[:, 1:2], 127, None, ALU.bitwise_and, None, 1, ["ip"], ["iq3"])
+    ts("ipar", T.iq[:, 4:5], T.ip[:, 0:1], 1, None, ALU.bitwise_and, None, 1, ["ip"], ["iq4"])
+    cp("gf", col(GF), T.iq[:, 0:1], 1, ["iq0"], ["gf"])
+    cp("pf", col(PF), T.ip[:, 0:1], 1, ["ip"], ["pf"])
+    cp("shf", T.col[:, SHF:SHF + 2], T.iq[:, 3:5], 2, ["iq3", "iq4"], ["shf", "parf"])
+    cp("w4", col(W4), T.wti[:, 0:1], 1, ["wti"], ["w4"])
+    ts("rsel", T.rsel[:, :], T.iom[:, 0:16], col(RF), None, ALU.is_equal, None, 16, ["iom", "rf"], ["rsel"])
+    ts("gsel", T.gsel[:, :], T.iom[:, 0:8], col(GF), None, ALU.is_equal, None, 8, ["iom", "gf"], ["gsel"])
+    ms("two", T.two[:, :], 2.0, 16, ["two"])
+    scan("pw", T.pw[:, :], T.two[:, :], T.two[:, :], 1.0, ALU.mult, ALU.max, ["two"], ["pw"])
+    tt("pwy", T.pw2[:, :], T.pw[:, :], T.rsel[:, :], ALU.mult, 16, ["pw", "rsel"], ["pw2"])
+    red("wt0", col(TMP), T.pw2[:, :], ["pw2"], ["tmp"])
+    lin("wt", col(WT), col(TMP), 1.0 / 512, 0.0, 1, ["tmp"], ["wt"])
+    ts("wp0", col(TMP + 1), col(RF), 8.0, 16.0 - 1.0 / 256, ALU.is_lt, ALU.mult, 1, ["rf"], ["tmp1"])
+    ts("wp", col(WP), col(TMP + 1), 1.0 / 256, col(WT), ALU.add, ALU.mult, 1, ["tmp1", "wt"], ["wp"])
+    ms("gm", T.gm[:, :], 0.0, 720, ["gm%d" % k for k in range(5)])
+    for fam, sc, key in ((GP, col(WP), "wp"), (GW, col(W4), "w4"), (GC, -BIG, "gf"), (G8, 0.125, "gf"), (GT, col(WT), "wt")):
+        lin("gm%d" % fam, T.gm[:, fam * 144 + 15:fam * 144 + 143:16], T.gsel[:, :], sc, 0.0, 8, ["gsel", key], ["gm%d" % fam])
+    ts("bo", T.bo[:, :], T.iog[:, :], col(GF), None, ALU.is_equal, None, 128, ["iog", "gf"], ["bo"])
+    lin("bw", T.bw[:, :], T.bo[:, :], col(WP), 0.0, 128, ["bo", "wp"], ["bw"], f=0.5)
+    ts("ih", T.ih[:, :], T.iom[:, :], col(PF), 0.5, ALU.is_equal, ALU.mult, 128, ["iom", "pf"], ["ih"])
+    for nm, sc in (("ione", 2.0), ("idf", 2.0), ("ipen", -2.0 * BIG)):
+        lin(nm, T[nm][:, :], T.ih[:, :], sc, 0.0, 128, ["ih"], [nm], f=0.5)
+    ts("ca", T.ca[:, 0:8], T.rsel[:, 0:8], T.rsel[:, 14:15], None, ALU.subtract, None, 8, ["rsel"], ["ca"])
+    lin("cb", T.ca[:, 8:16], T.rsel[:, 0:8], -1.0, T.rsel[:, 15:16], 8, ["rsel"], ["cb"])
+    for a in range(8):
+        lin("bkp%d" % a, T.bkp[:, 128 * a:128 * a + 128], T.bo[:, :], T.ca[:, a:a + 1], 0.0, 128, ["bo", "ca"], ["bkp%d" % a], f=0.5)
+        lin("bkn%d" % a, T.bkn[:, 128 * a:128 * a + 128], T.bo[:, :], T.ca[:, 8 + a:9 + a], 0.0, 128, ["bo", "cb"], ["bkn%d" % a], f=0.5)
+    lin("offa", col(TMP + 4), T.rsel[:, 15:16], M1, 0.0, 1, ["rsel"], ["offa"])
+    lin("offb", col(TMP + 5), T.rsel[:, 14:15], 0.25, col(TMP + 4), 1, ["rsel", "offa"], ["offb"])
+    ts("offc", col(TMP + 6), col(RF), 14.0, BIG, ALU.is_lt, ALU.mult, 1, ["rf"], ["offc"])
+    for k, off in enumerate((1.0, 101.0, 17.0, 117.0)):
+        lin("off%d" % k, col(OFF + k), col(TMP + 6), off, col(TMP + 5), 1, ["offb", "offc"], ["off%d" % k])
+    ms("nm1", NM1, -M1, 1, ["nm1"])
+    ms("nq", NQ, -0.5, 1, ["nq"])
+    ts("swa", col(TMP + 2), col(PARF), -2.0, 1.0, ALU.mult, ALU.add, 1, ["parf"], ["tmp2"])
+    lin("swf", col(SWF), col(TMP + 2), 1.0, col(PF), 1, ["tmp2", "pf"], ["swf"])
+    ts("swm", T.sw[:, :], T.iom[:, :], col(SWF), None, ALU.is_equal, None, 128, ["iom", "swf"], ["sw"])
+    ts("kb", col(KB), col(PARF), 14.0, None, ALU.add, None, 1, ["parf"], ["kb"])
+    ts("kc", KC, col(PARF), -1.0, None, ALU.add, None, 1, ["parf"], ["kc"])
+    lin("jl2", T.jl[:, :], T.jl[:, :], 1.0, col(RF), 32, ["jl", "rf"], ["jl"])
+    for e in range(3):
+        red("m3%d" % e, col(M3 + e), T.gsel[:, e:8:3], ["gsel"], ["m3%d" % e])
+        ts("sh%d" % e, T.sh[:, 128 * e:128 * e + 128], T.iom[:, :], col(SHF), col(M3 + e), ALU.is_equal, ALU.mult, 128, ["iom", "shf", "m3%d" % e], ["sh%d" % e])
+    ms("pay0", T.pay0[:, 0:PW], 0.0, PW, ["pay0"])
+    ms("pay1", T.pay1[:, 0:PW], 0.0, PW, ["pay1"])
+    ms("jt", T.jt[:, 0:272], 0.0, 272, ["jta"])
+
+    cp("nxl", T.nxl[:, :], T.nxi[:, :], 256, ["nxi"], ["nxl"])
+    Bt, Wt = [T.bn0, T.bn1, T.bn2, T.bn3], [T.w0, T.w1, T.w2]
+    BK = [["bn0_%d" % h for h in range(8)], ["bn1"], ["bn2"], ["bn3"]]
+    WK = [["w0_%d" % h for h in range(8)], ["w1"], ["w2"]]
+    for h in range(8):
+        ov = T.nxl[:, 32 * h:32 * h + 32]
+        gather("bn%d" % h, T.bn0[:, 512 * h:512 * h + 512], T.pat[:, :], ov, 512, ["pat", "patA", "patB", "nxl"], ["bn0_%d" % h])
+        gather("w0_%d" % h, T.w0[:, 512 * h:512 * h + 512], T.crd[:, :], ov, 512, ["crd0", "crd1", "nxl"], ["w0_%d" % h])
+    dma("cp_b1", "y", T.bn1[:, 0:V], T.bn0[:, :], 1048576, BK[0], BK[1])
+    dma("cp_w1", "y", T.w1[:, 0:V], T.w0[:, :], 1048576, WK[0], WK[1])
+    ts("cura", T.cura[:, :], T.curi[:, :], 255, None, ALU.bitwise_and, None, 80, ["curi"], ["cura"])
+    ts("curb", T.curb[:, :], T.curi[:, :], 8, None, ALU.arith_shift_right, None, 80, ["curi"], ["curb"])
+    ts("curf", T.curf[:, :], T.cura[:, :], 16.0, None, ALU.mult, None, 80, ["cura"], ["curf"])
+    tt("curg", T.curg[:, :], T.curf[:, :], T.curb[:, :], ALU.add, 80, ["curf", "curb"], ["curg"])
+    cp("x0a", T.xa[:, 0:16], T.curg[:, 0:16], 16, ["curg"], ["xa0_0"])
+    cp("x0b", T.xb[:, 0:64], T.curg[:, 16:80], 64, ["curg"], ["xb0_0"])
+
+    Dk, Ck = (T.d0, T.d1, T.d2), (T.c0, T.c1, T.c2)
+    rts = routes(T, topo)
+
+    def xl(part, par, s, lo=0, hi=None):
+        n = 16 if part == "a" else 64
+        buf = T.xa if part == "a" else T.xb
+        b = (6 * par + s) * n
+        return buf[:, b + lo:b + (n if hi is None else hi)]
+
+    def chunk_list(par, s, ch):
+        src = s - 1 if s < 5 else 5
+        if ch == 0:
+            return xl("a", par, src), "xa%d_%d" % (par, src)
+        return xl("b", par, src, 32 * ch - 32, 32 * ch), "xb%d_%d" % (par, src)
+
+    def pbv(par, s, lo, hi, step=1):
+        b = (5 * par + s - 1) * L
+        return T.pb[:, b + lo:b + hi:step] if step > 1 else T.pb[:, b + lo:b + hi]
+
+    def list_set(name, out, fam, src, n, r, w, bank):
+        return mm(name, [(out, gm(fam, a), src(a), a == 0, a == 15, n) for a in range(16)], r + ["gm%d" % fam], w, bank)
+
+    def walk_lists(t, part):
+        par = t % 2
+        n, o, lo, hi = (16, 0, 0, 256) if part == "a" else (64, 16, 256, L)
+        zk = ["z0"] if part == "a" else ["z1", "z2"]
+        ps, pu, bank = (T.c0[:, 128:144], T.c0[:, 304:320], "c0") if part == "a" else (T.lb[:, 64:128], T.lb[:, 208:272], "lb")
+        list_set("cl%s%d" % (part, t), ps, GW, lambda a: T.z[:, lo + a:hi:16], n, zk, ["pcl" + part], bank)
+        cp("cli", T.li[:, o:o + n], ps, n, ["pcl" + part], ["li" + part], bank)
+        ts("clj", T.lj[:, o:o + n], T.li[:, o:o + n], 3, None, ALU.bitwise_and, None, n, ["li" + part], ["lj" + part])
+        for s in range(4):
+            ts("cm", T.cm[:, 4 * o + s * n:4 * o + s * n + n], T.lj[:, o:o + n], float(s), None, ALU.is_equal, None, n, ["lj" + part], ["cm%s%d" % (part, s)])
+        buf = T.xa if part == "a" else T.xb
+        b = (6 * par + 1) * n
+        xf = T.xf[:, 4 * o:4 * o + 4 * n]
+        cp("xf", xf, buf[:, b:b + 4 * n], 4 * n, ["x%s%d_%d" % (part, par, s) for s in range(1, 5)], ["xf" + part])
+        tt("xm", xf, xf, T.cm[:, 4 * o:4 * o + 4 * n], ALU.mult, 4 * n, ["xf" + part] + ["cm%s%d" % (part, s) for s in range(4)], ["xf" + part])
+        mm("us" + part, [(pu, T.idf[:, :], T.xf[:, 4 * o + s * n:4 * o + s * n + n], s == 0, s == 3, n) for s in range(4)],
+           ["idf", "xf" + part], ["pus" + part], bank, x=4)
+        cp("ul", xl(part, par, 5), pu, n, ["pus" + part], ["x%s%d_5" % (part, par)], bank)
+
+    def z_chain(t, ch):
+        par = t % 2
+        lo, hi = CH[ch]
+        n = hi - lo
+        nb = n // 64
+        D, C, dk, ck, zk, hk = Dk[ch][:, 0:n], Ck[ch], "d%d" % ch, "c%d" % ch, "z%d" % ch, "dh%d" % ch
+        zz, dh, sgv, ml = T.z[:, lo:hi], T.dh[:, lo:hi], T.sg[:, lo:hi], T.ml[:, 64 * ch:64 * ch + 64]
+        ci, cj = T.ci[:, 64 * ch:64 * ch + 64], T.cj[:, 64 * ch:64 * ch + 64]
+        mm("cc%d%d" % (t, ch), [(C[:, 64:128], gm(GW, a), T.z[:, lo + 64 * a:lo + 64 * a + 64], a == 0, a == nb - 1, 64) for a in range(nb)],
+           [zk, "gm3"], ["pcc%d" % ch], ck)
+        cp("cci", ci, C[:, 64:128], 64, ["pcc%d" % ch], ["ci%d" % ch], ck)
+        ts("ccj", cj, ci, 3, None, ALU.bitwise_and, None, 64, ["ci%d" % ch], ["cj%d" % ch])
+        for s in range(2, 5):
+            b = 192 * ch + 64 * (s - 2)
+            ts("pen", T.pen[:, b:b + 64], cj, float(s - 1), 100.0, ALU.is_ge, ALU.mult, 64, ["cj%d" % ch], ["pen%d_%d" % (ch, s)])
+        for s in range(1, 6):
+            off, ok = chunk_list(par, s, ch)
+            gather_tt("gs%d%d%d" % (t, ch, s), dh, Wt[t][:, 0:V], off, zz, ALU.subtract, n, WK[t] + [ok, zk], [hk])
+            if s == 5:
+                add("abs%d%d" % (t, ch), {"s": (cv(n), lambda g: g.scalar.activation(zz, dh, ACT.Abs))}, [hk], [zk])
+                break
+            so = add("sg%d%d%d" % (t, ch, s), {"s": (cv(n), lambda g: g.scalar.activation(sgv, dh, ACT.Sign, bias=NQ)),
+                                               "v": (cv(n, 0.5), lambda g: g.vector.tensor_scalar(sgv, dh, 0.0, 2.0, ALU.is_gt, ALU.mult))},
+                     [hk, "nq"], ["sg%d" % ch])
+            items = [(C[:, 0:64], gm(GC, a), T.sg[:, lo + 64 * a:lo + 64 * a + 64], a == 0, s == 1 and a == nb - 1, 64) for a in range(nb)]
+            rk = ["sg%d" % ch, "gm2"]
+            if s > 1:
+                b = 192 * ch + 64 * (s - 2)
+                items.append((C[:, 0:64], T.ipen[:, :], T.pen[:, b:b + 64], False, True, 64))
+                rk += ["ipen", "pen%d_%d" % (ch, s)]
+            mm("cnt%d%d%d" % (t, ch, s), items, rk, ["pcn%d" % ch], ck)
+            oc = lambda so=so, s=s: col(OFF + (1 if s > 1 else 0) + (2 if ops[so]["e"] == "v" else 0))
+            add("ml%d%d%d" % (t, ch, s), {"v": (cv(64), lambda g, oc=oc: g.vector.tensor_scalar(ml, C[:, 0:64], oc(), 0.0, ALU.add, ALU.max)),
+                                          "s": (cv(64), lambda g, oc=oc: g.scalar.activation(ml, C[:, 0:64], ACT.Relu, bias=oc()))},
+                ["pcn%d" % ch, "off0", "off1", "off2", "off3"], ["ml%d" % ch], ck)
+            items = []
+            for a in range(nb):
+                o, c0 = Dk[ch][:, 64 * a:64 * a + 64], lo + 64 * a
+                items.append((o, T.bkp[:, 128 * a:128 * a + 128], ml, True, False, 64))
+                items.append((o, T.ih[:, :], T.dh[:, c0:c0 + 64], False, False, 64))
+                items.append((o, T.bkn[:, 128 * a:128 * a + 128], ml, False, False, 64))
+                items.append((o, T.ione[:, :], T.z[:, c0:c0 + 64], False, True, 64))
+            mm("upd%d%d%d" % (t, ch, s), items, ["ml%d" % ch, "ih", "ione", hk, zk] + ["bk%s%d" % (x, a) for a in range(nb) for x in "pn"], [dk], dk)
+            lin("zo%d%d%d" % (t, ch, s), zz, D, 1.0, NM1, n, [dk, "nm1"], [zk], dk)
+        if t == RO - 1:
+            dma("st_z%d" % ch, "y", T.yz[:, lo:hi], zz, n * 256, [zk], ["yz%d" % ch])
+
+    def send(g, t, pay):
+        near = T.cores[[r for r, h in rts[rank] if h is None][0]]
+        trs, k = [], 0
+        for e, (r, h) in enumerate(rts[rank]):
+            d = T.cores[r] if h is None else h
+            rid, pid = topo.addr(d, core)
+            if h is None:
+                engs, sem = topo.engines(core, d)[0:HE], T.sem["arr%d" % t]
+            else:
+                engs, sem = [x for x in topo.engines(core, h) if x not in topo.engines(core, near)][HE * k:HE * k + HE], T.sem["hin%d" % t]
+                k += 1
+            s = (3 * t + e) * PW
+            trs.append(RemoteDMATransfer(dst_ids=[DstId(rid=rid, pnc=pid)], dma_engine_mask=as_mask(engs), remote_sem=sem,
+                                         src=pay[:, 0:PW], dst=T.land[:, s:s + PW]))
+        g.remote_dma_fused(trs, local_sem=T.sem["sent%d" % t])
+
+    for t in range(RO):
+        par, nxt = t % 2, (t + 1) % 2
+        W, B = Wt[t], Bt[t]
+        LA, LB = T.c0[:, 144:160], T.lb[:, 0:64]
+
+        def ptr(s, ch):
+            lo, hi = CH[ch]
+            off, ok = chunk_list(par, s, ch)
+            gather("p%d%d%d" % (t, ch, s), pbv(par, s, lo, hi), B[:, 0:V], off, hi - lo, BK[t] + [ok], ["pb%d_%d_%d" % (par, ch, s)])
+
+        def lists(s, part):
+            dst = (par, s) if s < 5 else (nxt, 0)
+            if part == "a":
+                list_set("la%d%d" % (t, s), LA, GP, lambda a: pbv(par, s, a, A, 16), 16, ["pb%d_0_%d" % (par, s)], ["pla"], "c0")
+                cp("xa", xl("a", dst[0], dst[1]), LA, 16, ["pla"], ["xa%d_%d" % dst], "c0")
+            else:
+                list_set("lb%d%d" % (t, s), LB, GP, lambda a: pbv(par, s, A + a, L, 16), 64, ["pb%d_%d_%d" % (par, ch, s) for ch in (1, 2)], ["plb"], "lb")
+                cp("xb", xl("b", dst[0], dst[1]), LB, 64, ["plb"], ["xb%d_%d" % dst], "lb")
+
+        for s in range(1, 5):
+            for ch in range(3):
+                ptr(s, ch)
+            lists(s, "a")
+            lists(s, "b")
+        walk_lists(t, "a")
+        pR, pRk = pbv(par, 5, 0, A), "pb%d_0_5" % par
+        ptr(5, 0)
+        up = mm("upart", [(T.xk[:, 400:416], T.sw[:, :], T.xf[:, 16 * s:16 * s + 16], s == 0, s == 3, 16) for s in range(4)], ["sw", "xfa"], ["pup"], "xk", x=4)
+        mm("vwide", [(T.xk[:, 0:256], T.bw[:, :], pR, True, True, 256)], ["bw", pRk], ["pvw"], "xk")
+        list_set("lv%d" % t, LA, GP, lambda a: pbv(par, 5, a, A, 16), 16, [pRk], ["pla"], "c0")
+        ts("vw", T.vw[:, :], T.xk[:, 0:256], -2048.0, None, ALU.add, None, 256, ["pvw"], ["vw"], "xk")
+        ts("vl", T.vl[:, :], LA, -2048.0, None, ALU.add, None, 16, ["pla"], ["vl"], "c0")
+        if t < RO - 1:
+            cp("xa0", xl("a", nxt, 0), LA, 16, ["pla"], ["xa%d_0" % nxt], "c0")
+        PS, PR = T.xk[:, 256:384], T.xk[:, 384:400]
+        for k in range(16):
+            ts("eq%d" % k, T.eq[:, 256 * k:256 * k + 256], T.vw[:, :], T.vl[:, k:k + 1], None, ALU.is_equal, None, 256, ["vw", "vl"], ["eq%d" % k], f=0.5)
+            if k % 2 == 1:
+                items = [(PS, T.bo[:, :], T.eq[:, 256 * kk + h:256 * kk + 256:2], kk == 0 and h == 0, kk == 15 and h == 1, 128)
+                         for kk in (k - 1, k) for h in range(2)]
+                mm("S%d" % k, items, ["bo", "eq%d" % (k - 1), "eq%d" % k], ["pS"], "xk", after=[up])
+        ts("cutp", T.cutp[:, :], PS, 2.0, None, ALU.is_equal, None, 128, ["pS"], ["cutp"], "xk")
+        ts("cutq", T.cutq[:, :], PS, 2.0, None, ALU.not_equal, None, 128, ["pS"], ["cutq"], "xk")
+        scan("cum", T.cum[:, :], T.cutp[:, :], T.cutp[:, :], 0.0, ALU.add, ALU.max, ["cutp"], ["cum"])
+        tt("cutr", T.cutr[:, :], T.cutq[:, :], T.pc[:, :], ALU.mult, 128, ["cutq", "pc"], ["cutr"])
+        tt("rr", T.rr[:, :], T.cutr[:, :], T.cum[:, :], ALU.max, 128, ["cutr", "cum"], ["rr"])
+        list_set("R%d" % t, PR, G8, lambda a: T.rr[:, a // 2:128:8], 16, ["rr"], ["pR"], "xk")
+        pay = (T.pay0, T.pay1, None)[t]
+        if t < RO - 1:
+            ts("ipay", T.ipay[:, :], PR, col(KB), None, ALU.add, None, 16, ["pR", "kb"], ["ipay"], "xk")
+            lin("kf", T.kf[:, :], PR, 1.0, col(KB), 16, ["pR", "kb"], ["kf"], "xk")
+            lin("kg", T.kg[:, :], PR, 1.0, KC, 16, ["pR", "kc"], ["kg"], "xk")
+            ts("m", pay[:, 0:1], T.cum[:, 127:128], 2.0, 128.0, ALU.mult, ALU.min, 1, ["cum"], ["pay%d" % t])
+        ts("k1", T.k1[:, :], PR, -257.0, 16384.0, ALU.add, ALU.mult, 16, ["pR"], ["k1"], "xk")
+        tt("k2", T.k2[:, :], T.k1[:, :], T.jl[:, 16:32], ALU.min, 16, ["k1", "jl"], ["k2"])
+        tt("k3", T.k3[:, :], T.xk[:, 400:416], T.k2[:, :], ALU.max, 16, ["pup", "k2"], ["k3"], "xk")
+        itg = T.itg[:, 16 * par:16 * par + 16]
+        cp("itg", itg, T.k3[:, :], 16, ["k3"], ["itg%d" % par])
+        scatter("sbn%d" % t, Bt[t + 1][:, :], itg, pR, A, ["itg%d" % par, pRk], BK[t + 1])
+        if t < RO - 1:
+            dma("cp_b%d" % (t + 2), "y", Bt[t + 2][:, 0:V], Bt[t + 1][:, 0:V], 1048576, BK[t + 1], BK[t + 2])
+            gather("va%d" % t, T.jt[:, 272:528], W[:, 0:V], xl("a", par, 5), A, WK[t] + ["xa%d_5" % par], ["jtc"])
+            scatter("spay%d" % t, pay[:, :], T.ipay[:, :], T.jt[:, 272:528], A, ["ipay", "jtc"], ["pay%d" % t])
+            add("send%d" % t, {"g": ((600.0, 0, 0, 0, 0), lambda g, t=t, pay=pay: send(g, t, pay))}, ["pay%d" % t], ["land%d" % t],
+                lat=8000.0 if t == 0 else 6000.0, ext="send")
+        z_chain(t, 0)
+        walk_lists(t, "b")
+        ptr(5, 1)
+        ptr(5, 2)
+        if t < RO - 1:
+            lists(5, "b")
+        z_chain(t, 1)
+        z_chain(t, 2)
+        if t < RO - 1:
+            narr, items, PM = 0, [], T.c0[:, 160:160 + PW]
+            for e in range(3):
+                h = rts[(rank - 1 - e) % 4][e][1]
+                narr += HE if h is None else len(topo.engines(h, core))
+                s, m = (3 * t + e) * PW, (e - t) % 3
+                items.append((PM, T.sh[:, 128 * m:128 * m + 128], T.land[:, s:s + PW], e == 0, e == 2, PW))
+            i = mm("merge%d" % t, items, ["land%d" % t, "sh0", "sh1", "sh2"], ["pmg"], "c0")
+            ops[i]["ext"] = ("arr%d" % t, narr)
+            cp("jta", T.jt[:, 0:PW], PM, PW, ["pmg"], ["jta"], "c0", both=True)
+            ts("k4", T.k4[:, :], T.kg[:, :], T.jt[:, 0:1], 2000.0, ALU.subtract, ALU.mult, 16, ["kg", "jta"], ["k4"])
+            tt("k5", T.k5[:, :], T.k4[:, :], T.kf[:, :], ALU.max, 16, ["k4", "kf"], ["k5"])
+            tt("k6", T.k6[:, :], T.k5[:, :], T.jl[:, 0:16], ALU.min, 16, ["k5", "jl"], ["k6"])
+            cp("ijn", T.ijn[:, :], T.k6[:, :], 16, ["k6"], ["ijn"])
+            gather("vnew", T.vnew[:, :], T.jt[:, :], T.ijn[:, :], A, ["jta", "jtc", "ijn"], ["vnew"])
+            scatter("sw%d" % t, Wt[t + 1][:, :], itg, T.vnew[:, :], A, ["itg%d" % par, "vnew"], WK[t + 1])
+            if t == 0:
+                dma("cp_w2", "y", T.w2[:, 0:V], T.w1[:, 0:V], 1048576, ["w1"], ["w2"])
+    par = (RO - 1) % 2
+    list_set("yn", T.xk[:, 0:256], GT, lambda a: T.bn3[:, a:V:16], 256, BK[3], ["pvw"], "xk")
+    cp("yns", T.yns[:, :], T.xk[:, 0:256], 256, ["pvw"], ["yns"], "xk", both=True)
+    dma("st_n", "y", T.yn[:], T.yns[:, :], 131072, ["yns"], ["yn"])
+    list_set("yc", T.lb[:, 128:208], GT, lambda a: pbv(par, 5, 80 * a, 80 * a + 80), 80, ["pb%d_%d_5" % (par, ch) for ch in range(3)], ["pyc"], "lb")
+    cp("ycs", T.ycs[:, :], T.lb[:, 128:208], 80, ["pyc"], ["ycs"], "lb", both=True)
+    dma("st_c", "y", T.yc[:], T.ycs[:, :], 40960, ["ycs"], ["yc"])
+    return ops
+
+
+def place(ops, succ, cost, hop, weight, bias):
+    n = len(ops)
+    rank = [0.0] * n
+    for i in range(n - 1, -1, -1):
+        rank[i] += (min(cost[i].values()) + hop) * weight[i] + ops[i]["lat"]
+        for d in ops[i]["deps"]:
+            if rank[i] > rank[d]:
+                rank[d] = rank[i]
+    left, rdy = [len(o["deps"]) for o in ops], [0.0] * n
+    free, bank, eng, order = {e: 0.0 for e in "vstgy"}, {}, [None] * n, []
+    ready = [i for i in range(n) if not left[i]]
+    look = CFG["look"]
+    while ready:
+        best = None
+        for i in ready:
+            b = bank.get(ops[i]["bank"])
+            for e, c in cost[i].items():
+                t = rdy[i] if rdy[i] > free[e] else free[e]
+                if b and b[1] != e and b[0] + hop > t:
+                    t = b[0] + hop
+                key = t - look * rank[i] + (bias[i] * c if e == "v" else 0.0)
+                if best is None or key < best[0]:
+                    best = (key, i, e, t, c)
+        _k, i, e, t, c = best
+        ready.remove(i)
+        order.append(i)
+        eng[i], free[e] = e, t + c
+        if ops[i]["bank"]:
+            bank[ops[i]["bank"]] = (t + c, e)
+        for j in succ[i]:
+            rdy[j] = max(rdy[j], t + c + ops[i]["lat"] + (0.0 if e == "t" and "t" in cost[j] else hop))
+            left[j] -= 1
+            if not left[j]:
+                ready.append(j)
+    return order, eng
+
+
+def replay(ops, order, eng, cost, hop, lf):
+    free, bank, last, end, why = {}, {}, {}, [0.0] * len(ops), [None] * len(ops)
+    for i in order:
+        o, e, t, y = ops[i], eng[i], 0.0, None
+        for d in o["deps"]:
+            x = end[d] + (0.0 if e == "t" and eng[d] == "t" else hop)
+            if x > t:
+                t, y = x, (d, 0)
+        if free.get(e, 0.0) > t:
+            t, y = free[e], (last[e], 1)
+        if o["bank"]:
+            p = bank.get(o["bank"])
+            if p is not None and eng[p] != e and end[p] + hop > t:
+                t, y = end[p] + hop, (p, 1)
+            bank[o["bank"]] = i
+        free[e], last[e], why[i] = t + cost[i][e], i, y
+        end[i] = free[e] + o["lat"] * lf
+    return max(end), end, why
+
+
+PLAN = {}
+
+
+def schedule(ops):
+    if "order" not in PLAN:
+        costs = [[{e: sum(a * b for a, b in zip(c, m[0])) for e, (c, _f) in o["alts"].items()} for o in ops] for m in PLANS]
+        rng = np.random.default_rng(CFG["seed"])
+        n = len(ops)
+        succ = [[] for _ in ops]
+        for o in ops:
+            for d in o["deps"]:
+                succ[d].append(o["i"])
+
+        def judge(order, eng):
+            r = [replay(ops, order, eng, costs[j], m[1], m[2]) for j, m in enumerate(PLANS)]
+            return 2 * r[0][0] + r[1][0] + r[2][0], r
+
+        weight, best = np.ones(n), None
+        bias = np.array([3.0 if o["n"][:2] in ("p0", "p1", "p2", "va", "vn", "ml", "zo") else 0.0 for o in ops])
+        for it in range(CFG["iters"]):
+            w, b = weight.copy(), bias.copy()
+            if it:
+                k = rng.random(n) < 0.05
+                w[k] = np.exp(rng.normal(0.0, 0.8, int(k.sum())))
+                k = rng.random(n) < 0.03
+                b[k] = np.exp(rng.normal(0.5, 1.5, int(k.sum()))) - 0.5
+            order, eng = place(ops, succ, costs[0], PLANS[0][1], w.tolist(), b.tolist())
+            score, r = judge(order, eng)
+            if best is None or score <= best[0]:
+                best, weight, bias = (score, order, eng, r), w, b
+        score, order, eng, r = best
+        for it in range(CFG["polish"]):
+            _m, end, why = r[int(rng.integers(0, len(PLANS)))]
+            i, cand = int(np.argmax(end)), []
+            while why[i] is not None:
+                if why[i][1]:
+                    cand.append((i, why[i][0]))
+                i = why[i][0]
+            i, p = cand[int(rng.integers(0, len(cand)))]
+            o2, e2, u = order, eng, rng.random()
+            j = p if u < 0.25 else i
+            if u < 0.4 and len(ops[j]["alts"]) > 1:
+                e2 = list(eng)
+                e2[j] = "s" if eng[j] == "v" else "v"
+            else:
+                a, b = order.index(p), order.index(i)
+                seg, need = order[a:b + 1], {i}
+                for x in reversed(seg):
+                    if x in need:
+                        need.update(ops[x]["deps"])
+                if p in need:
+                    continue
+                o2 = order[:a] + [x for x in seg if x in need] + [x for x in seg if x not in need] + order[b + 1:]
+            s2, r2 = judge(o2, e2)
+            if s2 <= score + 150.0 * rng.random() ** 4:
+                score, order, eng, r = s2, o2, e2, r2
+        PLAN["order"], PLAN["eng"], PLAN["val"] = order, eng, [x[0] for x in r]
+    for o, e in zip(ops, PLAN["eng"]):
+        o["e"] = e
+    return PLAN["order"]
+
+
+def emit(g, T, ops, order):
+    queue = {"v": g.vector, "s": g.scalar, "t": g.tensor, "g": g, "y": g.sync}
+    sem = {"v": "nv", "s": "ns", "t": "nt", "g": "ng"}
+    count = {"v": 0, "s": 0, "t": 0, "g": 0}
+    seen = {e: {} for e in queue}
+    last_bank, tail, ndma = {}, {}, [0]
+
+    def wait(e, name, val):
+        if seen[e].get(name, 0) < val:
+            queue[e].wait_ge(T.sem[name], val)
+            seen[e][name] = val
+
+    for i in order:
+        o = ops[i]
+        e = o["e"]
+        deps = list(o["deps"])
+        if o["bank"]:
+            if o["bank"] in last_bank and ops[last_bank[o["bank"]]]["e"] != e:
+                deps.append(last_bank[o["bank"]])
+            last_bank[o["bank"]] = i
+        need = {}
+        for d in deps:
+            p = ops[d]
+            if p["ext"] == "send" or (e == "t" and p["e"] == "t"):
+                continue
+            name, val = p["tok"]
+            need[name] = max(need.get(name, 0), val)
+        for name in sorted(need):
+            wait(e, name, need[name])
+        if o["ext"] and o["ext"] != "send":
+            wait(e, o["ext"][0], o["ext"][1])
+        ins = o["alts"][e][1](g)
+        if o["ext"] == "send":
+            continue
+        if o["dma"]:
+            name = "dq%d" % ndma[0]
+            ndma[0] += 1
+            ins.then_inc(T.sem[name], 16)
+            o["tok"] = (name, 16)
+        else:
+            count[e] += 1
+            ins.then_inc(T.sem[sem[e]], 1)
+            o["tok"] = (sem[e], count[e])
+        tail[o["tok"][0]] = o["tok"][1]
+    for t in range(RO - 1):
+        wait("g", "sent%d" % t, 3 * HE)
+    for name in sorted(tail):
+        if max(seen[e].get(name, 0) for e in queue) < tail[name]:
+            wait("y", name, tail[name])
+
+
+def rank_program(g, core, T, topo):
+    rank = T.rank_of(core)
+    if rank is None:
+        for row in routes(T, topo):
+            for e, (r, h) in enumerate(row):
+                if h == core:
+                    helper_program(g, core, T, topo, e, r)
+        return
+    ops = build(T, topo, core, rank)
+    emit(g, T, ops, schedule(ops))

@@ -9,21 +9,21 @@ PW = 144
 BIG = float(2 ** 33)
 M1 = 1.5 * 2 ** 23
 CH = ((0, 256), (256, 768), (768, 1280))
-CFG = {"iters": 1500, "polish": 5000, "seed": 2, "look": 0.01}
-PLANS = (((1.0, 1.0, 1.56, 3.8, 0.5), 90.0, 1.0), ((1.0, 1.0, 1.15, 2.0, 0.5), 60.0, 1.2), ((1.0, 1.0, 2.0, 5.5, 0.5), 120.0, 0.9))
+CFG = {"iters": 1500, "polish": 6000, "seed": 2, "look": 0.01, "rev": (0, 1)}
+PLANS = (((1.0, 0.83, 1.3, 3.15, 0.42), 200.0, 1.3), ((1.0, 0.85, 1.0, 2.0, 0.5), 100.0, 1.7), ((1.0, 1.16, 2.25, 5.8, 0.63), 200.0, 1.3))
 
 _bf, _f, _i, _u = "bfloat16", "float32", "int32", "uint16"
 _SB = {
     _bf: {"crd": V, "pat": V, "bn0": V, "bn1": V + A, "bn2": V + A, "bn3": V + A, "w0": V, "w1": V + A, "w2": V + A, "r256": 16, "pc": 128,
-          "ih": 128, "ione": 128, "ipen": 128, "gm": 720, "bkp": 1024, "bkn": 1024, "bo": 128, "bw": 128, "sh": 384, "z": L, "dh": L,
-          "pb": 10 * L, "sg": L, "ml": 192, "pen": 576, "eq": 4096, "cutp": 128, "cutq": 128, "cutr": 128, "cum": 128, "rr": 128,
-          "pay0": 528, "pay1": 528, "jt": 528, "vnew": 256, "land": 6 * PW},
+          "ih": 128, "ione": 128, "ineg": 128, "cdr": L, "ipen": 128, "gm": 720, "bkp": 1024, "bkn": 1024, "bo": 128, "bw": 128, "sh": 384,
+          "z": L, "dh": L, "pb": 10 * L, "sg": L, "ml": 192, "pen": 576, "eq": 4096, "cutp": 128, "cutq": 128, "cutr": 128, "cum": 128,
+          "rr": 128, "pay0": 528, "pay1": 528, "jt": 528, "vnew": 256, "land": 6 * PW},
     _f: {"curf": 80, "curg": 80, "col": 32, "rsel": 16, "gsel": 8, "ca": 16, "two": 16, "pw": 16, "pw2": 16, "iom": 128, "iog": 128, "jl": 32,
-         "sw": 128, "idf": 128, "cm": 320, "xf": 320, "vl": 16, "kf": 16, "kg": 16, "k1": 16, "k2": 16, "k3": 16, "k4": 16, "k5": 16, "k6": 16,
+         "cm": 320, "cf": 192, "vl": 16, "kf": 16, "kg": 16, "k1": 16, "k2": 16, "k3": 16, "k4": 16, "k5": 16, "k6": 16,
          "ycs": 80, "yns": 256},
     _i: {"nxi": 256, "curi": 80, "cura": 80, "curb": 80, "wti": 8, "ip": 8, "iq": 8, "ci": 192, "cj": 192, "li": 80, "lj": 80},
     _u: {"nxl": 256, "xa": 192, "xb": 768, "ipay": 16, "itg": 32, "ijn": 16},
-    "float16": {"vw": 256},
+    "float16": {"vw": 256, "sw": 128, "idf": 128, "xf": 320},
 }
 SCRATCH = {k: ("sbuf", [128, n], d) for d, b in _SB.items() for k, n in b.items()}
 SCRATCH.update({k: ("psum", [128, 512], _f) for k in ("d0", "d1", "d2", "c0", "c1", "c2", "lb", "xk")})
@@ -130,12 +130,12 @@ def build(T, topo, core, rank):
     def scatter(name, win, off, in_, n, r, w):
         return add(name, {"v": ((55, 0, 0, n, 0), lambda g: g.vector.tensor_copy(win.indirect(off), in_))}, r, w)
 
-    def mm(name, items, r, w, bank, after=(), x=1):
+    def mm(name, items, r, w, bank, after=()):
         def fn(g):
             for o, a, b, s0, s1, _n in items:
                 ins = g.tensor.matmul(o, a, b, s0, s1)
             return ins
-        return add(name, {"t": ((20, 0, 0, 0, x * sum(max(64, it[5]) for it in items)), fn)}, r, w, bank, after=after)
+        return add(name, {"t": ((20, 0, 0, 0, sum(max(64, it[5]) for it in items)), fn)}, r, w, bank, after=after)
 
     def dma(name, q, out, in_, nbytes, r, w):
         fn = (lambda g: g.sync.dma_start(out, in_)) if q == "y" else (lambda g: g.scalar.dma_start(out, in_))
@@ -164,7 +164,7 @@ def build(T, topo, core, rank):
     iota("ip", T.ip[:, 0:2], [[16, 2]], 0, 1, 2, ["ip"], True)
     iota("iom", T.iom[:, :], [[1, 128]], 0, 0, 128, ["iom"])
     iota("iog", T.iog[:, :], [[1, 8], [0, 16]], 0, 0, 128, ["iog"])
-    iota("jl", T.jl[:, :], [[3824, 2], [16, 16]], 272, 0, 32, ["jl"])
+    iota("jl", T.jl[:, :], [[1776, 2], [16, 16]], 272, 0, 32, ["jl"])
     iota("pc", T.pc[:, :], [[1, 128]], 129, 0, 128, ["pc"])
     ts("ir", T.iq[:, 1:2], T.ip[:, 0:1], 15, None, ALU.bitwise_and, None, 1, ["ip"], ["iq1"])
     cp("rf", col(RF), T.iq[:, 1:2], 1, ["iq1"], ["rf"])
@@ -197,7 +197,10 @@ def build(T, topo, core, rank):
     ts("bo", T.bo[:, :], T.iog[:, :], col(GF), None, ALU.is_equal, None, 128, ["iog", "gf"], ["bo"])
     lin("bw", T.bw[:, :], T.bo[:, :], col(WP), 0.0, 128, ["bo", "wp"], ["bw"], f=0.5)
     ts("ih", T.ih[:, :], T.iom[:, :], col(PF), 0.5, ALU.is_equal, ALU.mult, 128, ["iom", "pf"], ["ih"])
-    for nm, sc in (("ione", 2.0), ("idf", 2.0), ("ipen", -2.0 * BIG)):
+    ts("idf", T.idf[:, :], T.ih[:, :], 2.0, None, ALU.mult, None, 128, ["ih"], ["idf"], f=0.5)
+    for k in range(3):
+        ms("pcol", col(TMP + 10 + k), 100.0 * (k + 1), 1, ["pcol%d" % k])
+    for nm, sc in (("ione", 2.0), ("ineg", -2.0)):
         lin(nm, T[nm][:, :], T.ih[:, :], sc, 0.0, 128, ["ih"], [nm], f=0.5)
     ts("ca", T.ca[:, 0:8], T.rsel[:, 0:8], T.rsel[:, 14:15], None, ALU.subtract, None, 8, ["rsel"], ["ca"])
     lin("cb", T.ca[:, 8:16], T.rsel[:, 0:8], -1.0, T.rsel[:, 15:16], 8, ["rsel"], ["cb"])
@@ -207,8 +210,9 @@ def build(T, topo, core, rank):
     lin("offa", col(TMP + 4), T.rsel[:, 15:16], M1, 0.0, 1, ["rsel"], ["offa"])
     lin("offb", col(TMP + 5), T.rsel[:, 14:15], 0.25, col(TMP + 4), 1, ["rsel", "offa"], ["offb"])
     ts("offc", col(TMP + 6), col(RF), 14.0, BIG, ALU.is_lt, ALU.mult, 1, ["rf"], ["offc"])
-    for k, off in enumerate((1.0, 101.0, 17.0, 117.0)):
+    for k, off in enumerate((1.0, 17.0)):
         lin("off%d" % k, col(OFF + k), col(TMP + 6), off, col(TMP + 5), 1, ["offb", "offc"], ["off%d" % k])
+    lin("ipen", T.ipen[:, :], T.ione[:, :], col(TMP + 6), 0.0, 128, ["ione", "offc"], ["ipen"], f=0.5)
     ms("nm1", NM1, -M1, 1, ["nm1"])
     ms("nq", NQ, -0.5, 1, ["nq"])
     ts("swa", col(TMP + 2), col(PARF), -2.0, 1.0, ALU.mult, ALU.add, 1, ["parf"], ["tmp2"])
@@ -276,11 +280,11 @@ def build(T, topo, core, rank):
         buf = T.xa if part == "a" else T.xb
         b = (6 * par + 1) * n
         xf = T.xf[:, 4 * o:4 * o + 4 * n]
-        cp("xf", xf, buf[:, b:b + 4 * n], 4 * n, ["x%s%d_%d" % (part, par, s) for s in range(1, 5)], ["xf" + part])
+        ts("xf", xf, buf[:, b:b + 4 * n], -2048.0, None, ALU.add, None, 4 * n, ["x%s%d_%d" % (part, par, s) for s in range(1, 5)], ["xf" + part], f=0.5)
         tt("xm", xf, xf, T.cm[:, 4 * o:4 * o + 4 * n], ALU.mult, 4 * n, ["xf" + part] + ["cm%s%d" % (part, s) for s in range(4)], ["xf" + part])
         mm("us" + part, [(pu, T.idf[:, :], T.xf[:, 4 * o + s * n:4 * o + s * n + n], s == 0, s == 3, n) for s in range(4)],
-           ["idf", "xf" + part], ["pus" + part], bank, x=4)
-        cp("ul", xl(part, par, 5), pu, n, ["pus" + part], ["x%s%d_5" % (part, par)], bank)
+           ["idf", "xf" + part], ["pus" + part], bank)
+        ts("ul", xl(part, par, 5), pu, 2048.0, None, ALU.add, None, n, ["pus" + part], ["x%s%d_5" % (part, par)], bank)
 
     def z_chain(t, ch):
         par = t % 2
@@ -289,16 +293,26 @@ def build(T, topo, core, rank):
         nb = n // 64
         D, C, dk, ck, zk, hk = Dk[ch][:, 0:n], Ck[ch], "d%d" % ch, "c%d" % ch, "z%d" % ch, "dh%d" % ch
         zz, dh, sgv, ml = T.z[:, lo:hi], T.dh[:, lo:hi], T.sg[:, lo:hi], T.ml[:, 64 * ch:64 * ch + 64]
-        ci, cj = T.ci[:, 64 * ch:64 * ch + 64], T.cj[:, 64 * ch:64 * ch + 64]
+        ci, cj, cf = T.ci[:, 64 * ch:64 * ch + 64], T.cj[:, 64 * ch:64 * ch + 64], T.cf[:, 64 * ch:64 * ch + 64]
         mm("cc%d%d" % (t, ch), [(C[:, 64:128], gm(GW, a), T.z[:, lo + 64 * a:lo + 64 * a + 64], a == 0, a == nb - 1, 64) for a in range(nb)],
            [zk, "gm3"], ["pcc%d" % ch], ck)
         cp("cci", ci, C[:, 64:128], 64, ["pcc%d" % ch], ["ci%d" % ch], ck)
         ts("ccj", cj, ci, 3, None, ALU.bitwise_and, None, 64, ["ci%d" % ch], ["cj%d" % ch])
+        cp("ccf", cf, cj, 64, ["cj%d" % ch], ["cf%d" % ch])
         for s in range(2, 5):
-            b = 192 * ch + 64 * (s - 2)
-            ts("pen", T.pen[:, b:b + 64], cj, float(s - 1), 100.0, ALU.is_ge, ALU.mult, 64, ["cj%d" % ch], ["pen%d_%d" % (ch, s)])
+            pen = T.pen[:, 192 * ch + 64 * (s - 2):192 * ch + 64 * (s - 1)]
+            add("pen", {"v": (cv(64), lambda g, s=s, pen=pen: g.vector.tensor_scalar(pen, cf, float(s - 1), 100.0, ALU.is_lt, ALU.mult)),
+                        "s": (cv(64), lambda g, s=s, pen=pen: g.scalar.activation(pen, cf, ACT.Relu, bias=col(TMP + 8 + s), scale=-100.0))},
+                ["cf%d" % ch, "pcol%d" % (s - 2)], ["pen%d_%d" % (ch, s)])
         for s in range(1, 6):
             off, ok = chunk_list(par, s, ch)
+            if s == 5 and ch in CFG["rev"]:
+                cd, kk = (T.jt[:, 272:528], "jtc") if ch == 0 and t < RO - 1 else (T.cdr[:, lo:hi], "cdr%d" % ch)
+                if kk != "jtc":
+                    gather("vr%d%d" % (t, ch), cd, Wt[t][:, 0:V], off, n, WK[t] + [ok], [kk])
+                mm("rv%d%d" % (t, ch), [(D, T.ione[:, :], cd, True, False, n), (D, T.ineg[:, :], zz, False, True, n)], [kk, zk, "ione", "ineg"], [dk], dk)
+                add("abs%d%d" % (t, ch), {"s": (cv(n), lambda g: g.scalar.activation(zz, D, ACT.Abs))}, [dk], [zk], dk)
+                break
             gather_tt("gs%d%d%d" % (t, ch, s), dh, Wt[t][:, 0:V], off, zz, ALU.subtract, n, WK[t] + [ok, zk], [hk])
             if s == 5:
                 add("abs%d%d" % (t, ch), {"s": (cv(n), lambda g: g.scalar.activation(zz, dh, ACT.Abs))}, [hk], [zk])
@@ -313,17 +327,14 @@ def build(T, topo, core, rank):
                 items.append((C[:, 0:64], T.ipen[:, :], T.pen[:, b:b + 64], False, True, 64))
                 rk += ["ipen", "pen%d_%d" % (ch, s)]
             mm("cnt%d%d%d" % (t, ch, s), items, rk, ["pcn%d" % ch], ck)
-            oc = lambda so=so, s=s: col(OFF + (1 if s > 1 else 0) + (2 if ops[so]["e"] == "v" else 0))
+            oc = lambda so=so: col(OFF + (1 if ops[so]["e"] == "v" else 0))
             add("ml%d%d%d" % (t, ch, s), {"v": (cv(64), lambda g, oc=oc: g.vector.tensor_scalar(ml, C[:, 0:64], oc(), 0.0, ALU.add, ALU.max)),
                                           "s": (cv(64), lambda g, oc=oc: g.scalar.activation(ml, C[:, 0:64], ACT.Relu, bias=oc()))},
-                ["pcn%d" % ch, "off0", "off1", "off2", "off3"], ["ml%d" % ch], ck)
-            items = []
-            for a in range(nb):
-                o, c0 = Dk[ch][:, 64 * a:64 * a + 64], lo + 64 * a
-                items.append((o, T.bkp[:, 128 * a:128 * a + 128], ml, True, False, 64))
-                items.append((o, T.ih[:, :], T.dh[:, c0:c0 + 64], False, False, 64))
-                items.append((o, T.bkn[:, 128 * a:128 * a + 128], ml, False, False, 64))
-                items.append((o, T.ione[:, :], T.z[:, c0:c0 + 64], False, True, 64))
+                ["pcn%d" % ch, "off0", "off1"], ["ml%d" % ch], ck)
+            items = [(D, T.ih[:, :], dh, True, False, n)]
+            for bk in (T.bkp, T.bkn):
+                items += [(Dk[ch][:, 64 * a:64 * a + 64], bk[:, 128 * a:128 * a + 128], ml, False, False, 64) for a in range(nb)]
+            items.append((D, T.ione[:, :], zz, False, True, n))
             mm("upd%d%d%d" % (t, ch, s), items, ["ml%d" % ch, "ih", "ione", hk, zk] + ["bk%s%d" % (x, a) for a in range(nb) for x in "pn"], [dk], dk)
             lin("zo%d%d%d" % (t, ch, s), zz, D, 1.0, NM1, n, [dk, "nm1"], [zk], dk)
         if t == RO - 1:
@@ -372,7 +383,7 @@ def build(T, topo, core, rank):
         walk_lists(t, "a")
         pR, pRk = pbv(par, 5, 0, A), "pb%d_0_5" % par
         ptr(5, 0)
-        up = mm("upart", [(T.xk[:, 400:416], T.sw[:, :], T.xf[:, 16 * s:16 * s + 16], s == 0, s == 3, 16) for s in range(4)], ["sw", "xfa"], ["pup"], "xk", x=4)
+        up = mm("upart", [(T.xk[:, 400:416], T.sw[:, :], T.xf[:, 16 * s:16 * s + 16], s == 0, s == 3, 16) for s in range(4)], ["sw", "xfa"], ["pup"], "xk")
         mm("vwide", [(T.xk[:, 0:256], T.bw[:, :], pR, True, True, 256)], ["bw", pRk], ["pvw"], "xk")
         list_set("lv%d" % t, LA, GP, lambda a: pbv(par, 5, a, A, 16), 16, [pRk], ["pla"], "c0")
         ts("vw", T.vw[:, :], T.xk[:, 0:256], -2048.0, None, ALU.add, None, 256, ["pvw"], ["vw"], "xk")
@@ -402,7 +413,7 @@ def build(T, topo, core, rank):
         tt("k2", T.k2[:, :], T.k1[:, :], T.jl[:, 16:32], ALU.min, 16, ["k1", "jl"], ["k2"])
         tt("k3", T.k3[:, :], T.xk[:, 400:416], T.k2[:, :], ALU.max, 16, ["pup", "k2"], ["k3"], "xk")
         itg = T.itg[:, 16 * par:16 * par + 16]
-        cp("itg", itg, T.k3[:, :], 16, ["k3"], ["itg%d" % par])
+        ts("itg", itg, T.k3[:, :], 2048.0, None, ALU.add, None, 16, ["k3"], ["itg%d" % par])
         scatter("sbn%d" % t, Bt[t + 1][:, :], itg, pR, A, ["itg%d" % par, pRk], BK[t + 1])
         if t < RO - 1:
             dma("cp_b%d" % (t + 2), "y", Bt[t + 2][:, 0:V], Bt[t + 1][:, 0:V], 1048576, BK[t + 1], BK[t + 2])
@@ -521,7 +532,7 @@ def schedule(ops):
             return 2 * r[0][0] + r[1][0] + r[2][0], r
 
         weight, best = np.ones(n), None
-        bias = np.array([3.0 if o["n"][:2] in ("p0", "p1", "p2", "va", "vn", "ml", "zo") else 0.0 for o in ops])
+        bias = np.array([3.0 if o["n"][:2] in ("p0", "p1", "p2", "va", "vn", "ml", "zo", "pe", "vr") else 0.0 for o in ops])
         for it in range(CFG["iters"]):
             w, b = weight.copy(), bias.copy()
             if it:

@@ -4,29 +4,38 @@ from concourse.mybir import dt, AluOpType, AxisListType, ActivationFunctionType
 
 ALU = AluOpType
 ACT = ActivationFunctionType
-V, L, A, RO = 4096, 1280, 256, 3
-PW = 144
+V, L, A, S, RO = 4096, 1280, 256, 128, 3
+PW = S + 8
 BIG = float(2 ** 33)
 M1 = 1.5 * 2 ** 23
-CH = ((0, 256), (256, 768), (768, 1280))
-CFG = {"iters": 1500, "polish": 6000, "seed": 2, "look": 0.01, "rev": (0, 1)}
+Z0 = 16
+CG, CS = V + 2 * S, 2 * V + V + 2 * S
+PS_, TS_ = V + 2 * A, V + 3 * A
+NC = 2178.0
+CFG = {"iters": 600, "polish": 14000, "seed": 1, "hand": 8.0,
+       "fold": ((1, 1), (0, 0), (0, 0)),
+       "ch": (0, 256, 576, 896, 1280),
+       "parts": (2, 2, 2),
+       "joint": (0, 0, 0),
+       "pieces": (0, 640, 1280),
+       "inv": ("ss", "ss", "ss")}
 PLANS = (((1.0, 0.83, 1.3, 3.15, 0.42), 200.0, 1.3), ((1.0, 0.85, 1.0, 2.0, 0.5), 100.0, 1.7), ((1.0, 1.16, 2.25, 5.8, 0.63), 200.0, 1.3))
 
-_bf, _f, _i, _u = "bfloat16", "float32", "int32", "uint16"
+_bf, _f, _i, _u, _h = "bfloat16", "float32", "int32", "uint16", "float16"
 _SB = {
-    _bf: {"crd": V, "pat": V, "bn0": V, "bn1": V + A, "bn2": V + A, "bn3": V + A, "w0": V, "w1": V + A, "w2": V + A, "r256": 16, "pc": 128,
-          "ih": 128, "ione": 128, "ineg": 128, "cdr": L, "ipen": 128, "gm": 720, "bkp": 1024, "bkn": 1024, "bo": 128, "bw": 128, "sh": 384,
-          "z": L, "dh": L, "pb": 10 * L, "sg": L, "ml": 192, "pen": 576, "eq": 4096, "cutp": 128, "cutq": 128, "cutr": 128, "cum": 128,
-          "rr": 128, "pay0": 528, "pay1": 528, "jt": 528, "vnew": 256, "land": 6 * PW},
-    _f: {"curf": 80, "curg": 80, "col": 32, "rsel": 16, "gsel": 8, "ca": 16, "two": 16, "pw": 16, "pw2": 16, "iom": 128, "iog": 128, "jl": 32,
-         "cm": 320, "cf": 192, "vl": 16, "kf": 16, "kg": 16, "k1": 16, "k2": 16, "k3": 16, "k4": 16, "k5": 16, "k6": 16,
-         "ycs": 80, "yns": 256},
-    _i: {"nxi": 256, "curi": 80, "cura": 80, "curb": 80, "wti": 8, "ip": 8, "iq": 8, "ci": 192, "cj": 192, "li": 80, "lj": 80},
-    _u: {"nxl": 256, "xa": 192, "xb": 768, "ipay": 16, "itg": 32, "ijn": 16},
-    "float16": {"vw": 256, "sw": 128, "idf": 128, "xf": 320},
+    _bf: {"ca": Z0 + CS, "cb": Z0 + CS, "pg": 128, "ih": 128, "inh": 128, "ione": 128, "i4k": 128, "gm": 288, "bkp": 1024, "bkn": 1024,
+          "bo": 128, "sh": 384, "z": L, "dh": L, "sg": L, "ml": 256, "eq": 4096, "cutp": 128, "cum": 128, "pay0": 16 + TS_, "pay1": 16 + S,
+          "arr": 2 * S, "va": A, "land": 6 * PW, "inv": 1200, "ones": 128},
+    _f: {"pc": Z0 + PS_, "nxf": 256, "tc": 2 * TS_, "col": 48, "rsel": 16, "gsel": 8, "pm": 144, "iom": 128, "kh": 8, "pcf": 128,
+         "vl": 16, "vt": 256, "uph": 16, "k3": 16, "ycs": 80},
+    _i: {"pa": Z0 + PS_, "pb": Z0 + PS_, "nxi": 256, "curi": 80, "wti": 8, "ip": 8, "iq": 8, "li": 80, "lj": 80},
+    _u: {"x0": 320, "xs": 960, "xu": 960, "ipay": 16, "itg": 16, "pl": 16, "dl": 16},
+    _h: {"nxh": 256, "idp": 144, "gp": 144, "bw": 128, "sw": 128, "fo": 5 * L, "xf": 320, "xm": 320, "vw": 256, "pcn": 128, "cutr": 128,
+         "rr": 128, "tch": 128, "t16": 16},
 }
 SCRATCH = {k: ("sbuf", [128, n], d) for d, b in _SB.items() for k, n in b.items()}
-SCRATCH.update({k: ("psum", [128, 512], _f) for k in ("d0", "d1", "d2", "c0", "c1", "c2", "lb", "xk")})
+BANKS = ("d0", "d1", "d2", "d3", "lb", "ma", "mb", "xk")
+SCRATCH.update({k: ("psum", [128, 512], _f) for k in BANKS})
 SEMAPHORES = ["nv", "ns", "nt", "ng", "arr0", "arr1", "hin0", "hin1", "sent0", "sent1"] + ["dq%d" % k for k in range(20)]
 HE = 4
 
@@ -86,6 +95,9 @@ def build(T, topo, core, rank):
         ops.append({"n": name, "alts": alts, "deps": sorted(deps), "bank": bank, "lat": lat, "dma": dma, "ext": ext, "i": i})
         return i
 
+    def keys(name, lo, hi):
+        return ["%s.%d" % (name, b) for b in range(lo // 64, (hi + 63) // 64)]
+
     def cv(n, f=1.0):
         return (30.0, max(64.0, n * f), 0, 0, 0)
 
@@ -99,8 +111,8 @@ def build(T, topo, core, rank):
     def tt(name, out, in0, in1, op, n, r, w, bank=None):
         return add(name, {"v": (cv(n, 1.0 if bank else 2.0), lambda g: g.vector.tensor_tensor(out, in0, in1, op))}, r, w, bank)
 
-    def cp(name, out, in_, n, r, w, bank=None, both=False):
-        alts = {"v": (cv(n), lambda g: g.vector.tensor_copy(out, in_))}
+    def cp(name, out, in_, n, r, w, bank=None, both=True, f=1.0):
+        alts = {"v": (cv(n, f), lambda g: g.vector.tensor_copy(out, in_))}
         if both:
             alts["s"] = (cv(n), lambda g: g.scalar.activation(out, in_, ACT.Copy))
         return add(name, alts, r, w, bank)
@@ -110,18 +122,26 @@ def build(T, topo, core, rank):
                 "s": (cv(n), lambda g: g.scalar.activation(out, in_, ACT.Identity, bias=bi, scale=sc))}
         return add(name, alts, r, w, bank)
 
-    def ms(name, ap, c, n, w):
-        return add(name, {"v": (cv(n, 0.5), lambda g: g.vector.memset(ap, c))}, (), w)
+    def relu(name, out, in_, bi, n, r, w, bank=None):
+        alts = {"v": (cv(n), lambda g: g.vector.tensor_scalar(out, in_, bi(), 0.0, ALU.add, ALU.max)),
+                "s": (cv(n), lambda g: g.scalar.activation(out, in_, ACT.Relu, bias=bi()))}
+        return add(name, alts, r, w, bank)
+
+    def ms(name, ap, c, n, w, f=0.5):
+        small = {} if f == 1.0 else {"allow_small_or_imprecise_dtypes": True}
+        return add(name, {"v": (cv(n, f), lambda g: g.vector.memset(ap, c)),
+                          "g": ((150, 2.0 * n, 0, 0, 0), lambda g: g.iota(ap, [[0, n]], int(c), 0, **small))}, (), w)
 
     def red(name, out, in_, r, w):
         return add(name, {"v": (cv(16), lambda g: g.vector.tensor_reduce(out, in_, AxisListType.X, ALU.add))}, r, w)
 
-    def scan(name, out, a, b, init, op0, op1, r, w):
-        return add(name, {"v": (cv(64), lambda g: g.vector.tensor_tensor_scan(out, a, b, init, op0, op1))}, r, w)
-
-    def gather(name, out, win, off, n, r, w):
-        alts = {"v": ((55, 0, n, 0, 0), lambda g: g.vector.tensor_copy(out, win.indirect(off))),
-                "s": ((70, 0, n, 0, 0), lambda g: g.scalar.activation(out, win.indirect(off), ACT.Copy))}
+    def gather(name, out, win, off, n, r, w, bi=None):
+        if bi is None:
+            alts = {"v": ((55, 0, n, 0, 0), lambda g: g.vector.tensor_copy(out, win.indirect(off))),
+                    "s": ((70, 0, n, 0, 0), lambda g: g.scalar.activation(out, win.indirect(off), ACT.Copy))}
+        else:
+            alts = {"v": ((55, 0, n, 0, 0), lambda g: g.vector.tensor_scalar(out, win.indirect(off), bi, None, ALU.add)),
+                    "s": ((70, 0, n, 0, 0), lambda g: g.scalar.activation(out, win.indirect(off), ACT.Identity, bias=bi))}
         return add(name, alts, r, w)
 
     def gather_tt(name, out, win, off, in1, op, n, r, w):
@@ -137,9 +157,9 @@ def build(T, topo, core, rank):
             return ins
         return add(name, {"t": ((20, 0, 0, 0, sum(max(64, it[5]) for it in items)), fn)}, r, w, bank, after=after)
 
-    def dma(name, q, out, in_, nbytes, r, w):
+    def dma(name, q, out, in_, nbytes, r, w, after=()):
         fn = (lambda g: g.sync.dma_start(out, in_)) if q == "y" else (lambda g: g.scalar.dma_start(out, in_))
-        return add(name, {q: ((100.0, 0, 0, 0, 0), fn)}, r, w, lat=1800 + nbytes / 200.0, dma=True)
+        return add(name, {q: ((100.0, 0, 0, 0, 0), fn)}, r, w, lat=1800 + nbytes / 200.0, dma=True, after=after)
 
     def iota(name, out, pattern, base, cm, n, w, integer=False):
         if integer:
@@ -148,199 +168,219 @@ def build(T, topo, core, rank):
             fn = lambda g: g.iota(out, pattern, base, cm, allow_small_or_imprecise_dtypes=True)
         return add(name, {"g": ((150, 2.0 * n, 0, 0, 0), fn)}, (), w)
 
-    col = lambda k: T.col[:, k:k + 1]
-    GF, RF, PF, SHF, PARF, WT, WP, W4, SWF, KB, OFF, M3, TMP = 0, 1, 2, 3, 4, 5, 6, 7, 8, 9, 10, 14, 17
-    NM1, NQ, KC = col(TMP + 7), col(TMP + 8), col(TMP + 9)
+    def select(name, out, in_, pattern, op, fill, base, cm, n, r, w):
+        return add(name, {"g": ((190, 2.0 * n, 0, 0, 0), lambda g: g.affine_select(out, in_, pattern, op, fill, base, cm))}, r, w)
+
+    names = ["GF", "PF", "SHF", "PARF", "W4", "SWF", "C14", "C15", "OFF0", "OFF1", "M30", "M31", "M32", "NM1", "P2K", "N2K", "YB0", "YB1",
+             "NQ", "TH2", "TH3", "TH4", "KP", "KU", "KT", "TA", "TB", "TC", "TD", "TE", "P2Z"]
+    col = lambda k: T.col[:, names.index(k):names.index(k) + 1]
     gm = lambda fam, a: T.gm[:, fam * 144 + 15 - a: fam * 144 + 15 - a + 128]
-    GP, GT, GC, GW, G8 = 0, 1, 2, 3, 4
+    gp = lambda a: T.gp[:, 15 - a:15 - a + 128]
+    GC, GW = 0, 1
+    idf = T.idp[:, 0:128]
+    cut = CFG["ch"]
+    CH = [(cut[k], cut[k + 1]) for k in range(len(cut) - 1)]
+    NB = max((hi - lo) // 64 for lo, hi in CH)
+    rows = slice(0, 128, 16)
+    vb, mb = ("d3", "d3") if len(CH) < 4 else ("xk", "lb")
 
-    dma("ld_nx", "y", T.nxi[:, :], T.nx[:], 131072, (), ["nxi"])
+    PA = ["pa%d" % b for b in range(8)]
+    for k, (a, b) in enumerate(((0, 384), (384, 1792))):
+        add("fill", {"v": (cv(b - a), lambda g, a=a, b=b: g.vector.memset(T.pa[:, a:b], 0))}, (), PA[k:k + 1])
+    for k in range(4):
+        add("fill", {"s": (cv(384), lambda g, k=k: g.scalar.activation(T.pa[:, 1792 + 384 * k:2176 + 384 * k], T.pa[:, 0:384], ACT.Copy))}, PA[0:1], PA[2 + k:3 + k])
+    iota("fill6", T.pa[:, 3328:Z0 + V], [[0, 784]], 0, 0, 784, PA[6:7], True)
+    nx = dma("ld_nx", "y", T.pa[rows, Z0:Z0 + V], T.nx[:], 131072, (), PA)
+    c1 = dma("ld_c1", "y", T.ca[:, Z0 + 2048:Z0 + V], T.cards[:, 2048:V], 600000, (), ["ca1"], after=ops[nx]["deps"])
     dma("ld_cur", "y", T.curi[:, :], T.cur[:], 40960, (), ["curi"])
-    dma("ld_c0", "s", T.crd[:, 0:2048], T.cards[:, 0:2048], 1000000, (), ["crd0"])
-    dma("ld_c1", "s", T.crd[:, 2048:V], T.cards[:, 2048:V], 1000000, (), ["crd1"])
+    c0 = dma("ld_c0", "y", T.ca[:, Z0:Z0 + 2048], T.cards[:, 0:2048], 900000, (), ["ca0"])
     dma("ld_wt", "y", T.wti[:, 0:1], T.wt[:], 10000, (), ["wti"])
-    dma("ld_z", "y", T.z[:, :], T.z0[:], 600000, (), ["z0", "z1", "z2"])
+    dma("ld_z", "y", T.z[:, :], T.z0[:], 500000, (), ["z%d" % k for k in range(len(CH))])
+    dma("ld_cb", "y", T.cb[:, Z0:Z0 + V], T.cards[:, :], 1048576, (), ["cb0"], after=[c0, c1])
 
+    iota("pm", T.pm[:, :], [[-1, 144]], 0, 1, 144, ["pm"])
     iota("ip", T.ip[:, 0:2], [[16, 2]], 0, 1, 2, ["ip"], True)
+    iota("pg", T.pg[:, :], [[-16, 8], [0, 16]], 0, 1, 128, ["pg"])
     iota("iom", T.iom[:, :], [[1, 128]], 0, 0, 128, ["iom"])
-    iota("iog", T.iog[:, :], [[1, 8], [0, 16]], 0, 0, 128, ["iog"])
-    iota("jl", T.jl[:, :], [[1776, 2], [16, 16]], 272, 0, 32, ["jl"])
-    iota("pc", T.pc[:, :], [[1, 128]], 129, 0, 128, ["pc"])
+    ts("idp", T.idp[:, :], T.pm[:, :], 0.0, None, ALU.is_equal, None, 144, ["pm"], ["idp"])
+    for nms, base, step in ((["NM1"], -int(M1), 0), (["P2K", "N2K"], 2048, -4096), (["P2Z"], 2048 + Z0, 0), (["YB0", "YB1"], Z0 - 2048, -4096), (["NQ", "TH2", "TH3", "TH4"], -1, 2)):
+        k = names.index(nms[0])
+        iota(nms[0], T.col[:, k:k + len(nms)], [[step, len(nms)]], base, 0, len(nms), nms)
+    lin("gp0", T.gp[:, :], T.pm[:, :], 0.0, 0.0, 144, ["pm"], ["gp"])
+    ts("gp", T.gp[:, 15:143:16], T.pg[:, 0:128:16], 0.0, None, ALU.is_equal, None, 8, ["pg"], ["gp"])
     ts("ir", T.iq[:, 1:2], T.ip[:, 0:1], 15, None, ALU.bitwise_and, None, 1, ["ip"], ["iq1"])
-    cp("rf", col(RF), T.iq[:, 1:2], 1, ["iq1"], ["rf"])
-    ts("r256", T.r256[:, :], T.iom[:, 0:16], col(RF), 256.0, ALU.is_equal, ALU.mult, 16, ["iom", "rf"], ["r256"])
-    ms("pat0", T.pat[:, 0:1], 0.0, 1, ["pat"])
-    for k in range(11):
-        n = 1 << k
-        ts("pat%d" % k, T.pat[:, n:2 * n], T.pat[:, 0:n], T.r256[:, k:k + 1], None, ALU.add, None, n, ["pat", "r256"], ["pat"], f=0.5)
-    lin("patA", T.pat[:, 2048:3392], T.pat[:, 0:1344], 1.0, T.r256[:, 11:12], 1344, ["pat", "r256"], ["patA"], f=0.5)
-    lin("patB", T.pat[:, 3392:V], T.pat[:, 1344:2048], 1.0, T.r256[:, 11:12], 704, ["pat", "r256"], ["patB"], f=0.5)
     ts("ig", T.iq[:, 0:1], T.ip[:, 0:1], 4, None, ALU.arith_shift_right, None, 1, ["ip"], ["iq0"])
     ts("ish", T.iq[:, 3:4], T.ip[:, 1:2], 127, None, ALU.bitwise_and, None, 1, ["ip"], ["iq3"])
     ts("ipar", T.iq[:, 4:5], T.ip[:, 0:1], 1, None, ALU.bitwise_and, None, 1, ["ip"], ["iq4"])
-    cp("gf", col(GF), T.iq[:, 0:1], 1, ["iq0"], ["gf"])
-    cp("pf", col(PF), T.ip[:, 0:1], 1, ["ip"], ["pf"])
-    cp("shf", T.col[:, SHF:SHF + 2], T.iq[:, 3:5], 2, ["iq3", "iq4"], ["shf", "parf"])
-    cp("w4", col(W4), T.wti[:, 0:1], 1, ["wti"], ["w4"])
-    ts("rsel", T.rsel[:, :], T.iom[:, 0:16], col(RF), None, ALU.is_equal, None, 16, ["iom", "rf"], ["rsel"])
-    ts("gsel", T.gsel[:, :], T.iom[:, 0:8], col(GF), None, ALU.is_equal, None, 8, ["iom", "gf"], ["gsel"])
-    ms("two", T.two[:, :], 2.0, 16, ["two"])
-    scan("pw", T.pw[:, :], T.two[:, :], T.two[:, :], 1.0, ALU.mult, ALU.max, ["two"], ["pw"])
-    tt("pwy", T.pw2[:, :], T.pw[:, :], T.rsel[:, :], ALU.mult, 16, ["pw", "rsel"], ["pw2"])
-    red("wt0", col(TMP), T.pw2[:, :], ["pw2"], ["tmp"])
-    lin("wt", col(WT), col(TMP), 1.0 / 512, 0.0, 1, ["tmp"], ["wt"])
-    ts("wp0", col(TMP + 1), col(RF), 8.0, 16.0 - 1.0 / 256, ALU.is_lt, ALU.mult, 1, ["rf"], ["tmp1"])
-    ts("wp", col(WP), col(TMP + 1), 1.0 / 256, col(WT), ALU.add, ALU.mult, 1, ["tmp1", "wt"], ["wp"])
-    ms("gm", T.gm[:, :], 0.0, 720, ["gm%d" % k for k in range(5)])
-    for fam, sc, key in ((GP, col(WP), "wp"), (GW, col(W4), "w4"), (GC, -BIG, "gf"), (G8, 0.125, "gf"), (GT, col(WT), "wt")):
-        lin("gm%d" % fam, T.gm[:, fam * 144 + 15:fam * 144 + 143:16], T.gsel[:, :], sc, 0.0, 8, ["gsel", key], ["gm%d" % fam])
-    ts("bo", T.bo[:, :], T.iog[:, :], col(GF), None, ALU.is_equal, None, 128, ["iog", "gf"], ["bo"])
-    lin("bw", T.bw[:, :], T.bo[:, :], col(WP), 0.0, 128, ["bo", "wp"], ["bw"], f=0.5)
-    ts("ih", T.ih[:, :], T.iom[:, :], col(PF), 0.5, ALU.is_equal, ALU.mult, 128, ["iom", "pf"], ["ih"])
-    ts("idf", T.idf[:, :], T.ih[:, :], 2.0, None, ALU.mult, None, 128, ["ih"], ["idf"], f=0.5)
-    for k in range(3):
-        ms("pcol", col(TMP + 10 + k), 100.0 * (k + 1), 1, ["pcol%d" % k])
-    for nm, sc in (("ione", 2.0), ("ineg", -2.0)):
-        lin(nm, T[nm][:, :], T.ih[:, :], sc, 0.0, 128, ["ih"], [nm], f=0.5)
-    ts("ca", T.ca[:, 0:8], T.rsel[:, 0:8], T.rsel[:, 14:15], None, ALU.subtract, None, 8, ["rsel"], ["ca"])
-    lin("cb", T.ca[:, 8:16], T.rsel[:, 0:8], -1.0, T.rsel[:, 15:16], 8, ["rsel"], ["cb"])
-    for a in range(8):
-        lin("bkp%d" % a, T.bkp[:, 128 * a:128 * a + 128], T.bo[:, :], T.ca[:, a:a + 1], 0.0, 128, ["bo", "ca"], ["bkp%d" % a], f=0.5)
-        lin("bkn%d" % a, T.bkn[:, 128 * a:128 * a + 128], T.bo[:, :], T.ca[:, 8 + a:9 + a], 0.0, 128, ["bo", "cb"], ["bkn%d" % a], f=0.5)
-    lin("offa", col(TMP + 4), T.rsel[:, 15:16], M1, 0.0, 1, ["rsel"], ["offa"])
-    lin("offb", col(TMP + 5), T.rsel[:, 14:15], 0.25, col(TMP + 4), 1, ["rsel", "offa"], ["offb"])
-    ts("offc", col(TMP + 6), col(RF), 14.0, BIG, ALU.is_lt, ALU.mult, 1, ["rf"], ["offc"])
+    cp("gf", col("GF"), T.iq[:, 0:1], 1, ["iq0"], ["GF"])
+    cp("pf", col("PF"), T.ip[:, 0:1], 1, ["ip"], ["PF"])
+    cp("shf", T.col[:, names.index("SHF"):names.index("SHF") + 2], T.iq[:, 3:5], 2, ["iq3", "iq4"], ["SHF", "PARF"])
+    cp("w4", col("W4"), T.wti[:, 0:1], 1, ["wti"], ["W4"])
+    ts("gsel", T.gsel[:, :], T.iom[:, 0:8], col("GF"), None, ALU.is_equal, None, 8, ["iom", "GF"], ["gsel"])
+    ms("gm", T.gm[:, :], 0.0, 288, ["gm0", "gm1"])
+    lin("gw", T.gm[:, GW * 144 + 15:GW * 144 + 143:16], T.gsel[:, :], col("W4"), 0.0, 8, ["gsel", "W4"], ["gm%d" % GW])
+    lin("gc", T.gm[:, GC * 144 + 15:GC * 144 + 143:16], T.gsel[:, :], -BIG, 0.0, 8, ["gsel"], ["gm%d" % GC])
+    for nm, sc in (("ih", 0.5), ("inh", -0.5), ("ione", 1.0), ("i4k", -4096.0)):
+        lin(nm, T[nm][:, :], idf, sc, 0.0, 128, ["idp"], [nm], f=0.5)
+    ts("c14", col("C14"), T.iq[:, 1:2], 14.0, -0.125, ALU.is_equal, ALU.mult, 1, ["iq1"], ["C14"])
+    ts("c15a", col("TA"), T.iq[:, 1:2], 15.0, None, ALU.is_equal, None, 1, ["iq1"], ["TA"])
+    ts("c15", col("C15"), col("TA"), -0.125, 1.0, ALU.mult, ALU.add, 1, ["TA"], ["C15"])
+    for a in range(NB):
+        ts("bkp%d" % a, T.bkp[:, 128 * a:128 * a + 128], T.pg[:, :], float(a), col("C14"), ALU.is_equal, ALU.add, 128, ["pg", "C14"], ["bkp%d" % a], f=0.5)
+        ts("bkn%d" % a, T.bkn[:, 128 * a:128 * a + 128], T.pg[:, :], float(a), col("C15"), ALU.not_equal, ALU.subtract, 128, ["pg", "C15"], ["bkn%d" % a], f=0.5)
+    lin("offa", col("TE"), col("C14"), -2.0, 0.0, 1, ["C14"], ["TE"])
+    lin("offb", col("TB"), col("TA"), M1, col("TE"), 1, ["TA", "TE"], ["TB"])
+    ts("offc", col("TC"), T.iq[:, 1:2], 14.0, BIG, ALU.is_lt, ALU.mult, 1, ["iq1"], ["TC"])
     for k, off in enumerate((1.0, 17.0)):
-        lin("off%d" % k, col(OFF + k), col(TMP + 6), off, col(TMP + 5), 1, ["offb", "offc"], ["off%d" % k])
-    lin("ipen", T.ipen[:, :], T.ione[:, :], col(TMP + 6), 0.0, 128, ["ione", "offc"], ["ipen"], f=0.5)
-    ms("nm1", NM1, -M1, 1, ["nm1"])
-    ms("nq", NQ, -0.5, 1, ["nq"])
-    ts("swa", col(TMP + 2), col(PARF), -2.0, 1.0, ALU.mult, ALU.add, 1, ["parf"], ["tmp2"])
-    lin("swf", col(SWF), col(TMP + 2), 1.0, col(PF), 1, ["tmp2", "pf"], ["swf"])
-    ts("swm", T.sw[:, :], T.iom[:, :], col(SWF), None, ALU.is_equal, None, 128, ["iom", "swf"], ["sw"])
-    ts("kb", col(KB), col(PARF), 14.0, None, ALU.add, None, 1, ["parf"], ["kb"])
-    ts("kc", KC, col(PARF), -1.0, None, ALU.add, None, 1, ["parf"], ["kc"])
-    lin("jl2", T.jl[:, :], T.jl[:, :], 1.0, col(RF), 32, ["jl", "rf"], ["jl"])
+        lin("off%d" % k, col("OFF%d" % k), col("TC"), off, col("TB"), 1, ["TB", "TC"], ["OFF%d" % k])
+    ms("ones", T.ones[:, :], 4096.0, 128, ["ones"])
+    select("boa", T.bo[:, :], T.ones[:, :], [[-16, 8], [0, 16]], ALU.is_ge, 0.0, 0, 1, 128, ["ones"], ["bo"])
+    select("bob", T.bo[:, :], T.bo[:, :], [[16, 8], [0, 16]], ALU.is_ge, 0.0, 15, -1, 128, ["bo"], ["bo"])
+    ts("bw", T.bw[:, :], T.pg[:, :], 0.0, None, ALU.is_equal, None, 128, ["pg"], ["bw"], f=0.5)
+    ts("swa", col("TD"), col("PARF"), -2.0, 1.0, ALU.mult, ALU.add, 1, ["PARF"], ["TD"])
+    lin("swf", col("SWF"), col("TD"), 1.0, col("PF"), 1, ["TD", "PF"], ["SWF"])
+    ts("swm", T.sw[:, :], T.iom[:, :], col("SWF"), None, ALU.is_equal, None, 128, ["iom", "SWF"], ["sw"])
+    ts("kp", col("KP"), col("PARF"), -2.0, None, ALU.add, None, 1, ["PARF"], ["KP"])
+    ts("kt", col("KT"), col("PARF"), -258.0, None, ALU.add, None, 1, ["PARF"], ["KT"])
+    ts("ku", col("KU"), col("PARF"), -0.5, 1153.0, ALU.mult, ALU.add, 1, ["PARF"], ["KU"])
+    iota("pcf", T.pcf[:, :], [[2, 128]], int(NC), 0, 128, ["pcf"])
+    cp("pcn", T.pcn[:, :], T.pcf[:, :], 128, ["pcf"], ["pcn"])
+    iota("kh0", T.kh[:, :], [[16, 8]], 0, 1, 8, ["kh"])
+    ts("kh1", col("TD"), col("GF"), -8.0, None, ALU.mult, None, 1, ["GF", "SWF"], ["TD"])
+    lin("kh2", T.kh[:, :], T.kh[:, :], 0.5, col("TD"), 8, ["kh", "TD"], ["kh"])
     for e in range(3):
-        red("m3%d" % e, col(M3 + e), T.gsel[:, e:8:3], ["gsel"], ["m3%d" % e])
-        ts("sh%d" % e, T.sh[:, 128 * e:128 * e + 128], T.iom[:, :], col(SHF), col(M3 + e), ALU.is_equal, ALU.mult, 128, ["iom", "shf", "m3%d" % e], ["sh%d" % e])
-    ms("pay0", T.pay0[:, 0:PW], 0.0, PW, ["pay0"])
-    ms("pay1", T.pay1[:, 0:PW], 0.0, PW, ["pay1"])
-    ms("jt", T.jt[:, 0:272], 0.0, 272, ["jta"])
+        red("m3%d" % e, col("M3%d" % e), T.gsel[:, e:8:3], ["gsel"], ["M3%d" % e])
+        ts("sh%d" % e, T.sh[:, 128 * e:128 * e + 128], T.iom[:, :], col("SHF"), col("M3%d" % e), ALU.is_equal, ALU.mult, 128, ["iom", "SHF", "M3%d" % e], ["sh%d" % e])
+    for nm in ("ca", "cb"):
+        ms(nm + "z", T[nm][:, 0:Z0], 0.0, Z0, [nm + "z"])
+        ms(nm + "y", T[nm][:, Z0 + V:Z0 + CG], 0.0, CG - V, [nm + "y"])
+    ms("pay0", T.pay0[:, 16:16 + S], 0.0, S, ["pay0"])
+    for k in range(8):
+        iota("junk", T.pb[:, 514 * k:514 * k + 514], [[0, 514]], 0, 0, 514, ["pb%d" % k], True)
+    for t in range(RO - 1):
+        iota("tc%d" % t, T.tc[:, TS_ * t:TS_ * t + S], [[2, S]], V, 0, S, ["tc%d" % t])
 
-    cp("nxl", T.nxl[:, :], T.nxi[:, :], 256, ["nxi"], ["nxl"])
-    Bt, Wt = [T.bn0, T.bn1, T.bn2, T.bn3], [T.w0, T.w1, T.w2]
-    BK = [["bn0_%d" % h for h in range(8)], ["bn1"], ["bn2"], ["bn3"]]
-    WK = [["w0_%d" % h for h in range(8)], ["w1"], ["w2"]]
-    for h in range(8):
-        ov = T.nxl[:, 32 * h:32 * h + 32]
-        gather("bn%d" % h, T.bn0[:, 512 * h:512 * h + 512], T.pat[:, :], ov, 512, ["pat", "patA", "patB", "nxl"], ["bn0_%d" % h])
-        gather("w0_%d" % h, T.w0[:, 512 * h:512 * h + 512], T.crd[:, :], ov, 512, ["crd0", "crd1", "nxl"], ["w0_%d" % h])
-    dma("cp_b1", "y", T.bn1[:, 0:V], T.bn0[:, :], 1048576, BK[0], BK[1])
-    dma("cp_w1", "y", T.w1[:, 0:V], T.w0[:, :], 1048576, WK[0], WK[1])
-    ts("cura", T.cura[:, :], T.curi[:, :], 255, None, ALU.bitwise_and, None, 80, ["curi"], ["cura"])
-    ts("curb", T.curb[:, :], T.curi[:, :], 8, None, ALU.arith_shift_right, None, 80, ["curi"], ["curb"])
-    ts("curf", T.curf[:, :], T.cura[:, :], 16.0, None, ALU.mult, None, 80, ["cura"], ["curf"])
-    tt("curg", T.curg[:, :], T.curf[:, :], T.curb[:, :], ALU.add, 80, ["curf", "curb"], ["curg"])
-    cp("x0a", T.xa[:, 0:16], T.curg[:, 0:16], 16, ["curg"], ["xa0_0"])
-    cp("x0b", T.xb[:, 0:64], T.curg[:, 16:80], 64, ["curg"], ["xb0_0"])
+    dma("ld_pb", "y", T.pb[rows, Z0:Z0 + V], T.nx[:], 131072, (), ["pb"] + ["pb%d" % k for k in range(8)])
+    Pt, PK = [T.pa, T.pb, T.pa, T.pc], [PA, ["pb"], PA, ["pc"]]
+    CA = ["ca0", "ca1", "caz", "cay"]
+    Ct, CK = [T.ca, T.cb, T.ca], [CA, ["cb0", "cbz", "cby"], CA]
+    cp("x0", T.x0[:, 0:80], T.curi[:, :], 80, ["curi"], keys("x0_0", 0, L))
 
-    Dk, Ck = (T.d0, T.d1, T.d2), (T.c0, T.c1, T.c2)
     rts = routes(T, topo)
 
-    def xl(part, par, s, lo=0, hi=None):
-        n = 16 if part == "a" else 64
-        buf = T.xa if part == "a" else T.xb
-        b = (6 * par + s) * n
-        return buf[:, b + lo:b + (n if hi is None else hi)]
+    def parts(t):
+        return [(0, L)] if CFG["parts"][t] == 1 else [(0, CH[0][1]), (CH[0][1], L)]
 
-    def chunk_list(par, s, ch):
-        src = s - 1 if s < 5 else 5
-        if ch == 0:
-            return xl("a", par, src), "xa%d_%d" % (par, src)
-        return xl("b", par, src, 32 * ch - 32, 32 * ch), "xb%d_%d" % (par, src)
+    def part_of(t, lo):
+        return [p for p in parts(t) if p[0] <= lo < p[1]][0]
 
-    def pbv(par, s, lo, hi, step=1):
-        b = (5 * par + s - 1) * L
-        return T.pb[:, b + lo:b + hi:step] if step > 1 else T.pb[:, b + lo:b + hi]
+    def xl(t, k, lo, hi):
+        if k == 0:
+            ap = T.x0[:, 80 * t + lo // 16:80 * t + hi // 16]
+        elif k < 5:
+            p0, p1 = part_of(t, lo)
+            b = 320 * t + p0 // 4 + (k - 1) * (p1 - p0) // 16 - p0 // 16
+            ap = T.xs[:, b + lo // 16:b + hi // 16]
+        elif k == 5:
+            ap = T.xu[:, 320 * t + lo // 16:320 * t + hi // 16]
+        else:
+            p0, p1 = part_of(t, lo)
+            b = 320 * t + 80 + 3 * p0 // 16 + (k - 6) * (p1 - p0) // 16 - p0 // 16
+            ap = T.xu[:, b + lo // 16:b + hi // 16]
+        return ap, keys("x%d_%d" % (k, t), lo, hi)
 
-    def list_set(name, out, fam, src, n, r, w, bank):
-        return mm(name, [(out, gm(fam, a), src(a), a == 0, a == 15, n) for a in range(16)], r + ["gm%d" % fam], w, bank)
+    def fo(s, lo, hi, step=1):
+        b = (s - 1) * L
+        return T.fo[:, b + lo:b + hi:step] if step > 1 else T.fo[:, b + lo:b + hi]
 
-    def walk_lists(t, part):
-        par = t % 2
-        n, o, lo, hi = (16, 0, 0, 256) if part == "a" else (64, 16, 256, L)
-        zk = ["z0"] if part == "a" else ["z1", "z2"]
-        ps, pu, bank = (T.c0[:, 128:144], T.c0[:, 304:320], "c0") if part == "a" else (T.lb[:, 64:128], T.lb[:, 208:272], "lb")
-        list_set("cl%s%d" % (part, t), ps, GW, lambda a: T.z[:, lo + a:hi:16], n, zk, ["pcl" + part], bank)
-        cp("cli", T.li[:, o:o + n], ps, n, ["pcl" + part], ["li" + part], bank)
-        ts("clj", T.lj[:, o:o + n], T.li[:, o:o + n], 3, None, ALU.bitwise_and, None, n, ["li" + part], ["lj" + part])
-        for s in range(4):
-            ts("cm", T.cm[:, 4 * o + s * n:4 * o + s * n + n], T.lj[:, o:o + n], float(s), None, ALU.is_equal, None, n, ["lj" + part], ["cm%s%d" % (part, s)])
-        buf = T.xa if part == "a" else T.xb
-        b = (6 * par + 1) * n
-        xf = T.xf[:, 4 * o:4 * o + 4 * n]
-        ts("xf", xf, buf[:, b:b + 4 * n], -2048.0, None, ALU.add, None, 4 * n, ["x%s%d_%d" % (part, par, s) for s in range(1, 5)], ["xf" + part], f=0.5)
-        tt("xm", xf, xf, T.cm[:, 4 * o:4 * o + 4 * n], ALU.mult, 4 * n, ["xf" + part] + ["cm%s%d" % (part, s) for s in range(4)], ["xf" + part])
-        mm("us" + part, [(pu, T.idf[:, :], T.xf[:, 4 * o + s * n:4 * o + s * n + n], s == 0, s == 3, n) for s in range(4)],
-           ["idf", "xf" + part], ["pus" + part], bank)
-        ts("ul", xl(part, par, 5), pu, 2048.0, None, ALU.add, None, n, ["pus" + part], ["x%s%d_5" % (part, par)], bank)
+    def list_set(name, out, src, n, r, w, bank, fam=None):
+        st = gp if fam is None else (lambda a: gm(fam, a))
+        return mm(name, [(out, st(a), src(a), a == 0, a == 15, n) for a in range(16)], r + ["gp" if fam is None else "gm%d" % fam], w, bank)
+
+    def folded(t, lo):
+        return CFG["fold"][t][parts(t).index(part_of(t, lo))]
+
+    over = {}
+
+    def walk_lists(t, j, first):
+        lo, hi = parts(t)[j]
+        n, o = (hi - lo) // 16, lo // 16
+        one = len(parts(t)) == 1
+        b1, b2 = ("ma", "mb") if one else (("ma", "ma") if j == 0 else ("mb", "mb"))
+        pcl, pcy = T[b1][:, 0:n], T[b1][:, n:4 * n]
+        q = 0 if one else 4 * n
+        psel, pus = T[b2][:, q:q + 4 * n], (T[b2][:, 4 * n:5 * n] if one else pcl)
+        kus = "B%s2" % b2 if one else "B%s0" % b1
+        zk = ["z%d" % k for k, c in enumerate(CH) if lo <= c[0] < hi]
+        xk = lambda k: xl(t, k, lo, hi)
+        e = CFG["inv"][t][j]
+        ib = 400 * t + 5 * o
+        iv = lambda s0, s1: T.inv[:, ib + (s0 - 1) * n:ib + s1 * n]
+        ik = "inv%d%d" % (t, j)
+        iks = [ik + x for x in ("e1", "2", "3", "4", "e5")]
+        yb = col("YB1" if e == "v" else "YB0")
+        if first:
+            over[t, lo] = (iv, ik, yb)
+            list_set("cl%d%d" % (t, j), pcl, lambda a: T.z[:, lo + a:hi:16], n, zk, ["B%s%d" % (b, k) for b in (b1, b2) for k in range(4)], b1, GW)
+            cp("cli", T.li[:, o:o + n], pcl, n, ["B%s0" % b1], keys("li", lo, hi), b1)
+            lj = T.lj[:, o:o + n]
+            ts("clj", lj, T.li[:, o:o + n], 3, None, ALU.bitwise_and, None, n, keys("li", lo, hi), keys("lj", lo, hi))
+            for s, c in ((1, -1.0), (5, 1.0)):
+                ms("inve", iv(s, s), c - (e == "v"), n, [ik + "e%d" % s])
+            for s in range(2, 5):
+                if e == "s":
+                    fn = lambda g, s=s: g.scalar.activation(iv(s, s), lj, ACT.Sign, bias=col("TH%d" % s), scale=-2.0)
+                else:
+                    fn = lambda g, s=s: g.vector.tensor_scalar(iv(s, s), lj, s - 1.5, -2.0, ALU.is_gt, ALU.mult)
+                add("inv", {e: (cv(n), fn)}, keys("lj", lo, hi) + ["TH%d" % s], [ik + str(s)])
+            mm("sel%d%d" % (t, j), [(psel, T.ih[:, :], iv(2, 5), True, False, 4 * n), (psel, T.inh[:, :], iv(1, 4), False, True, 4 * n)],
+               iks + ["ih", "inh"], ["B%s3" % b2], b2)
+            return
+        xf, xm = T.xf[:, 4 * o:4 * o + 4 * n], T.xm[:, 4 * o:4 * o + 4 * n]
+        src = T.xs[:, 320 * t + 4 * o:320 * t + 4 * o + 4 * n]
+        ts("xf", xf, src, -2048.0 - Z0 * folded(t, lo), None, ALU.add, None, 4 * n, sum((xk(s)[1] for s in range(1, 5)), []), keys("xf", lo, hi), f=0.5)
+        if not folded(t, lo):
+            mm("cy%d%d" % (t, j), [(pcy, idf, T.xf[:, 4 * o + n:4 * o + 4 * n], True, False, 3 * n), (pcy, T.i4k[:, :], iv(2, 4), False, True, 3 * n)],
+               iks + ["idp", "i4k"] + keys("xf", lo, hi), ["B%s1" % b1], b1)
+            b = 320 * t + 80 + 3 * o
+            relu("yl", T.xu[:, b:b + 3 * n], pcy, lambda: yb, 3 * n, ["B%s1" % b1, "YB0", "YB1"], sum((xk(k)[1] for k in range(6, 9)), []), b1)
+        tt("xm", xm, psel, xf, ALU.mult, 4 * n, ["B%s3" % b2] + keys("xf", lo, hi), keys("xm", lo, hi), b2)
+        mm("us%d%d" % (t, j), [(pus, idf, T.xm[:, 4 * o + s * n:4 * o + s * n + n], s == 0, s == 3, n) for s in range(4)],
+           ["idp"] + keys("xm", lo, hi), [kus], b2)
+        lin("ul", xk(5)[0], pus, 1.0, col("P2K"), n, [kus, "P2K"], xk(5)[1], b2)
 
     def z_chain(t, ch):
-        par = t % 2
         lo, hi = CH[ch]
         n = hi - lo
         nb = n // 64
-        D, C, dk, ck, zk, hk = Dk[ch][:, 0:n], Ck[ch], "d%d" % ch, "c%d" % ch, "z%d" % ch, "dh%d" % ch
+        dk, zk, hk = "d%d" % ch, "z%d" % ch, "dh%d" % ch
+        D, C = T[dk][:, 0:n], T[dk][:, 448:512]
         zz, dh, sgv, ml = T.z[:, lo:hi], T.dh[:, lo:hi], T.sg[:, lo:hi], T.ml[:, 64 * ch:64 * ch + 64]
-        ci, cj, cf = T.ci[:, 64 * ch:64 * ch + 64], T.cj[:, 64 * ch:64 * ch + 64], T.cf[:, 64 * ch:64 * ch + 64]
-        mm("cc%d%d" % (t, ch), [(C[:, 64:128], gm(GW, a), T.z[:, lo + 64 * a:lo + 64 * a + 64], a == 0, a == nb - 1, 64) for a in range(nb)],
-           [zk, "gm3"], ["pcc%d" % ch], ck)
-        cp("cci", ci, C[:, 64:128], 64, ["pcc%d" % ch], ["ci%d" % ch], ck)
-        ts("ccj", cj, ci, 3, None, ALU.bitwise_and, None, 64, ["ci%d" % ch], ["cj%d" % ch])
-        cp("ccf", cf, cj, 64, ["cj%d" % ch], ["cf%d" % ch])
-        for s in range(2, 5):
-            pen = T.pen[:, 192 * ch + 64 * (s - 2):192 * ch + 64 * (s - 1)]
-            add("pen", {"v": (cv(64), lambda g, s=s, pen=pen: g.vector.tensor_scalar(pen, cf, float(s - 1), 100.0, ALU.is_lt, ALU.mult)),
-                        "s": (cv(64), lambda g, s=s, pen=pen: g.scalar.activation(pen, cf, ACT.Relu, bias=col(TMP + 8 + s), scale=-100.0))},
-                ["cf%d" % ch, "pcol%d" % (s - 2)], ["pen%d_%d" % (ch, s)])
         for s in range(1, 6):
-            off, ok = chunk_list(par, s, ch)
-            if s == 5 and ch in CFG["rev"]:
-                cd, kk = (T.jt[:, 272:528], "jtc") if ch == 0 and t < RO - 1 else (T.cdr[:, lo:hi], "cdr%d" % ch)
-                if kk != "jtc":
-                    gather("vr%d%d" % (t, ch), cd, Wt[t][:, 0:V], off, n, WK[t] + [ok], [kk])
-                mm("rv%d%d" % (t, ch), [(D, T.ione[:, :], cd, True, False, n), (D, T.ineg[:, :], zz, False, True, n)], [kk, zk, "ione", "ineg"], [dk], dk)
-                add("abs%d%d" % (t, ch), {"s": (cv(n), lambda g: g.scalar.activation(zz, D, ACT.Abs))}, [dk], [zk], dk)
-                break
-            gather_tt("gs%d%d%d" % (t, ch, s), dh, Wt[t][:, 0:V], off, zz, ALU.subtract, n, WK[t] + [ok, zk], [hk])
+            fold = folded(t, lo)
+            off, ok = xl(t + 1, 0, lo, hi) if s == 5 else xl(t, s if fold or s == 1 else s + 4, lo, hi)
+            win = Ct[t][:, Z0:Z0 + V] if s == 5 or (s == 1 and not fold) else Ct[t][:, 0:Z0 + V]
+            gather_tt("gs%d%d%d" % (t, ch, s), dh, win, off, zz, ALU.subtract, n, CK[t] + ok + [zk], [hk])
             if s == 5:
                 add("abs%d%d" % (t, ch), {"s": (cv(n), lambda g: g.scalar.activation(zz, dh, ACT.Abs))}, [hk], [zk])
                 break
-            so = add("sg%d%d%d" % (t, ch, s), {"s": (cv(n), lambda g: g.scalar.activation(sgv, dh, ACT.Sign, bias=NQ)),
+            so = add("sg%d%d%d" % (t, ch, s), {"s": (cv(n), lambda g: g.scalar.activation(sgv, dh, ACT.Sign, bias=col("NQ"), scale=2.0)),
                                                "v": (cv(n, 0.5), lambda g: g.vector.tensor_scalar(sgv, dh, 0.0, 2.0, ALU.is_gt, ALU.mult))},
-                     [hk, "nq"], ["sg%d" % ch])
-            items = [(C[:, 0:64], gm(GC, a), T.sg[:, lo + 64 * a:lo + 64 * a + 64], a == 0, s == 1 and a == nb - 1, 64) for a in range(nb)]
-            rk = ["sg%d" % ch, "gm2"]
-            if s > 1:
-                b = 192 * ch + 64 * (s - 2)
-                items.append((C[:, 0:64], T.ipen[:, :], T.pen[:, b:b + 64], False, True, 64))
-                rk += ["ipen", "pen%d_%d" % (ch, s)]
-            mm("cnt%d%d%d" % (t, ch, s), items, rk, ["pcn%d" % ch], ck)
-            oc = lambda so=so: col(OFF + (1 if ops[so]["e"] == "v" else 0))
-            add("ml%d%d%d" % (t, ch, s), {"v": (cv(64), lambda g, oc=oc: g.vector.tensor_scalar(ml, C[:, 0:64], oc(), 0.0, ALU.add, ALU.max)),
-                                          "s": (cv(64), lambda g, oc=oc: g.scalar.activation(ml, C[:, 0:64], ACT.Relu, bias=oc()))},
-                ["pcn%d" % ch, "off0", "off1"], ["ml%d" % ch], ck)
+                     [hk, "NQ"], ["sg%d" % ch])
+            mm("cnt%d%d%d" % (t, ch, s), [(C, gm(GC, a), T.sg[:, lo + 64 * a:lo + 64 * a + 64], a == 0, a == nb - 1, 64) for a in range(nb)],
+               ["sg%d" % ch, "gm%d" % GC, "B" + dk], ["pcn%d" % ch], dk)
+            relu("ml%d%d%d" % (t, ch, s), ml, C, lambda so=so: col("OFF1" if ops[so]["e"] == "v" else "OFF0"), 64,
+                 ["pcn%d" % ch, "OFF0", "OFF1"], ["ml%d" % ch], dk)
             items = [(D, T.ih[:, :], dh, True, False, n)]
             for bk in (T.bkp, T.bkn):
-                items += [(Dk[ch][:, 64 * a:64 * a + 64], bk[:, 128 * a:128 * a + 128], ml, False, False, 64) for a in range(nb)]
+                items += [(T[dk][:, 64 * a:64 * a + 64], bk[:, 128 * a:128 * a + 128], ml, False, False, 64) for a in range(nb)]
             items.append((D, T.ione[:, :], zz, False, True, n))
             mm("upd%d%d%d" % (t, ch, s), items, ["ml%d" % ch, "ih", "ione", hk, zk] + ["bk%s%d" % (x, a) for a in range(nb) for x in "pn"], [dk], dk)
-            lin("zo%d%d%d" % (t, ch, s), zz, D, 1.0, NM1, n, [dk, "nm1"], [zk], dk)
+            lin("zo%d%d%d" % (t, ch, s), zz, D, 1.0, col("NM1"), n, [dk, "NM1"], [zk], dk)
         if t == RO - 1:
             dma("st_z%d" % ch, "y", T.yz[:, lo:hi], zz, n * 256, [zk], ["yz%d" % ch])
 
-    def send(g, t, pay):
+    def send(g, t):
         near = T.cores[[r for r, h in rts[rank] if h is None][0]]
         trs, k = [], 0
         for e, (r, h) in enumerate(rts[rank]):
@@ -353,145 +393,176 @@ def build(T, topo, core, rank):
                 k += 1
             s = (3 * t + e) * PW
             trs.append(RemoteDMATransfer(dst_ids=[DstId(rid=rid, pnc=pid)], dma_engine_mask=as_mask(engs), remote_sem=sem,
-                                         src=pay[:, 0:PW], dst=T.land[:, s:s + PW]))
+                                         src=T["pay%d" % t][:, 8:8 + PW], dst=T.land[:, s:s + PW]))
         g.remote_dma_fused(trs, local_sem=T.sem["sent%d" % t])
 
     for t in range(RO):
-        par, nxt = t % 2, (t + 1) % 2
-        W, B = Wt[t], Bt[t]
-        LA, LB = T.c0[:, 144:160], T.lb[:, 0:64]
+        one = len(parts(t)) == 1
+        pieces = [(a, b) for a, b in zip(CFG["pieces"], CFG["pieces"][1:])] if one else CH
 
-        def ptr(s, ch):
-            lo, hi = CH[ch]
-            off, ok = chunk_list(par, s, ch)
-            gather("p%d%d%d" % (t, ch, s), pbv(par, s, lo, hi), B[:, 0:V], off, hi - lo, BK[t] + [ok], ["pb%d_%d_%d" % (par, ch, s)])
+        def ptr(s, lo, hi):
+            off, ok = xl(t, s - 1 if s < 5 else 5, lo, hi)
+            win = Pt[t][:, 0:Z0 + V] if 1 < s < 5 and folded(t, lo) else Pt[t][:, Z0:Z0 + V]
+            gather("p%d%d_%d" % (t, s, lo), fo(s, lo, hi), win, off, hi - lo, PK[t] + ok + ["N2K"], keys("fo%d" % s, lo, hi), col("N2K"))
 
-        def lists(s, part):
-            dst = (par, s) if s < 5 else (nxt, 0)
-            if part == "a":
-                list_set("la%d%d" % (t, s), LA, GP, lambda a: pbv(par, s, a, A, 16), 16, ["pb%d_0_%d" % (par, s)], ["pla"], "c0")
-                cp("xa", xl("a", dst[0], dst[1]), LA, 16, ["pla"], ["xa%d_%d" % dst], "c0")
-            else:
-                list_set("lb%d%d" % (t, s), LB, GP, lambda a: pbv(par, s, A + a, L, 16), 64, ["pb%d_%d_%d" % (par, ch, s) for ch in (1, 2)], ["plb"], "lb")
-                cp("xb", xl("b", dst[0], dst[1]), LB, 64, ["plb"], ["xb%d_%d" % dst], "lb")
+        def lists(s, lo, hi):
+            q = 80 * (s % 2) + 160 * (s == 5)
+            ps, pk = T.lb[:, q + lo // 16:q + hi // 16], keys("Blb%d" % q, lo, hi)
+            mine = [p for p in parts(t) if lo <= p[0] < hi]
+            more = [p for p in mine if 1 < s < 5 and folded(t, p[0])]
+            items = [(ps, gp(a), fo(s, lo + a, hi, 16), a == 0, a == 15 and not more, (hi - lo) // 16) for a in range(16)]
+            items += [(T.lb[:, q + p[0] // 16:q + p[1] // 16], T.i4k[:, :], over[t, p[0]][0](s, s), False, p == more[-1], (p[1] - p[0]) // 16) for p in more]
+            mm("ls%d%d_%d" % (t, s, lo), items, keys("fo%d" % s, lo, hi) + ["gp", "i4k"] + [over[t, p[0]][1] + str(s) for p in more], pk, "lb")
+            for p0, p1 in mine:
+                out, ok = xl(t, s, p0, p1) if s < 5 else xl(t + 1, 0, p0, p1)
+                src, n, rk = T.lb[:, q + p0 // 16:q + p1 // 16], (p1 - p0) // 16, keys("Blb%d" % q, p0, p1)
+                if s == 5 and p0 == 0:
+                    cp("vl", T.vl[:, :], T.lb[:, q:q + 16], 16, keys("Blb%d" % q, 0, A), ["vl"], "lb")
+                if (p0, p1) in more:
+                    relu("xl", out, src, lambda p0=p0, t=t: over[t, p0][2], n, rk + ["YB0", "YB1"], ok, "lb")
+                else:
+                    bi = "P2Z" if s < 5 and folded(t, p0) else "P2K"
+                    lin("xl", out, src, 1.0, col(bi), n, rk + [bi], ok, "lb")
 
+        for j in range(len(parts(t))):
+            walk_lists(t, j, True)
         for s in range(1, 5):
-            for ch in range(3):
-                ptr(s, ch)
-            lists(s, "a")
-            lists(s, "b")
-        walk_lists(t, "a")
-        pR, pRk = pbv(par, 5, 0, A), "pb%d_0_5" % par
-        ptr(5, 0)
-        up = mm("upart", [(T.xk[:, 400:416], T.sw[:, :], T.xf[:, 16 * s:16 * s + 16], s == 0, s == 3, 16) for s in range(4)], ["sw", "xfa"], ["pup"], "xk")
-        mm("vwide", [(T.xk[:, 0:256], T.bw[:, :], pR, True, True, 256)], ["bw", pRk], ["pvw"], "xk")
-        list_set("lv%d" % t, LA, GP, lambda a: pbv(par, 5, a, A, 16), 16, [pRk], ["pla"], "c0")
-        ts("vw", T.vw[:, :], T.xk[:, 0:256], -2048.0, None, ALU.add, None, 256, ["pvw"], ["vw"], "xk")
-        ts("vl", T.vl[:, :], LA, -2048.0, None, ALU.add, None, 16, ["pla"], ["vl"], "c0")
-        if t < RO - 1:
-            cp("xa0", xl("a", nxt, 0), LA, 16, ["pla"], ["xa%d_0" % nxt], "c0")
-        PS, PR = T.xk[:, 256:384], T.xk[:, 384:400]
+            for lo, hi in pieces:
+                ptr(s, lo, hi)
+            for lo, hi in ([(0, L)] if CFG["joint"][t] else parts(t)):
+                lists(s, lo, hi)
+        walk_lists(t, 0, False)
+        p1 = parts(t)[0][1]
+        for lo, hi in pieces:
+            if hi <= p1:
+                ptr(5, lo, hi)
+        n0 = p1 // 16
+        up = mm("upart", [(T.xk[:, 400:416], T.sw[:, :], T.xm[:, n0 * s:n0 * s + 16], s == 0, s == 3, 16) for s in range(4)],
+                ["sw", "Bxk"] + keys("xm", 0, p1), ["pup"], "xk")
+        uh = lin("uph", T.uph[:, :], T.xk[:, 400:416], 0.5, col("KU"), 16, ["pup", "KU"], ["uph"], "xk")
+        mm("vwide", [(T[vb][:, 0:256], T.bw[:, :], fo(5, 0, A), True, True, 256)], ["bw", "B" + vb] + keys("fo5", 0, A), ["pvw"], vb)
+        lists(5, 0, p1)
+        cp("vw", T.vw[:, :], T[vb][:, 0:256], 256, ["pvw"], ["vw"], vb)
+        lin("vt", T.vt[:, :], T[vb][:, 0:256], 1.0, col("P2K"), 256, ["pvw", "P2K"], ["vt"], vb)
+        PS, PR, PT = T.xk[:, 256:384], T.xk[:, 384:400], T.xk[:, 416:424]
         for k in range(16):
-            ts("eq%d" % k, T.eq[:, 256 * k:256 * k + 256], T.vw[:, :], T.vl[:, k:k + 1], None, ALU.is_equal, None, 256, ["vw", "vl"], ["eq%d" % k], f=0.5)
+            ts("eq%d" % k, T.eq[:, 256 * k:256 * k + 256], T.vw[:, :], T.vl[:, k:k + 1], 1.0 / 256, ALU.is_equal, ALU.subtract, 256, ["vw", "vl"], ["eq%d" % k], f=0.5)
             if k % 2 == 1:
                 items = [(PS, T.bo[:, :], T.eq[:, 256 * kk + h:256 * kk + 256:2], kk == 0 and h == 0, kk == 15 and h == 1, 128)
                          for kk in (k - 1, k) for h in range(2)]
-                mm("S%d" % k, items, ["bo", "eq%d" % (k - 1), "eq%d" % k], ["pS"], "xk", after=[up])
-        ts("cutp", T.cutp[:, :], PS, 2.0, None, ALU.is_equal, None, 128, ["pS"], ["cutp"], "xk")
-        ts("cutq", T.cutq[:, :], PS, 2.0, None, ALU.not_equal, None, 128, ["pS"], ["cutq"], "xk")
-        scan("cum", T.cum[:, :], T.cutp[:, :], T.cutp[:, :], 0.0, ALU.add, ALU.max, ["cutp"], ["cum"])
-        tt("cutr", T.cutr[:, :], T.cutq[:, :], T.pc[:, :], ALU.mult, 128, ["cutq", "pc"], ["cutr"])
+                mm("S%d" % k, items, ["bo", "eq%d" % (k - 1), "eq%d" % k, "pT"], ["pS"], "xk", after=[up, uh])
+        ts("cutp", T.cutp[:, :], PS, 0.0, None, ALU.is_equal, None, 128, ["pS"], ["cutp"], "xk")
+        tt("cutr", T.cutr[:, :], PS, T.pcn[:, :], ALU.min, 128, ["pS", "pcn"], ["cutr"], "xk")
+        add("cum", {"v": (cv(64), lambda g: g.vector.tensor_tensor_scan(T.cum[:, :], T.cutp[:, :], T.cutp[:, :], 0.0, ALU.add, ALU.max))}, ["cutp"], ["cum"])
         tt("rr", T.rr[:, :], T.cutr[:, :], T.cum[:, :], ALU.max, 128, ["cutr", "cum"], ["rr"])
-        list_set("R%d" % t, PR, G8, lambda a: T.rr[:, a // 2:128:8], 16, ["rr"], ["pR"], "xk")
-        pay = (T.pay0, T.pay1, None)[t]
+        list_set("R%d" % t, PR, lambda a: T.rr[:, a // 2:128:8], 16, ["rr"], ["pR"], "xk")
         if t < RO - 1:
-            ts("ipay", T.ipay[:, :], PR, col(KB), None, ALU.add, None, 16, ["pR", "kb"], ["ipay"], "xk")
-            lin("kf", T.kf[:, :], PR, 1.0, col(KB), 16, ["pR", "kb"], ["kf"], "xk")
-            lin("kg", T.kg[:, :], PR, 1.0, KC, 16, ["pR", "kc"], ["kg"], "xk")
-            ts("m", pay[:, 0:1], T.cum[:, 127:128], 2.0, 128.0, ALU.mult, ALU.min, 1, ["cum"], ["pay%d" % t])
-        ts("k1", T.k1[:, :], PR, -257.0, 16384.0, ALU.add, ALU.mult, 16, ["pR"], ["k1"], "xk")
-        tt("k2", T.k2[:, :], T.k1[:, :], T.jl[:, 16:32], ALU.min, 16, ["k1", "jl"], ["k2"])
-        tt("k3", T.k3[:, :], T.xk[:, 400:416], T.k2[:, :], ALU.max, 16, ["pup", "k2"], ["k3"], "xk")
-        itg = T.itg[:, 16 * par:16 * par + 16]
-        ts("itg", itg, T.k3[:, :], 2048.0, None, ALU.add, None, 16, ["k3"], ["itg%d" % par])
-        scatter("sbn%d" % t, Bt[t + 1][:, :], itg, pR, A, ["itg%d" % par, pRk], BK[t + 1])
+            lin("ipay", T.ipay[:, :], PR, 2.0, col("KP"), 16, ["pR", "KP"], ["ipay"], "xk")
+        tt("k3", T.k3[:, :], PR, T.uph[:, :], ALU.max, 16, ["pR", "uph"], ["k3"], "xk")
+        lin("itg", T.itg[:, :], T.k3[:, :], 2.0, col("KT"), 16, ["k3", "KT"], ["itg"])
         if t < RO - 1:
-            dma("cp_b%d" % (t + 2), "y", Bt[t + 2][:, 0:V], Bt[t + 1][:, 0:V], 1048576, BK[t + 1], BK[t + 2])
-            gather("va%d" % t, T.jt[:, 272:528], W[:, 0:V], xl("a", par, 5), A, WK[t] + ["xa%d_5" % par], ["jtc"])
-            scatter("spay%d" % t, pay[:, :], T.ipay[:, :], T.jt[:, 272:528], A, ["ipay", "jtc"], ["pay%d" % t])
-            add("send%d" % t, {"g": ((600.0, 0, 0, 0, 0), lambda g, t=t, pay=pay: send(g, t, pay))}, ["pay%d" % t], ["land%d" % t],
+            tc = T.tc[:, TS_ * t:TS_ * t + TS_]
+            pay = T["pay%d" % t]
+            if t == 0:
+                off, ok = xl(1, 0, 0, A)
+                gather("va", T.va[:, :], Ct[0][:, Z0:Z0 + V], off, A, CK[0] + ok, ["va"])
+                scatter("spay", pay[:, 16:16 + TS_], T.ipay[:, :], T.va[:, :], A, ["ipay", "va"], ["pay0"])
+            scatter("stc%d" % t, tc, T.ipay[:, :], T.vt[:, :], A, ["ipay", "vt"], ["tc%d" % t])
+            lin("tch", T.tch[:, :], T.tc[:, TS_ * t:TS_ * t + S], 1.0, col("N2K"), S, ["tc%d" % t, "N2K"], ["tch"])
+            list_set("TL%d" % t, PT, lambda a: T.tch[:, a:S:16], 8, ["tch"], ["pT"], "xk")
+            pl = T.pl[:, 8 * t:8 * t + 8]
+            cp("t16", T.t16[:, 8 * t:8 * t + 8], PT, 8, ["pT"], ["t16%d" % t], "xk")
+            ts("mark", pay[:, 8:16], T.kh[:, :], T.cum[:, 127:128], 2.0 * V, ALU.is_ge, ALU.mult, 8, ["kh", "cum"], ["mark%d" % t])
+            if t > 0:
+                lin("pl", pl, PT, 1.0, col("P2K"), 8, ["pT", "P2K"], ["pl%d" % t], "xk")
+                gather("pay%d" % t, pay[:, 16:16 + S], Ct[t][:, Z0:Z0 + CG], pl, S, CK[t] + ["pl%d" % t], ["pay%d" % t])
+            add("send%d" % t, {"g": ((600.0, 0, 0, 0, 0), lambda g, t=t: send(g, t))}, ["pay%d" % t, "mark%d" % t], ["land%d" % t],
                 lat=8000.0 if t == 0 else 6000.0, ext="send")
-        z_chain(t, 0)
-        walk_lists(t, "b")
-        ptr(5, 1)
-        ptr(5, 2)
+        scatter("sbn%d" % t, Pt[t + 1][:, Z0:Z0 + PS_], T.itg[:, :], T.vt[:, :], A, ["itg", "vt"], PK[t + 1])
+        if not one:
+            z_chain(t, 0)
+            walk_lists(t, 1, False)
+            for lo, hi in pieces:
+                if hi > p1:
+                    ptr(5, lo, hi)
+            lists(5, p1, L)
+        if t == 0:
+            dma("cp_p2", "y", Pt[2][rows, Z0:Z0 + V], Pt[1][rows, Z0:Z0 + V], 131072, PK[1], PK[2])
+        if t == 1:
+            dma("cp_p3a", "y", T.nxi[:, :], Pt[2][rows, Z0:Z0 + V], 131072, PK[2], ["nxi"])
+            cp("nxf", T.nxf[:, :], T.nxi[:, :], 256, ["nxi"], ["nxf"])
+            dma("cp_p3", "y", Pt[3][rows, Z0:Z0 + V], T.nxf[:, :], 131072, ["nxf"], PK[3])
+        for ch in range(0 if one else 1, len(CH)):
+            z_chain(t, ch)
         if t < RO - 1:
-            lists(5, "b")
-        z_chain(t, 1)
-        z_chain(t, 2)
-        if t < RO - 1:
-            narr, items, PM = 0, [], T.c0[:, 160:160 + PW]
+            narr, PM = 0, T[mb][:, 320:320 + PW]
+            items = []
             for e in range(3):
                 h = rts[(rank - 1 - e) % 4][e][1]
                 narr += HE if h is None else len(topo.engines(h, core))
                 s, m = (3 * t + e) * PW, (e - t) % 3
-                items.append((PM, T.sh[:, 128 * m:128 * m + 128], T.land[:, s:s + PW], e == 0, e == 2, PW))
-            i = mm("merge%d" % t, items, ["land%d" % t, "sh0", "sh1", "sh2"], ["pmg"], "c0")
+                items.append((PM, T.sh[:, 128 * m:128 * m + 128], T.land[:, s:s + PW], e == 0, False, PW))
+            items.append((T[mb][:, 320:328], idf, T.t16[:, 8 * t:8 * t + 8], False, True, 8))
+            i = mm("merge%d" % t, items, ["land%d" % t, "sh0", "sh1", "sh2", "idp", "t16%d" % t, "B" + mb], ["pmg"], mb)
             ops[i]["ext"] = ("arr%d" % t, narr)
-            cp("jta", T.jt[:, 0:PW], PM, PW, ["pmg"], ["jta"], "c0", both=True)
-            ts("k4", T.k4[:, :], T.kg[:, :], T.jt[:, 0:1], 2000.0, ALU.subtract, ALU.mult, 16, ["kg", "jta"], ["k4"])
-            tt("k5", T.k5[:, :], T.k4[:, :], T.kf[:, :], ALU.max, 16, ["k4", "kf"], ["k5"])
-            tt("k6", T.k6[:, :], T.k5[:, :], T.jl[:, 0:16], ALU.min, 16, ["k5", "jl"], ["k6"])
-            cp("ijn", T.ijn[:, :], T.k6[:, :], 16, ["k6"], ["ijn"])
-            gather("vnew", T.vnew[:, :], T.jt[:, :], T.ijn[:, :], A, ["jta", "jtc", "ijn"], ["vnew"])
-            scatter("sw%d" % t, Wt[t + 1][:, :], itg, T.vnew[:, :], A, ["itg%d" % par, "vnew"], WK[t + 1])
-            if t == 0:
-                dma("cp_w2", "y", T.w2[:, 0:V], T.w1[:, 0:V], 1048576, ["w1"], ["w2"])
-    par = (RO - 1) % 2
-    list_set("yn", T.xk[:, 0:256], GT, lambda a: T.bn3[:, a:V:16], 256, BK[3], ["pvw"], "xk")
-    cp("yns", T.yns[:, :], T.xk[:, 0:256], 256, ["pvw"], ["yns"], "xk", both=True)
-    dma("st_n", "y", T.yn[:], T.yns[:, :], 131072, ["yns"], ["yn"])
-    list_set("yc", T.lb[:, 128:208], GT, lambda a: pbv(par, 5, 80 * a, 80 * a + 80), 80, ["pb%d_%d_5" % (par, ch) for ch in range(3)], ["pyc"], "lb")
-    cp("ycs", T.ycs[:, :], T.lb[:, 128:208], 80, ["pyc"], ["ycs"], "lb", both=True)
+            arr, dl = T.arr[:, S * t:S * t + S], T.dl[:, 8 * t:8 * t + 8]
+            cp("arr", arr, T[mb][:, 328:328 + S], S, ["pmg"], ["arr%d" % t], mb)
+            lin("dl", dl, T[mb][:, 320:328], 1.0, col("P2K"), 8, ["pmg", "P2K"], ["dl%d" % t], mb)
+            for u in range(t + 1, RO):
+                scatter("sw%d%d" % (t, u), Ct[u][:, Z0:Z0 + CS], dl, arr, S, ["dl%d" % t, "arr%d" % t], CK[u])
+    dma("st_n", "y", T.yn[:], T.pc[rows, Z0:Z0 + V], 131072, PK[3], ["yn"])
+    list_set("yc", T[mb][:, 320:400], lambda a: fo(5, 80 * a, 80 * a + 80), 80, keys("fo5", 0, L), ["pmg"], mb)
+    lin("ycs", T.ycs[:, :], T[mb][:, 320:400], 1.0, col("P2K"), 80, ["pmg", "P2K"], ["ycs"], mb)
     dma("st_c", "y", T.yc[:], T.ycs[:, :], 40960, ["ycs"], ["yc"])
     return ops
 
 
-def place(ops, succ, cost, hop, weight, bias):
-    n = len(ops)
-    rank = [0.0] * n
-    for i in range(n - 1, -1, -1):
-        rank[i] += (min(cost[i].values()) + hop) * weight[i] + ops[i]["lat"]
-        for d in ops[i]["deps"]:
-            if rank[i] > rank[d]:
-                rank[d] = rank[i]
-    left, rdy = [len(o["deps"]) for o in ops], [0.0] * n
-    free, bank, eng, order = {e: 0.0 for e in "vstgy"}, {}, [None] * n, []
-    ready = [i for i in range(n) if not left[i]]
-    look = CFG["look"]
+def after(xs, x):
+    lo, hi = 0, len(xs)
+    while lo < hi:
+        m = (lo + hi) // 2
+        if xs[m] > x:
+            hi = m
+        else:
+            lo = m + 1
+    return lo
+
+
+def lay(pred, succ, bank, head, hop, prio, pick):
+    n = len(pred)
+    left = [len(p) for p in pred]
+    ready = sorted((prio[i], i) for i in range(n) if not left[i])
+    start, end, eng = [0.0] * n, [0.0] * n, [None] * n
+    busy, used = {e: ([], []) for e in "vstgy"}, {}
     while ready:
+        _p, i = ready.pop(0)
+        t0 = max([head[i]] + [end[d] + lag for d, lag in pred[i]])
         best = None
-        for i in ready:
-            b = bank.get(ops[i]["bank"])
-            for e, c in cost[i].items():
-                t = rdy[i] if rdy[i] > free[e] else free[e]
-                if b and b[1] != e and b[0] + hop > t:
-                    t = b[0] + hop
-                key = t - look * rank[i] + (bias[i] * c if e == "v" else 0.0)
-                if best is None or key < best[0]:
-                    best = (key, i, e, t, c)
-        _k, i, e, t, c = best
-        ready.remove(i)
-        order.append(i)
-        eng[i], free[e] = e, t + c
-        if ops[i]["bank"]:
-            bank[ops[i]["bank"]] = (t + c, e)
+        for e, c, h in pick[i]:
+            s, f = busy[e]
+            t, moved = t0, True
+            while moved:
+                k = after(f, t)
+                while k < len(s) and s[k] < t + c:
+                    t = f[k] if f[k] > t else t
+                    k += 1
+                moved = False
+                for bs, bf, be in used.get(bank[i], ()):
+                    if be != e and bs - hop < t + c and bf + hop > t:
+                        t, moved = bf + hop, True
+            if best is None or t + c + h < best[0]:
+                best = (t + c + h, t, e, c, k)
+        _x, t, e, c, k = best
+        busy[e][0].insert(k, t)
+        busy[e][1].insert(k, t + c)
+        if bank[i]:
+            used.setdefault(bank[i], []).append((t, t + c, e))
+        start[i], end[i], eng[i] = t, t + c, e
         for j in succ[i]:
-            rdy[j] = max(rdy[j], t + c + ops[i]["lat"] + (0.0 if e == "t" and "t" in cost[j] else hop))
             left[j] -= 1
             if not left[j]:
-                ready.append(j)
-    return order, eng
+                ready.insert(after(ready, (prio[j], j)), (prio[j], j))
+    return start, end, eng
 
 
 def replay(ops, order, eng, cost, hop, lf):
@@ -521,29 +592,48 @@ def schedule(ops):
     if "order" not in PLAN:
         costs = [[{e: sum(a * b for a, b in zip(c, m[0])) for e, (c, _f) in o["alts"].items()} for o in ops] for m in PLANS]
         rng = np.random.default_rng(CFG["seed"])
-        n = len(ops)
-        succ = [[] for _ in ops]
+        n, hop = len(ops), PLANS[0][1]
+        lat, bank = [o["lat"] * PLANS[0][2] for o in ops], [o["bank"] for o in ops]
+        gap = lambda a, b: lat[a] + (0.0 if "t" in ops[a]["alts"] and "t" in ops[b]["alts"] else hop)
+        fp, bs = [[(d, gap(d, o["i"])) for d in o["deps"]] for o in ops], [o["deps"] for o in ops]
+        fs, bp = [[] for _ in ops], [[] for _ in ops]
         for o in ops:
             for d in o["deps"]:
-                succ[d].append(o["i"])
+                fs[d].append(o["i"])
+                bp[d].append((o["i"], gap(d, o["i"])))
 
         def judge(order, eng):
             r = [replay(ops, order, eng, costs[j], m[1], m[2]) for j, m in enumerate(PLANS)]
             return 2 * r[0][0] + r[1][0] + r[2][0], r
 
-        weight, best = np.ones(n), None
-        bias = np.array([3.0 if o["n"][:2] in ("p0", "p1", "p2", "va", "vn", "ml", "zo", "pe", "vr") else 0.0 for o in ops])
+        def both(prio, hand):
+            pick = [[(e, c, hand[i] * c if e == "v" else 0.0) for e, c in costs[0][i].items()] for i in range(n)]
+            _s, f, eng = lay(fp, fs, bank, [0.0] * n, hop, prio, pick)
+            fixed = [[(eng[i], costs[0][i][eng[i]], 0.0)] for i in range(n)]
+            _s, f, _e = lay(bp, bs, bank, lat, hop, [-(f[i] + lat[i]) for i in range(n)], fixed)
+            s, _f, eng = lay(fp, fs, bank, [0.0] * n, hop, [-x for x in f], pick)
+            return s, eng
+
+        rank = [0.0] * n
+        for i in range(n - 1, -1, -1):
+            rank[i] = min(costs[0][i].values()) + max([lat[i]] + [rank[j] + lag for j, lag in bp[i]])
+        prio, h0 = -np.array(rank), CFG["hand"]
+        hand = np.array([-h0 if o["n"][:2] == "sg" else h0 for o in ops])
+        best = score = None
         for it in range(CFG["iters"]):
-            w, b = weight.copy(), bias.copy()
+            p, h = prio.copy(), hand.copy()
             if it:
-                k = rng.random(n) < 0.05
-                w[k] = np.exp(rng.normal(0.0, 0.8, int(k.sum())))
-                k = rng.random(n) < 0.03
-                b[k] = np.exp(rng.normal(0.5, 1.5, int(k.sum()))) - 0.5
-            order, eng = place(ops, succ, costs[0], PLANS[0][1], w.tolist(), b.tolist())
-            score, r = judge(order, eng)
-            if best is None or score <= best[0]:
-                best, weight, bias = (score, order, eng, r), w, b
+                k = rng.random(n) < rng.choice([0.02, 0.1, 0.5])
+                p[k] += rng.normal(0.0, 600.0 * rng.choice([0.3, 1.0, 3.0]), int(k.sum()))
+                k = rng.random(n) < 0.005
+                h[k] = rng.normal(0.0, h0, int(k.sum()))
+            s, eng = both(p.tolist(), h.tolist())
+            order = sorted(range(n), key=lambda i: (s[i], i))
+            s2, r = judge(order, eng)
+            if score is None or s2 <= score + 1500.0 * (1 - it / CFG["iters"]) * rng.random() ** 2:
+                score, prio, hand = s2, np.array(s), h
+            if best is None or s2 < best[0]:
+                best = (s2, order, eng, r)
         score, order, eng, r = best
         for it in range(CFG["polish"]):
             _m, end, why = r[int(rng.integers(0, len(PLANS)))]
@@ -557,7 +647,7 @@ def schedule(ops):
             j = p if u < 0.25 else i
             if u < 0.4 and len(ops[j]["alts"]) > 1:
                 e2 = list(eng)
-                e2[j] = "s" if eng[j] == "v" else "v"
+                e2[j] = [e for e in ops[j]["alts"] if e != eng[j]][0]
             else:
                 a, b = order.index(p), order.index(i)
                 seg, need = order[a:b + 1], {i}
@@ -568,9 +658,11 @@ def schedule(ops):
                     continue
                 o2 = order[:a] + [x for x in seg if x in need] + [x for x in seg if x not in need] + order[b + 1:]
             s2, r2 = judge(o2, e2)
-            if s2 <= score + 150.0 * rng.random() ** 4:
+            if s2 <= score + 300.0 * (1 - it / CFG["polish"]) * rng.random() ** 4:
                 score, order, eng, r = s2, o2, e2, r2
-        PLAN["order"], PLAN["eng"], PLAN["val"] = order, eng, [x[0] for x in r]
+            if score < best[0]:
+                best = (score, order, eng, r)
+        PLAN["order"], PLAN["eng"], PLAN["val"] = best[1], best[2], [x[0] for x in best[3]]
     for o, e in zip(ops, PLAN["eng"]):
         o["e"] = e
     return PLAN["order"]

@@ -1,3 +1,4 @@
+import math
 import numpy as np
 from concourse.bass import DstId, RemoteDMATransfer
 from concourse.mybir import dt, AluOpType, AxisListType, ActivationFunctionType
@@ -6,14 +7,16 @@ ALU = AluOpType
 ACT = ActivationFunctionType
 V, L, A, S, RO = 4096, 1280, 256, 128, 3
 PW = S + 8
-BIG = float(2 ** 33)
+BIG = float(2 ** 36)
+ZH = 1280.0
 M1 = 1.5 * 2 ** 23
 Z0 = 16
 CG, CS = V + 2 * S, 2 * V + V + 2 * S
 PS_, TS_ = V + 2 * A, V + 3 * A
 NC = 2178.0
-CFG = {"iters": 600, "polish": 14000, "seed": 1, "hand": 8.0,
-       "fold": ((1, 1), (0, 0), (0, 0)),
+CFG = {"iters": 60, "polish": ((60000, 400.0, True), (7500, 100.0, False)), "spay": 1, "cutb": 2, "thrift": 0.3, "byv": 0.6, "ycd": 1, "cuta": (1, 1, 0), "seed": 2, "hand": 8.0,
+       "fold": ((1, 1), (0, 1), (0, 1)),
+       "two": ((0, 0), (0, 0), (0, 0)),
        "ch": (0, 256, 576, 896, 1280),
        "parts": (2, 2, 2),
        "joint": (0, 0, 0),
@@ -24,13 +27,13 @@ PLANS = (((1.0, 0.83, 1.3, 3.15, 0.42), 200.0, 1.3), ((1.0, 0.85, 1.0, 2.0, 0.5)
 _bf, _f, _i, _u, _h = "bfloat16", "float32", "int32", "uint16", "float16"
 _SB = {
     _bf: {"ca": Z0 + CS, "cb": Z0 + CS, "pg": 128, "ih": 128, "inh": 128, "ione": 128, "i4k": 128, "gm": 288, "bkp": 1024, "bkn": 1024,
-          "bo": 128, "sh": 384, "z": L, "dh": L, "sg": L, "ml": 256, "eq": 4096, "cutp": 128, "cum": 128, "pay0": 16 + TS_, "pay1": 16 + S,
-          "arr": 2 * S, "va": A, "land": 6 * PW, "inv": 1200, "ones": 128},
+          "st": 128, "sh": 384, "z": L, "sg": L, "ml": 320, "eq": 4096, "pay0": 16 + TS_, "pay1": 16 + S,
+          "arr": 2 * S, "land": 6 * PW, "inv": 1200},
     _f: {"pc": Z0 + PS_, "nxf": 256, "tc": 2 * TS_, "col": 48, "rsel": 16, "gsel": 8, "pm": 144, "iom": 128, "kh": 8, "pcf": 128,
          "vl": 16, "vt": 256, "uph": 16, "k3": 16, "ycs": 80},
     _i: {"pa": Z0 + PS_, "pb": Z0 + PS_, "nxi": 256, "curi": 80, "wti": 8, "ip": 8, "iq": 8, "li": 80, "lj": 80},
     _u: {"x0": 320, "xs": 960, "xu": 960, "ipay": 16, "itg": 16, "pl": 16, "dl": 16},
-    _h: {"nxh": 256, "idp": 144, "gp": 144, "bw": 128, "sw": 128, "fo": 5 * L, "xf": 320, "xm": 320, "vw": 256, "pcn": 128, "cutr": 128,
+    _h: {"cv": L, "ineg": 128, "ych": 80, "zh": L, "dh": L, "ihh": 128, "tw": 128, "cutp": 128, "cum": 128, "idp": 144, "gp": 144, "bw": 128, "sw": 128, "fo": 5 * L, "xf": 320, "xm": 320, "vw": 256, "pcn": 128, "cutr": 128,
          "rr": 128, "tch": 128, "t16": 16},
 }
 SCRATCH = {k: ("sbuf", [128, n], d) for d, b in _SB.items() for k, n in b.items()}
@@ -151,11 +154,14 @@ def build(T, topo, core, rank):
         return add(name, {"v": ((55, 0, 0, n, 0), lambda g: g.vector.tensor_copy(win.indirect(off), in_))}, r, w)
 
     def mm(name, items, r, w, bank, after=()):
-        def fn(g):
-            for o, a, b, s0, s1, _n in items:
+        def fn(g, i=len(ops)):
+            its = items
+            if "short" in ops[i] and ops[ops[i]["short"]]["e"] == "v":
+                its = items[:-2] + [items[-2][:4] + items[-1][4:]]
+            for o, a, b, s0, s1, _n in its:
                 ins = g.tensor.matmul(o, a, b, s0, s1)
             return ins
-        return add(name, {"t": ((20, 0, 0, 0, sum(max(64, it[5]) for it in items)), fn)}, r, w, bank, after=after)
+        return add(name, {"t": ((20, 0, 0, 0, sum(max(64, it[5]) if it[5] > 0 else -it[5] for it in items)), fn)}, r, w, bank, after=after)
 
     def dma(name, q, out, in_, nbytes, r, w, after=()):
         fn = (lambda g: g.sync.dma_start(out, in_)) if q == "y" else (lambda g: g.scalar.dma_start(out, in_))
@@ -168,10 +174,8 @@ def build(T, topo, core, rank):
             fn = lambda g: g.iota(out, pattern, base, cm, allow_small_or_imprecise_dtypes=True)
         return add(name, {"g": ((150, 2.0 * n, 0, 0, 0), fn)}, (), w)
 
-    def select(name, out, in_, pattern, op, fill, base, cm, n, r, w):
-        return add(name, {"g": ((190, 2.0 * n, 0, 0, 0), lambda g: g.affine_select(out, in_, pattern, op, fill, base, cm))}, r, w)
-
-    names = ["GF", "PF", "SHF", "PARF", "W4", "SWF", "C14", "C15", "OFF0", "OFF1", "M30", "M31", "M32", "NM1", "P2K", "N2K", "YB0", "YB1",
+    names = ["GF", "PF", "SHF", "PARF", "W4", "SWF", "C14", "C15", "OFF0s", "OFF0v", "OFF1s", "OFF1v", "OFF2s", "OFF2v", "R13", "R14", "R15",
+             "K0", "K1", "K2", "NQH", "PZH", "M30", "M31", "M32", "NM1", "P2K", "N2K", "YB0", "YB1",
              "NQ", "TH2", "TH3", "TH4", "KP", "KU", "KT", "TA", "TB", "TC", "TD", "TE", "P2Z"]
     col = lambda k: T.col[:, names.index(k):names.index(k) + 1]
     gm = lambda fam, a: T.gm[:, fam * 144 + 15 - a: fam * 144 + 15 - a + 128]
@@ -185,11 +189,11 @@ def build(T, topo, core, rank):
     vb, mb = ("d3", "d3") if len(CH) < 4 else ("xk", "lb")
 
     PA = ["pa%d" % b for b in range(8)]
-    for k, (a, b) in enumerate(((0, 384), (384, 1792))):
+    for k, (a, b) in enumerate(((0, 320), (320, 1952))):
         add("fill", {"v": (cv(b - a), lambda g, a=a, b=b: g.vector.memset(T.pa[:, a:b], 0))}, (), PA[k:k + 1])
     for k in range(4):
-        add("fill", {"s": (cv(384), lambda g, k=k: g.scalar.activation(T.pa[:, 1792 + 384 * k:2176 + 384 * k], T.pa[:, 0:384], ACT.Copy))}, PA[0:1], PA[2 + k:3 + k])
-    iota("fill6", T.pa[:, 3328:Z0 + V], [[0, 784]], 0, 0, 784, PA[6:7], True)
+        add("fill", {"s": (cv(320), lambda g, k=k: g.scalar.activation(T.pa[:, 1952 + 320 * k:2272 + 320 * k], T.pa[:, 0:320], ACT.Copy))}, PA[0:1], PA[2 + k:3 + k])
+    iota("fill6", T.pa[:, 3232:Z0 + V], [[0, 880]], 0, 0, 880, PA[6:7], True)
     nx = dma("ld_nx", "y", T.pa[rows, Z0:Z0 + V], T.nx[:], 131072, (), PA)
     c1 = dma("ld_c1", "y", T.ca[:, Z0 + 2048:Z0 + V], T.cards[:, 2048:V], 600000, (), ["ca1"], after=ops[nx]["deps"])
     dma("ld_cur", "y", T.curi[:, :], T.cur[:], 40960, (), ["curi"])
@@ -203,7 +207,7 @@ def build(T, topo, core, rank):
     iota("pg", T.pg[:, :], [[-16, 8], [0, 16]], 0, 1, 128, ["pg"])
     iota("iom", T.iom[:, :], [[1, 128]], 0, 0, 128, ["iom"])
     ts("idp", T.idp[:, :], T.pm[:, :], 0.0, None, ALU.is_equal, None, 144, ["pm"], ["idp"])
-    for nms, base, step in ((["NM1"], -int(M1), 0), (["P2K", "N2K"], 2048, -4096), (["P2Z"], 2048 + Z0, 0), (["YB0", "YB1"], Z0 - 2048, -4096), (["NQ", "TH2", "TH3", "TH4"], -1, 2)):
+    for nms, base, step in ((["NM1"], -int(M1 + ZH), 0), (["NQH", "PZH"], int(2 * ZH) - 1, 1 - int(ZH)), (["P2K", "N2K"], 2048, -4096), (["P2Z"], 2048 + Z0, 0), (["YB0", "YB1"], Z0 - 2048, -4096), (["NQ", "TH2", "TH3", "TH4"], -1, 2)):
         k = names.index(nms[0])
         iota(nms[0], T.col[:, k:k + len(nms)], [[step, len(nms)]], base, 0, len(nms), nms)
     lin("gp0", T.gp[:, :], T.pm[:, :], 0.0, 0.0, 144, ["pm"], ["gp"])
@@ -220,22 +224,23 @@ def build(T, topo, core, rank):
     ms("gm", T.gm[:, :], 0.0, 288, ["gm0", "gm1"])
     lin("gw", T.gm[:, GW * 144 + 15:GW * 144 + 143:16], T.gsel[:, :], col("W4"), 0.0, 8, ["gsel", "W4"], ["gm%d" % GW])
     lin("gc", T.gm[:, GC * 144 + 15:GC * 144 + 143:16], T.gsel[:, :], -BIG, 0.0, 8, ["gsel"], ["gm%d" % GC])
-    for nm, sc in (("ih", 0.5), ("inh", -0.5), ("ione", 1.0), ("i4k", -4096.0)):
+    for nm, sc in (("ihh", 0.5), ("ih", 0.5), ("inh", -0.5), ("ione", 1.0), ("ineg", -1.0), ("i4k", -4096.0)):
         lin(nm, T[nm][:, :], idf, sc, 0.0, 128, ["idp"], [nm], f=0.5)
-    ts("c14", col("C14"), T.iq[:, 1:2], 14.0, -0.125, ALU.is_equal, ALU.mult, 1, ["iq1"], ["C14"])
-    ts("c15a", col("TA"), T.iq[:, 1:2], 15.0, None, ALU.is_equal, None, 1, ["iq1"], ["TA"])
-    ts("c15", col("C15"), col("TA"), -0.125, 1.0, ALU.mult, ALU.add, 1, ["TA"], ["C15"])
+    for k in range(3):
+        ts("r%d" % k, col("R1%d" % (3 + k)), T.iq[:, 1:2], 13.0 + k, None, ALU.is_equal, None, 1, ["iq1"], ["R1%d" % (3 + k)])
+    ts("c14", col("C14"), col("R13"), col("R14"), 0.125, ALU.subtract, ALU.mult, 1, ["R13", "R14"], ["C14"])
+    ts("c15", col("C15"), col("R15"), -0.125, 1.0, ALU.mult, ALU.add, 1, ["R15"], ["C15"])
     for a in range(NB):
         ts("bkp%d" % a, T.bkp[:, 128 * a:128 * a + 128], T.pg[:, :], float(a), col("C14"), ALU.is_equal, ALU.add, 128, ["pg", "C14"], ["bkp%d" % a], f=0.5)
         ts("bkn%d" % a, T.bkn[:, 128 * a:128 * a + 128], T.pg[:, :], float(a), col("C15"), ALU.not_equal, ALU.subtract, 128, ["pg", "C15"], ["bkn%d" % a], f=0.5)
-    lin("offa", col("TE"), col("C14"), -2.0, 0.0, 1, ["C14"], ["TE"])
-    lin("offb", col("TB"), col("TA"), M1, col("TE"), 1, ["TA", "TE"], ["TB"])
-    ts("offc", col("TC"), T.iq[:, 1:2], 14.0, BIG, ALU.is_lt, ALU.mult, 1, ["iq1"], ["TC"])
-    for k, off in enumerate((1.0, 17.0)):
-        lin("off%d" % k, col("OFF%d" % k), col("TC"), off, col("TB"), 1, ["TB", "TC"], ["OFF%d" % k])
-    ms("ones", T.ones[:, :], 4096.0, 128, ["ones"])
-    select("boa", T.bo[:, :], T.ones[:, :], [[-16, 8], [0, 16]], ALU.is_ge, 0.0, 0, 1, 128, ["ones"], ["bo"])
-    select("bob", T.bo[:, :], T.bo[:, :], [[16, 8], [0, 16]], ALU.is_ge, 0.0, 15, -1, 128, ["bo"], ["bo"])
+    lin("offa", col("K0"), col("R14"), 0.25, 0.0, 1, ["R14"], ["K0"])
+    lin("offb", col("K1"), col("R13"), ZH / 2, col("K0"), 1, ["R13", "K0"], ["K1"])
+    lin("offb", col("K2"), col("R15"), M1, col("K1"), 1, ["R15", "K1"], ["K2"])
+    ts("offc", col("TC"), T.iq[:, 1:2], 13.0, BIG, ALU.is_lt, ALU.mult, 1, ["iq1"], ["TC"])
+    for k in range(3):
+        for e, off in (("s", 1.0), ("v", 17.0)):
+            lin("off", col("OFF%d%s" % (k, e)), col("TC"), off, col("K%d" % k), 1, ["K%d" % k, "TC"], ["OFF%d%s" % (k, e)])
+    ms("st", T.st[:, :], 0.0, 128, ["st"])
     ts("bw", T.bw[:, :], T.pg[:, :], 0.0, None, ALU.is_equal, None, 128, ["pg"], ["bw"], f=0.5)
     ts("swa", col("TD"), col("PARF"), -2.0, 1.0, ALU.mult, ALU.add, 1, ["PARF"], ["TD"])
     lin("swf", col("SWF"), col("TD"), 1.0, col("PF"), 1, ["TD", "PF"], ["SWF"])
@@ -293,9 +298,15 @@ def build(T, topo, core, rank):
         b = (s - 1) * L
         return T.fo[:, b + lo:b + hi:step] if step > 1 else T.fo[:, b + lo:b + hi]
 
-    def list_set(name, out, src, n, r, w, bank, fam=None):
-        st = gp if fam is None else (lambda a: gm(fam, a))
-        return mm(name, [(out, st(a), src(a), a == 0, a == 15, n) for a in range(16)], r + ["gp" if fam is None else "gm%d" % fam], w, bank)
+    def list_set(name, out, src, n, r, w, bank, fam=None, more=(), two=False):
+        if two:
+            mm(name + "a", [(T.ma[0:n, 384 + a:512:16], src(a), T.gp[:, 15:143:16], True, True, -n) for a in range(16)], r + ["gp"], ["Bma4"], "ma")
+            cp("tw", T.tw[0:n, :], T.ma[0:n, 384:512], 128, ["Bma4"], ["tw"], "ma")
+            items, r = [(out, T.tw[0:n, :], T.idp[0:n, 0:n], True, not more, n)], ["tw", "idp"]
+        else:
+            st = gp if fam is None else (lambda a: gm(fam, a))
+            items, r = [(out, st(a), src(a), a == 0, a == 15 and not more, n) for a in range(16)], r + ["gp" if fam is None else "gm%d" % fam]
+        return mm(name, items + [m[0] for m in more], r + [k for m in more for k in m[1]], w, bank)
 
     def folded(t, lo):
         return CFG["fold"][t][parts(t).index(part_of(t, lo))]
@@ -307,10 +318,13 @@ def build(T, topo, core, rank):
         n, o = (hi - lo) // 16, lo // 16
         one = len(parts(t)) == 1
         b1, b2 = ("ma", "mb") if one else (("ma", "ma") if j == 0 else ("mb", "mb"))
-        pcl, pcy = T[b1][:, 0:n], T[b1][:, n:4 * n]
-        q = 0 if one else 4 * n
+        k1, k2, u = b1, b2, 0
+        if len(CH) > 4 and j == 0:
+            b1, b2, u = "mb", "mb", 64
+        pcl, pcy = T[b1][:, u:u + n], T[b1][:, u + n:u + 4 * n]
+        q = 0 if one else u + 4 * n
         psel, pus = T[b2][:, q:q + 4 * n], (T[b2][:, 4 * n:5 * n] if one else pcl)
-        kus = "B%s2" % b2 if one else "B%s0" % b1
+        kus = "B%s2" % k2 if one else "B%s0" % k1
         zk = ["z%d" % k for k, c in enumerate(CH) if lo <= c[0] < hi]
         xk = lambda k: xl(t, k, lo, hi)
         e = CFG["inv"][t][j]
@@ -321,8 +335,8 @@ def build(T, topo, core, rank):
         yb = col("YB1" if e == "v" else "YB0")
         if first:
             over[t, lo] = (iv, ik, yb)
-            list_set("cl%d%d" % (t, j), pcl, lambda a: T.z[:, lo + a:hi:16], n, zk, ["B%s%d" % (b, k) for b in (b1, b2) for k in range(4)], b1, GW)
-            cp("cli", T.li[:, o:o + n], pcl, n, ["B%s0" % b1], keys("li", lo, hi), b1)
+            list_set("cl%d%d" % (t, j), pcl, lambda a: T.z[:, lo + a:hi:16], n, zk, ["B%s%d" % (b, k) for b in (k1, k2) for k in range(4)], b1, GW)
+            cp("cli", T.li[:, o:o + n], pcl, n, ["B%s0" % k1], keys("li", lo, hi), b1)
             lj = T.lj[:, o:o + n]
             ts("clj", lj, T.li[:, o:o + n], 3, None, ALU.bitwise_and, None, n, keys("li", lo, hi), keys("lj", lo, hi))
             for s, c in ((1, -1.0), (5, 1.0)):
@@ -334,17 +348,17 @@ def build(T, topo, core, rank):
                     fn = lambda g, s=s: g.vector.tensor_scalar(iv(s, s), lj, s - 1.5, -2.0, ALU.is_gt, ALU.mult)
                 add("inv", {e: (cv(n), fn)}, keys("lj", lo, hi) + ["TH%d" % s], [ik + str(s)])
             mm("sel%d%d" % (t, j), [(psel, T.ih[:, :], iv(2, 5), True, False, 4 * n), (psel, T.inh[:, :], iv(1, 4), False, True, 4 * n)],
-               iks + ["ih", "inh"], ["B%s3" % b2], b2)
+               iks + ["ih", "inh"], ["B%s3" % k2], b2)
             return
         xf, xm = T.xf[:, 4 * o:4 * o + 4 * n], T.xm[:, 4 * o:4 * o + 4 * n]
         src = T.xs[:, 320 * t + 4 * o:320 * t + 4 * o + 4 * n]
         ts("xf", xf, src, -2048.0 - Z0 * folded(t, lo), None, ALU.add, None, 4 * n, sum((xk(s)[1] for s in range(1, 5)), []), keys("xf", lo, hi), f=0.5)
         if not folded(t, lo):
             mm("cy%d%d" % (t, j), [(pcy, idf, T.xf[:, 4 * o + n:4 * o + 4 * n], True, False, 3 * n), (pcy, T.i4k[:, :], iv(2, 4), False, True, 3 * n)],
-               iks + ["idp", "i4k"] + keys("xf", lo, hi), ["B%s1" % b1], b1)
+               iks + ["idp", "i4k"] + keys("xf", lo, hi), ["B%s1" % k1], b1)
             b = 320 * t + 80 + 3 * o
-            relu("yl", T.xu[:, b:b + 3 * n], pcy, lambda: yb, 3 * n, ["B%s1" % b1, "YB0", "YB1"], sum((xk(k)[1] for k in range(6, 9)), []), b1)
-        tt("xm", xm, psel, xf, ALU.mult, 4 * n, ["B%s3" % b2] + keys("xf", lo, hi), keys("xm", lo, hi), b2)
+            relu("yl", T.xu[:, b:b + 3 * n], pcy, lambda: yb, 3 * n, ["B%s1" % k1, "YB0", "YB1"], sum((xk(k)[1] for k in range(6, 9)), []), b1)
+        tt("xm", xm, psel, xf, ALU.mult, 4 * n, ["B%s3" % k2] + keys("xf", lo, hi), keys("xm", lo, hi), b2)
         mm("us%d%d" % (t, j), [(pus, idf, T.xm[:, 4 * o + s * n:4 * o + s * n + n], s == 0, s == 3, n) for s in range(4)],
            ["idp"] + keys("xm", lo, hi), [kus], b2)
         lin("ul", xk(5)[0], pus, 1.0, col("P2K"), n, [kus, "P2K"], xk(5)[1], b2)
@@ -353,32 +367,48 @@ def build(T, topo, core, rank):
         lo, hi = CH[ch]
         n = hi - lo
         nb = n // 64
-        dk, zk, hk = "d%d" % ch, "z%d" % ch, "dh%d" % ch
+        dk, zk, hk = ("d0", "d1", "d2", "d3", "ma")[ch], "z%d" % ch, "dh%d" % ch
         D, C = T[dk][:, 0:n], T[dk][:, 448:512]
         zz, dh, sgv, ml = T.z[:, lo:hi], T.dh[:, lo:hi], T.sg[:, lo:hi], T.ml[:, 64 * ch:64 * ch + 64]
-        for s in range(1, 6):
-            fold = folded(t, lo)
-            off, ok = xl(t + 1, 0, lo, hi) if s == 5 else xl(t, s if fold or s == 1 else s + 4, lo, hi)
-            win = Ct[t][:, Z0:Z0 + V] if s == 5 or (s == 1 and not fold) else Ct[t][:, 0:Z0 + V]
-            gather_tt("gs%d%d%d" % (t, ch, s), dh, win, off, zz, ALU.subtract, n, CK[t] + ok + [zk], [hk])
-            if s == 5:
-                add("abs%d%d" % (t, ch), {"s": (cv(n), lambda g: g.scalar.activation(zz, dh, ACT.Abs))}, [hk], [zk])
-                break
-            so = add("sg%d%d%d" % (t, ch, s), {"s": (cv(n), lambda g: g.scalar.activation(sgv, dh, ACT.Sign, bias=col("NQ"), scale=2.0)),
-                                               "v": (cv(n, 0.5), lambda g: g.vector.tensor_scalar(sgv, dh, 0.0, 2.0, ALU.is_gt, ALU.mult))},
-                     [hk, "NQ"], ["sg%d" % ch])
+        zh, cv5, fold = T.zh[:, lo:hi], T.cv[:, lo:hi], folded(t, lo)
+        for s in range(1, 5):
+            off, ok = xl(t, s if fold or s == 1 else s + 4, lo, hi)
+            win = Ct[t][:, Z0:Z0 + V] if s == 1 and not fold else Ct[t][:, 0:Z0 + V]
+            zin, zr, one, nq, th = (zz, zk, T.ione[:, :], "NQ", 0.0) if s == 1 else (zh, "h" + zk, idf, "NQH", -ZH)
+            gather_tt("gs%d%d%d" % (t, ch, s), dh, win, off, zin, ALU.subtract, n, CK[t] + ok + [zr], [hk])
+            so = add("sg%d%d%d" % (t, ch, s), {"s": (cv(n), lambda g, nq=nq: g.scalar.activation(sgv, dh, ACT.Sign, bias=col(nq), scale=2.0)),
+                                               "v": (cv(n, 0.5), lambda g, th=th: g.vector.tensor_scalar(sgv, dh, th, 2.0, ALU.is_gt, ALU.mult))},
+                     [hk, nq], ["sg%d" % ch])
             mm("cnt%d%d%d" % (t, ch, s), [(C, gm(GC, a), T.sg[:, lo + 64 * a:lo + 64 * a + 64], a == 0, a == nb - 1, 64) for a in range(nb)],
-               ["sg%d" % ch, "gm%d" % GC, "B" + dk], ["pcn%d" % ch], dk)
-            relu("ml%d%d%d" % (t, ch, s), ml, C, lambda so=so: col("OFF1" if ops[so]["e"] == "v" else "OFF0"), 64,
-                 ["pcn%d" % ch, "OFF0", "OFF1"], ["ml%d" % ch], dk)
-            items = [(D, T.ih[:, :], dh, True, False, n)]
+               ["sg%d" % ch, "gm%d" % GC], ["pcn%d" % ch], dk)
+            kind = "OFF%d" % (0, 1, 1, 2)[s - 1]
+            relu("ml%d%d%d" % (t, ch, s), ml, C, lambda so=so, kind=kind: col(kind + ops[so]["e"]), 64,
+                 ["pcn%d" % ch, kind + "v", kind + "s"], ["ml%d" % ch], dk)
+            items = [(D, T.ihh[:, :], dh, True, False, n)]
             for bk in (T.bkp, T.bkn):
                 items += [(T[dk][:, 64 * a:64 * a + 64], bk[:, 128 * a:128 * a + 128], ml, False, False, 64) for a in range(nb)]
-            items.append((D, T.ione[:, :], zz, False, True, n))
-            mm("upd%d%d%d" % (t, ch, s), items, ["ml%d" % ch, "ih", "ione", hk, zk] + ["bk%s%d" % (x, a) for a in range(nb) for x in "pn"], [dk], dk)
-            lin("zo%d%d%d" % (t, ch, s), zz, D, 1.0, col("NM1"), n, [dk, "NM1"], [zk], dk)
+            items.append((D, one, zin, False, s < 4, n))
+            up = mm("upd%d%d%d" % (t, ch, s), items, ["ml%d" % ch, "ihh", "ione", hk, zr] + ["bk%s%d" % (x, a) for a in range(nb) for x in "pn"], [dk], dk)
+            if s == 1:
+                lin("zo%d%d%d" % (t, ch, s), zh, D, 1.0, col("PZH"), n, [dk, "PZH"], ["h" + zk], dk)
+            elif s < 4:
+                i = add("zo%d%d%d" % (t, ch, s), {"v": (cv(n), lambda g: g.vector.tensor_tensor(zh, D, zh, ALU.add)),
+                                                  "s": (cv(n), lambda g: g.scalar.activation(zh, D, ACT.Copy))}, [dk], ["h" + zk], dk)
+                ops[i]["link"], ops[up]["short"] = (up, n), i
+            else:
+                if (t, ch) not in shown:
+                    off, ok = xl(t + 1, 0, lo, hi)
+                    src = Ct[t][:, Z0:Z0 + V].indirect(off)
+                    i = add("cv%d%d" % (t, ch), {"v": ((55, 0, n, 0, 0), lambda g: g.vector.tensor_tensor(cv5, src, zh, ALU.subtract)),
+                                                 "s": ((70, 0, n, 0, 0), lambda g: g.scalar.activation(cv5, src, ACT.Copy))},
+                            CK[t] + ok + [zr], ["cv%d" % ch])
+                    ops[i]["link"], ops[up]["short"] = (up, n), i
+                mm("rv%d%d" % (t, ch), [(D, T.ineg[:, :], cv5, False, True, n)], ["ineg", "cv%d" % ch], [dk], dk)
+        add("abs%d%d" % (t, ch), {"s": (cv(n), lambda g: g.scalar.activation(zz, D, ACT.Abs, bias=col("NM1")))}, [dk, "NM1"], [zk], dk)
         if t == RO - 1:
             dma("st_z%d" % ch, "y", T.yz[:, lo:hi], zz, n * 256, [zk], ["yz%d" % ch])
+
+    shown = [(0, 0)] if CFG["spay"] else []
 
     def send(g, t):
         near = T.cores[[r for r, h in rts[rank] if h is None][0]]
@@ -399,6 +429,9 @@ def build(T, topo, core, rank):
     for t in range(RO):
         one = len(parts(t)) == 1
         pieces = [(a, b) for a, b in zip(CFG["pieces"], CFG["pieces"][1:])] if one else CH
+        if not one and CFG["cutb"]:
+            w = (L - CH[0][1]) // CFG["cutb"]
+            pieces = ([(0, CH[0][1] // 2), (CH[0][1] // 2, CH[0][1])] if CFG["cuta"][t] else [CH[0]]) + [(CH[0][1] + w * k, CH[0][1] + w * k + w) for k in range(CFG["cutb"])]
 
         def ptr(s, lo, hi):
             off, ok = xl(t, s - 1 if s < 5 else 5, lo, hi)
@@ -410,9 +443,10 @@ def build(T, topo, core, rank):
             ps, pk = T.lb[:, q + lo // 16:q + hi // 16], keys("Blb%d" % q, lo, hi)
             mine = [p for p in parts(t) if lo <= p[0] < hi]
             more = [p for p in mine if 1 < s < 5 and folded(t, p[0])]
-            items = [(ps, gp(a), fo(s, lo + a, hi, 16), a == 0, a == 15 and not more, (hi - lo) // 16) for a in range(16)]
-            items += [(T.lb[:, q + p[0] // 16:q + p[1] // 16], T.i4k[:, :], over[t, p[0]][0](s, s), False, p == more[-1], (p[1] - p[0]) // 16) for p in more]
-            mm("ls%d%d_%d" % (t, s, lo), items, keys("fo%d" % s, lo, hi) + ["gp", "i4k"] + [over[t, p[0]][1] + str(s) for p in more], pk, "lb")
+            items = [((T.lb[:, q + p[0] // 16:q + p[1] // 16], T.i4k[:, :], over[t, p[0]][0](s, s), False, p == more[-1], (p[1] - p[0]) // 16),
+                      ["i4k", over[t, p[0]][1] + str(s)]) for p in more]
+            list_set("ls%d%d_%d" % (t, s, lo), ps, lambda a: fo(s, lo + a, hi, 16), (hi - lo) // 16, keys("fo%d" % s, lo, hi), pk, "lb",
+                     more=items, two=hi - lo <= 512 and CFG["two"][t][0])
             for p0, p1 in mine:
                 out, ok = xl(t, s, p0, p1) if s < 5 else xl(t + 1, 0, p0, p1)
                 src, n, rk = T.lb[:, q + p0 // 16:q + p1 // 16], (p1 - p0) // 16, keys("Blb%d" % q, p0, p1)
@@ -442,20 +476,25 @@ def build(T, topo, core, rank):
         uh = lin("uph", T.uph[:, :], T.xk[:, 400:416], 0.5, col("KU"), 16, ["pup", "KU"], ["uph"], "xk")
         mm("vwide", [(T[vb][:, 0:256], T.bw[:, :], fo(5, 0, A), True, True, 256)], ["bw", "B" + vb] + keys("fo5", 0, A), ["pvw"], vb)
         lists(5, 0, p1)
+        if (t, 0) in shown:
+            off, ok = xl(t + 1, 0, *CH[0])
+            gather("cv00", T.cv[:, 0:CH[0][1]], Ct[t][:, Z0:Z0 + V], off, CH[0][1], CK[t] + ok, ["cv0"])
         cp("vw", T.vw[:, :], T[vb][:, 0:256], 256, ["pvw"], ["vw"], vb)
         lin("vt", T.vt[:, :], T[vb][:, 0:256], 1.0, col("P2K"), 256, ["pvw", "P2K"], ["vt"], vb)
         PS, PR, PT = T.xk[:, 256:384], T.xk[:, 384:400], T.xk[:, 416:424]
         for k in range(16):
             ts("eq%d" % k, T.eq[:, 256 * k:256 * k + 256], T.vw[:, :], T.vl[:, k:k + 1], 1.0 / 256, ALU.is_equal, ALU.subtract, 256, ["vw", "vl"], ["eq%d" % k], f=0.5)
             if k % 2 == 1:
-                items = [(PS, T.bo[:, :], T.eq[:, 256 * kk + h:256 * kk + 256:2], kk == 0 and h == 0, kk == 15 and h == 1, 128)
-                         for kk in (k - 1, k) for h in range(2)]
-                mm("S%d" % k, items, ["bo", "eq%d" % (k - 1), "eq%d" % k, "pT"], ["pS"], "xk", after=[up, uh])
+                items = [(T.xk[:, 424:432], T.eq[:, 256 * kk + h:256 * kk + 256:2], T.gm[:, GC * 144 + 15:GC * 144 + 143:16],
+                          kk == 0 and h == 0, kk == 15 and h == 1, 8) for kk in (k - 1, k) for h in range(2)]
+                mm("S%d" % k, items, ["gm%d" % GC, "eq%d" % (k - 1), "eq%d" % k, "pT", "pC"], ["pS0"], "xk", after=[up, uh])
+        cp("st", T.st[:, 0:128:16], T.xk[:, 424:432], 8, ["pS0"], ["st"], "xk")
+        mm("S", [(PS, T.st[:, :], T.i4k[:, :], True, True, 128)], ["st", "i4k"], ["pS"], "xk")
         ts("cutp", T.cutp[:, :], PS, 0.0, None, ALU.is_equal, None, 128, ["pS"], ["cutp"], "xk")
         tt("cutr", T.cutr[:, :], PS, T.pcn[:, :], ALU.min, 128, ["pS", "pcn"], ["cutr"], "xk")
         add("cum", {"v": (cv(64), lambda g: g.vector.tensor_tensor_scan(T.cum[:, :], T.cutp[:, :], T.cutp[:, :], 0.0, ALU.add, ALU.max))}, ["cutp"], ["cum"])
         tt("rr", T.rr[:, :], T.cutr[:, :], T.cum[:, :], ALU.max, 128, ["cutr", "cum"], ["rr"])
-        list_set("R%d" % t, PR, lambda a: T.rr[:, a // 2:128:8], 16, ["rr"], ["pR"], "xk")
+        list_set("R%d" % t, PR, lambda a: T.rr[:, a // 2:128:8], 16, ["rr"], ["pR"], "xk", two=CFG["two"][t][1])
         if t < RO - 1:
             lin("ipay", T.ipay[:, :], PR, 2.0, col("KP"), 16, ["pR", "KP"], ["ipay"], "xk")
         tt("k3", T.k3[:, :], PR, T.uph[:, :], ALU.max, 16, ["pR", "uph"], ["k3"], "xk")
@@ -463,17 +502,16 @@ def build(T, topo, core, rank):
         if t < RO - 1:
             tc = T.tc[:, TS_ * t:TS_ * t + TS_]
             pay = T["pay%d" % t]
-            if t == 0:
-                off, ok = xl(1, 0, 0, A)
-                gather("va", T.va[:, :], Ct[0][:, Z0:Z0 + V], off, A, CK[0] + ok, ["va"])
-                scatter("spay", pay[:, 16:16 + TS_], T.ipay[:, :], T.va[:, :], A, ["ipay", "va"], ["pay0"])
+            if t == 0 and CFG["spay"]:
+                scatter("spay", pay[:, 16:16 + TS_], T.ipay[:, :], T.cv[:, 0:A], A, ["ipay", "cv0"], ["pay0"])
             scatter("stc%d" % t, tc, T.ipay[:, :], T.vt[:, :], A, ["ipay", "vt"], ["tc%d" % t])
             lin("tch", T.tch[:, :], T.tc[:, TS_ * t:TS_ * t + S], 1.0, col("N2K"), S, ["tc%d" % t, "N2K"], ["tch"])
-            list_set("TL%d" % t, PT, lambda a: T.tch[:, a:S:16], 8, ["tch"], ["pT"], "xk")
+            list_set("TL%d" % t, PT, lambda a: T.tch[:, a:S:16], 8, ["tch"], ["pT"], "xk", two=CFG["two"][t][1])
             pl = T.pl[:, 8 * t:8 * t + 8]
             cp("t16", T.t16[:, 8 * t:8 * t + 8], PT, 8, ["pT"], ["t16%d" % t], "xk")
-            ts("mark", pay[:, 8:16], T.kh[:, :], T.cum[:, 127:128], 2.0 * V, ALU.is_ge, ALU.mult, 8, ["kh", "cum"], ["mark%d" % t])
-            if t > 0:
+            mm("cb", [(T.xk[:, 432:433], T.bw[:, :], T.cum[:, 127:128], True, True, 1)], ["bw", "cum"], ["pC"], "xk")
+            ts("mark", pay[:, 8:16], T.kh[:, :], T.xk[:, 432:433], 2.0 * V, ALU.is_ge, ALU.mult, 8, ["kh", "pC"], ["mark%d" % t], "xk")
+            if t > 0 or not CFG["spay"]:
                 lin("pl", pl, PT, 1.0, col("P2K"), 8, ["pT", "P2K"], ["pl%d" % t], "xk")
                 gather("pay%d" % t, pay[:, 16:16 + S], Ct[t][:, Z0:Z0 + CG], pl, S, CK[t] + ["pl%d" % t], ["pay%d" % t])
             add("send%d" % t, {"g": ((600.0, 0, 0, 0, 0), lambda g, t=t: send(g, t))}, ["pay%d" % t, "mark%d" % t], ["land%d" % t],
@@ -511,8 +549,12 @@ def build(T, topo, core, rank):
             for u in range(t + 1, RO):
                 scatter("sw%d%d" % (t, u), Ct[u][:, Z0:Z0 + CS], dl, arr, S, ["dl%d" % t, "arr%d" % t], CK[u])
     dma("st_n", "y", T.yn[:], T.pc[rows, Z0:Z0 + V], 131072, PK[3], ["yn"])
-    list_set("yc", T[mb][:, 320:400], lambda a: fo(5, 80 * a, 80 * a + 80), 80, keys("fo5", 0, L), ["pmg"], mb)
-    lin("ycs", T.ycs[:, :], T[mb][:, 320:400], 1.0, col("P2K"), 80, ["pmg", "P2K"], ["ycs"], mb)
+    if CFG["ycd"]:
+        dma("cp_c", "y", T.ych[:, :], T.fo[rows, 4 * L:5 * L], 20480, keys("fo5", 0, L), ["ych"])
+        lin("ycs", T.ycs[:, :], T.ych[:, :], 1.0, col("P2K"), 80, ["ych", "P2K"], ["ycs"])
+    else:
+        list_set("yc", T[mb][:, 320:400], lambda a: fo(5, 80 * a, 80 * a + 80), 80, keys("fo5", 0, L), ["pmg"], mb)
+        lin("ycs", T.ycs[:, :], T[mb][:, 320:400], 1.0, col("P2K"), 80, ["pmg", "P2K"], ["ycs"], mb)
     dma("st_c", "y", T.yc[:], T.ycs[:, :], 40960, ["ycs"], ["yc"])
     return ops
 
@@ -547,16 +589,20 @@ def lay(pred, succ, bank, head, hop, prio, pick):
                     t = f[k] if f[k] > t else t
                     k += 1
                 moved = False
-                for bs, bf, be in used.get(bank[i], ()):
-                    if be != e and bs - hop < t + c and bf + hop > t:
-                        t, moved = bf + hop, True
+                if bank[i]:
+                    u = used.setdefault(bank[i], [])
+                    m = after(u, (t - hop,))
+                    while m < len(u) and u[m][1] - hop < t + c:
+                        if u[m][2] != e and u[m][0] + hop > t:
+                            t, moved = u[m][0] + hop, True
+                        m += 1
             if best is None or t + c + h < best[0]:
                 best = (t + c + h, t, e, c, k)
         _x, t, e, c, k = best
         busy[e][0].insert(k, t)
         busy[e][1].insert(k, t + c)
         if bank[i]:
-            used.setdefault(bank[i], []).append((t, t + c, e))
+            u.insert(after(u, (t + c,)), (t + c, t, e))
         start[i], end[i], eng[i] = t, t + c, e
         for j in succ[i]:
             left[j] -= 1
@@ -565,23 +611,35 @@ def lay(pred, succ, bank, head, hop, prio, pick):
     return start, end, eng
 
 
-def replay(ops, order, eng, cost, hop, lf):
-    free, bank, last, end, why = {}, {}, {}, [0.0] * len(ops), [None] * len(ops)
-    for i in order:
-        o, e, t, y = ops[i], eng[i], 0.0, None
-        for d in o["deps"]:
-            x = end[d] + (0.0 if e == "t" and eng[d] == "t" else hop)
-            if x > t:
-                t, y = x, (d, 0)
-        if free.get(e, 0.0) > t:
-            t, y = free[e], (last[e], 1)
-        if o["bank"]:
-            p = bank.get(o["bank"])
-            if p is not None and eng[p] != e and end[p] + hop > t:
-                t, y = end[p] + hop, (p, 1)
-            bank[o["bank"]] = i
-        free[e], last[e], why[i] = t + cost[i][e], i, y
-        end[i] = free[e] + o["lat"] * lf
+def replay(ops, order, eng, cost, hop, lf, a=0, old=None):
+    free, bank, last, end, why = dict.fromkeys("vstgy", 0.0), {}, {}, [0.0] * len(ops), [None] * len(ops)
+    if old:
+        end, why = list(old[1]), list(old[2])
+        for i in order[:a]:
+            last[eng[i]] = bank[ops[i]["bank"]] = i
+        for e, i in last.items():
+            free[e] = end[i] - ops[i]["lat"] * lf
+    for i in order[a:]:
+        far, near, b, lat = ops[i]["plan"]
+        e = eng[i]
+        t, y, q = -hop, None, 0
+        for d in far:
+            if end[d] > t:
+                t, y = end[d], d
+        if b:
+            p = bank.get(b)
+            if p is not None and end[p] > t and eng[p] != e:
+                t, y, q = end[p], p, 1
+            bank[b] = i
+        t += hop
+        for d in near:
+            if end[d] > t:
+                t, y, q = end[d], d, 0
+        if free[e] > t:
+            t, y, q = free[e], last[e], 1
+        t += cost[i][e]
+        free[e], last[e], end[i] = t, i, t + lat * lf
+        why[i] = None if y is None else (y, q)
     return max(end), end, why
 
 
@@ -589,6 +647,9 @@ PLAN = {}
 
 
 def schedule(ops):
+    for o in ops:
+        near = [d for d in o["deps"] if "t" in o["alts"] and "t" in ops[d]["alts"]]
+        o["plan"] = ([d for d in o["deps"] if d not in near], near, o["bank"], o["lat"])
     if "order" not in PLAN:
         costs = [[{e: sum(a * b for a, b in zip(c, m[0])) for e, (c, _f) in o["alts"].items()} for o in ops] for m in PLANS]
         rng = np.random.default_rng(CFG["seed"])
@@ -602,12 +663,25 @@ def schedule(ops):
                 fs[d].append(o["i"])
                 bp[d].append((o["i"], gap(d, o["i"])))
 
-        def judge(order, eng):
-            r = [replay(ops, order, eng, costs[j], m[1], m[2]) for j, m in enumerate(PLANS)]
-            return 2 * r[0][0] + r[1][0] + r[2][0], r
+        def judge(order, eng, most=1e30, few=False, a=0, old=(None, None, None)):
+            r = [replay(ops, order, eng, costs[0], PLANS[0][1], PLANS[0][2], a, old[0])]
+            if r[0][0] > most or few:
+                return (1e30 if r[0][0] > most else r[0][0]), r
+            r += [replay(ops, order, eng, costs[j], PLANS[j][1], PLANS[j][2], a, old[j]) for j in (1, 2)]
+            return (2 * r[0][0] + r[1][0] + r[2][0]) / 4, r
+
+        links = [i for i in range(n) if "link" in ops[i]]
+        full = {i: [c[ops[i]["link"][0]]["t"] for c in costs] for i in links}
+
+        def relink(i, e):
+            for j, c in enumerate(costs):
+                c[ops[i]["link"][0]]["t"] = full[i][j] - (ops[i]["link"][1] * PLANS[j][0][4] if e == "v" else 0.0)
 
         def both(prio, hand):
-            pick = [[(e, c, hand[i] * c if e == "v" else 0.0) for e, c in costs[0][i].items()] for i in range(n)]
+            for i in links:
+                relink(i, "v" if hand[i] < 0 else "s")
+            pick = [[(e, c, hand[i] * c if e == "v" else 0.0) for e, c in costs[0][i].items() if i not in full or (e == "v") == (hand[i] < 0)]
+                    for i in range(n)]
             _s, f, eng = lay(fp, fs, bank, [0.0] * n, hop, prio, pick)
             fixed = [[(eng[i], costs[0][i][eng[i]], 0.0)] for i in range(n)]
             _s, f, _e = lay(bp, bs, bank, lat, hop, [-(f[i] + lat[i]) for i in range(n)], fixed)
@@ -619,6 +693,7 @@ def schedule(ops):
             rank[i] = min(costs[0][i].values()) + max([lat[i]] + [rank[j] + lag for j, lag in bp[i]])
         prio, h0 = -np.array(rank), CFG["hand"]
         hand = np.array([-h0 if o["n"][:2] == "sg" else h0 for o in ops])
+        hand[links] *= np.where(rng.random(len(links)) < CFG["byv"], -1.0, 1.0)
         best = score = None
         for it in range(CFG["iters"]):
             p, h = prio.copy(), hand.copy()
@@ -630,39 +705,66 @@ def schedule(ops):
             s, eng = both(p.tolist(), h.tolist())
             order = sorted(range(n), key=lambda i: (s[i], i))
             s2, r = judge(order, eng)
-            if score is None or s2 <= score + 1500.0 * (1 - it / CFG["iters"]) * rng.random() ** 2:
+            if score is None or s2 <= score + 400.0 * (1 - it / CFG["iters"]) * rng.random() ** 2:
                 score, prio, hand = s2, np.array(s), h
             if best is None or s2 < best[0]:
                 best = (s2, order, eng, r)
-        score, order, eng, r = best
-        for it in range(CFG["polish"]):
-            _m, end, why = r[int(rng.integers(0, len(PLANS)))]
-            i, cand = int(np.argmax(end)), []
-            while why[i] is not None:
-                if why[i][1]:
-                    cand.append((i, why[i][0]))
-                i = why[i][0]
-            i, p = cand[int(rng.integers(0, len(cand)))]
-            o2, e2, u = order, eng, rng.random()
-            j = p if u < 0.25 else i
-            if u < 0.4 and len(ops[j]["alts"]) > 1:
-                e2 = list(eng)
-                e2[j] = [e for e in ops[j]["alts"] if e != eng[j]][0]
-            else:
-                a, b = order.index(p), order.index(i)
-                seg, need = order[a:b + 1], {i}
-                for x in reversed(seg):
-                    if x in need:
-                        need.update(ops[x]["deps"])
-                if p in need:
-                    continue
-                o2 = order[:a] + [x for x in seg if x in need] + [x for x in seg if x not in need] + order[b + 1:]
-            s2, r2 = judge(o2, e2)
-            if s2 <= score + 300.0 * (1 - it / CFG["polish"]) * rng.random() ** 4:
-                score, order, eng, r = s2, o2, e2, r2
-            if score < best[0]:
-                best = (score, order, eng, r)
-        PLAN["order"], PLAN["eng"], PLAN["val"] = best[1], best[2], [x[0] for x in best[3]]
+
+        def waits(r):
+            out = []
+            for m, end, why in r:
+                i = end.index(m)
+                while why[i] is not None:
+                    if why[i][1]:
+                        out.append((i, why[i][0]))
+                    i = why[i][0]
+            return out
+
+        order, eng = best[1:3]
+        dear = [i for i in range(n) if len(costs[0][i]) > 1 and max(costs[0][i].values()) > min(costs[0][i].values()) + 50.0]
+        dear += links
+        for many, heat, few in CFG["polish"]:
+            for i in links:
+                relink(i, eng[i])
+            score, r = judge(order, eng, few=few)
+            best, cand = (score, order, eng), waits(r)
+            for it, (u0, u, u2, u3) in enumerate(rng.random((many, 4)).tolist()):
+                if it % 200 == 0:
+                    order = sorted(order, key=lambda i: r[0][1][i] - lat[i] - costs[0][i][eng[i]])
+                    score, r = judge(order, eng, few=few)
+                    cand = waits(r)
+                i, p = cand[int(u0 * len(cand))]
+                o2, e2 = order, eng
+                j = dear[int(u0 * len(dear))] if u < 0.05 else p if u < 0.2 else i
+                if u < 0.3 and len(ops[j]["alts"]) > 1:
+                    e2, a = list(eng), order.index(j)
+                    e2[j] = [e for e in ops[j]["alts"] if e != eng[j]][0]
+                    if j in full:
+                        relink(j, e2[j])
+                        a = min(a, order.index(ops[j]["link"][0]))
+                else:
+                    a, b = order.index(p), order.index(i)
+                    seg, ahead = order[a:b + 1], u2 < 0.5
+                    need = {i if ahead else p}
+                    for x in (reversed(seg) if ahead else seg):
+                        if x in need:
+                            need.update(bs[x] if ahead else fs[x])
+                    if p in need and i in need:
+                        continue
+                    o2 = order[:a] + [x for x in seg if (x in need) == ahead] + [x for x in seg if (x in need) != ahead] + order[b + 1:]
+                h = heat * (1 - it / many)
+                s2, r2 = judge(o2, e2, r[0][0] + 300.0 + h, few, a, r)
+                if s2 + CFG["thrift"] * (costs[0][j][e2[j]] - costs[0][j][eng[j]]) <= score - 0.3 * h * math.log(u3 + 1e-12):
+                    score, order, eng, r = s2, o2, e2, r2
+                    cand = waits(r)
+                    if score < best[0]:
+                        best = (score, order, eng)
+                elif j in full:
+                    relink(j, eng[j])
+            order, eng = best[1:3]
+        for i in links:
+            relink(i, eng[i])
+        PLAN["order"], PLAN["eng"], PLAN["val"] = order, eng, [x[0] for x in judge(order, eng)[1]]
     for o, e in zip(ops, PLAN["eng"]):
         o["e"] = e
     return PLAN["order"]

import math
import numpy as np
from concourse.bass import DstId, RemoteDMATransfer
from concourse.mybir import dt, AluOpType, AxisListType, ActivationFunctionType

ALU = AluOpType
ACT = ActivationFunctionType
V, L, A, S, RO = 4096, 1280, 256, 128, 3
PW = S + 8
BIG = float(2 ** 36)
ZH = 1280.0
M1 = 1.5 * 2 ** 23
Z0 = 16
CG, CS = V + 2 * S, 2 * V + V + 2 * S
PS_, TS_ = V + 2 * A, V + 3 * A
NC = 2178.0
CFG = {"iters": 60, "polish": ((60000, 400.0, True), (7500, 100.0, False)), "spay": 1, "cutb": 2, "thrift": 0.3, "byv": 0.6, "ycd": 1, "cuta": (1, 1, 0), "seed": 2, "hand": 8.0,
       "fold": ((1, 1), (0, 1), (0, 1)),
       "two": ((0, 0), (0, 0), (0, 0)),
       "ch": (0, 256, 576, 896, 1280),
       "parts": (2, 2, 2),
       "joint": (0, 0, 0),
       "pieces": (0, 640, 1280),
       "inv": ("ss", "ss", "ss")}
PLANS = (((1.0, 0.83, 1.3, 3.15, 0.42), 200.0, 1.3), ((1.0, 0.85, 1.0, 2.0, 0.5), 100.0, 1.7), ((1.0, 1.16, 2.25, 5.8, 0.63), 200.0, 1.3))

_bf, _f, _i, _u, _h = "bfloat16", "float32", "int32", "uint16", "float16"
_SB = {
    _bf: {"ca": Z0 + CS, "cb": Z0 + CS, "pg": 128, "ih": 128, "inh": 128, "ione": 128, "i4k": 128, "gm": 288, "bkp": 1024, "bkn": 1024,
          "st": 128, "sh": 384, "z": L, "sg": L, "ml": 320, "eq": 4096, "pay0": 16 + TS_, "pay1": 16 + S,
          "arr": 2 * S, "land": 6 * PW, "inv": 1200},
    _f: {"pc": Z0 + PS_, "nxf": 256, "tc": 2 * TS_, "col": 48, "rsel": 16, "gsel": 8, "pm": 144, "iom": 128, "kh": 8, "pcf": 128,
         "vl": 16, "vt": 256, "uph": 16, "k3": 16, "ycs": 80},
    _i: {"pa": Z0 + PS_, "pb": Z0 + PS_, "nxi": 256, "curi": 80, "wti": 8, "ip": 8, "iq": 8, "li": 80, "lj": 80},
    _u: {"x0": 320, "xs": 960, "xu": 960, "ipay": 16, "itg": 16, "pl": 16, "dl": 16},
    _h: {"cv": L, "ineg": 128, "ych": 80, "zh": L, "dh": L, "ihh": 128, "tw": 128, "cutp": 128, "cum": 128, "idp": 144, "gp": 144, "bw": 128, "sw": 128, "fo": 5 * L, "xf": 320, "xm": 320, "vw": 256, "pcn": 128, "cutr": 128,
         "rr": 128, "tch": 128, "t16": 16},
}
SCRATCH = {k: ("sbuf", [128, n], d) for d, b in _SB.items() for k, n in b.items()}
BANKS = ("d0", "d1", "d2", "d3", "lb", "ma", "mb", "xk")
SCRATCH.update({k: ("psum", [128, 512], _f) for k in BANKS})
SEMAPHORES = ["nv", "ns", "nt", "ng", "arr0", "arr1", "hin0", "hin1", "sent0", "sent1"] + ["dq%d" % k for k in range(20)]
HE = 4


def routes(T, topo):
    out = []
    n = len(T.cores)
    for q, c in enumerate(T.cores):
        used, row = [], []
        for e in range(n - 1):
            r = (q + 1 + e) % n
            d = T.cores[r]
            if topo.may_write(c, d):
                row.append((r, None))
                continue
            able = [h for h in topo.cores_of(c) if h not in T.cores and topo.may_write(h, d) and h not in used]
            able.sort(key=lambda h: topo.die(h) != topo.die(c))
            used.append(able[0])
            row.append((r, able[0]))
        out.append(row)
    return out


def as_mask(engs):
    return sum(1 << e for e in engs)


def helper_program(g, core, T, topo, e, r):
    d = T.cores[r]
    engs = topo.engines(core, d)
    rid, pid = topo.addr(d, core)
    for t in range(RO - 1):
        g.wait_ge(T.sem["hin%d" % t], HE)
        s = (3 * t + e) * PW
        g.remote_dma(T.land[:, s:s + PW], T.land[:, s:s + PW], T.sem["arr%d" % t], T.sem["sent%d" % t], pid, rid, as_mask(engs))
    for t in range(RO - 1):
        g.wait_ge(T.sem["sent%d" % t], len(engs))


def build(T, topo, core, rank):
    ops, last_w, readers = [], {}, {}

    def add(name, alts, r=(), w=(), bank=None, lat=0.0, dma=False, after=(), ext=None):
        i = len(ops)
        deps = set(after)
        for k in list(r) + list(w):
            if k in last_w:
                deps.add(last_w[k])
        for k in w:
            deps.update(readers.get(k, ()))
        for k in r:
            readers.setdefault(k, []).append(i)
        for k in w:
            last_w[k] = i
            readers[k] = []
        deps.discard(i)
        ops.append({"n": name, "alts": alts, "deps": sorted(deps), "bank": bank, "lat": lat, "dma": dma, "ext": ext, "i": i})
        return i

    def keys(name, lo, hi):
        return ["%s.%d" % (name, b) for b in range(lo // 64, (hi + 63) // 64)]

    def cv(n, f=1.0):
        return (30.0, max(64.0, n * f), 0, 0, 0)

    def ts(name, out, in0, s1, s2, op0, op1, n, r, w, bank=None, f=1.0):
        if op1 is None:
            fn = lambda g: g.vector.tensor_scalar(out, in0, s1, None, op0)
        else:
            fn = lambda g: g.vector.tensor_scalar(out, in0, s1, s2, op0, op1)
        return add(name, {"v": (cv(n, f), fn)}, r, w, bank)

    def tt(name, out, in0, in1, op, n, r, w, bank=None):
        return add(name, {"v": (cv(n, 1.0 if bank else 2.0), lambda g: g.vector.tensor_tensor(out, in0, in1, op))}, r, w, bank)

    def cp(name, out, in_, n, r, w, bank=None, both=True, f=1.0):
        alts = {"v": (cv(n, f), lambda g: g.vector.tensor_copy(out, in_))}
        if both:
            alts["s"] = (cv(n), lambda g: g.scalar.activation(out, in_, ACT.Copy))
        return add(name, alts, r, w, bank)

    def lin(name, out, in_, sc, bi, n, r, w, bank=None, f=1.0):
        alts = {"v": (cv(n, f), lambda g: g.vector.tensor_scalar(out, in_, sc, bi, ALU.mult, ALU.add)),
                "s": (cv(n), lambda g: g.scalar.activation(out, in_, ACT.Identity, bias=bi, scale=sc))}
        return add(name, alts, r, w, bank)

    def relu(name, out, in_, bi, n, r, w, bank=None):
        alts = {"v": (cv(n), lambda g: g.vector.tensor_scalar(out, in_, bi(), 0.0, ALU.add, ALU.max)),
                "s": (cv(n), lambda g: g.scalar.activation(out, in_, ACT.Relu, bias=bi()))}
        return add(name, alts, r, w, bank)

    def ms(name, ap, c, n, w, f=0.5):
        small = {} if f == 1.0 else {"allow_small_or_imprecise_dtypes": True}
        return add(name, {"v": (cv(n, f), lambda g: g.vector.memset(ap, c)),
                          "g": ((150, 2.0 * n, 0, 0, 0), lambda g: g.iota(ap, [[0, n]], int(c), 0, **small))}, (), w)

    def red(name, out, in_, r, w):
        return add(name, {"v": (cv(16), lambda g: g.vector.tensor_reduce(out, in_, AxisListType.X, ALU.add))}, r, w)

    def gather(name, out, win, off, n, r, w, bi=None):
        if bi is None:
            alts = {"v": ((55, 0, n, 0, 0), lambda g: g.vector.tensor_copy(out, win.indirect(off))),
                    "s": ((70, 0, n, 0, 0), lambda g: g.scalar.activation(out, win.indirect(off), ACT.Copy))}
        else:
            alts = {"v": ((55, 0, n, 0, 0), lambda g: g.vector.tensor_scalar(out, win.indirect(off), bi, None, ALU.add)),
                    "s": ((70, 0, n, 0, 0), lambda g: g.scalar.activation(out, win.indirect(off), ACT.Identity, bias=bi))}
        return add(name, alts, r, w)

    def gather_tt(name, out, win, off, in1, op, n, r, w):
        return add(name, {"v": ((55, 0, n, 0, 0), lambda g: g.vector.tensor_tensor(out, win.indirect(off), in1, op))}, r, w)

    def scatter(name, win, off, in_, n, r, w):
        return add(name, {"v": ((55, 0, 0, n, 0), lambda g: g.vector.tensor_copy(win.indirect(off), in_))}, r, w)

    def mm(name, items, r, w, bank, after=()):
        def fn(g, i=len(ops)):
            its = items
            if "short" in ops[i] and ops[ops[i]["short"]]["e"] == "v":
                its = items[:-2] + [items[-2][:4] + items[-1][4:]]
            for o, a, b, s0, s1, _n in its:
                ins = g.tensor.matmul(o, a, b, s0, s1)
            return ins
        return add(name, {"t": ((20, 0, 0, 0, sum(max(64, it[5]) if it[5] > 0 else -it[5] for it in items)), fn)}, r, w, bank, after=after)

    def dma(name, q, out, in_, nbytes, r, w, after=()):
        fn = (lambda g: g.sync.dma_start(out, in_)) if q == "y" else (lambda g: g.scalar.dma_start(out, in_))
        return add(name, {q: ((100.0, 0, 0, 0, 0), fn)}, r, w, lat=1800 + nbytes / 200.0, dma=True, after=after)

    def iota(name, out, pattern, base, cm, n, w, integer=False):
        if integer:
            fn = lambda g: g.iota(out, pattern, base, cm)
        else:
            fn = lambda g: g.iota(out, pattern, base, cm, allow_small_or_imprecise_dtypes=True)
        return add(name, {"g": ((150, 2.0 * n, 0, 0, 0), fn)}, (), w)

    names = ["GF", "PF", "SHF", "PARF", "W4", "SWF", "C14", "C15", "OFF0s", "OFF0v", "OFF1s", "OFF1v", "OFF2s", "OFF2v", "R13", "R14", "R15",
             "K0", "K1", "K2", "NQH", "PZH", "M30", "M31", "M32", "NM1", "P2K", "N2K", "YB0", "YB1",
             "NQ", "TH2", "TH3", "TH4", "KP", "KU", "KT", "TA", "TB", "TC", "TD", "TE", "P2Z"]
    col = lambda k: T.col[:, names.index(k):names.index(k) + 1]
    gm = lambda fam, a: T.gm[:, fam * 144 + 15 - a: fam * 144 + 15 - a + 128]
    gp = lambda a: T.gp[:, 15 - a:15 - a + 128]
    GC, GW = 0, 1
    idf = T.idp[:, 0:128]
    cut = CFG["ch"]
    CH = [(cut[k], cut[k + 1]) for k in range(len(cut) - 1)]
    NB = max((hi - lo) // 64 for lo, hi in CH)
    rows = slice(0, 128, 16)
    vb, mb = ("d3", "d3") if len(CH) < 4 else ("xk", "lb")

    PA = ["pa%d" % b for b in range(8)]
    for k, (a, b) in enumerate(((0, 320), (320, 1952))):
        add("fill", {"v": (cv(b - a), lambda g, a=a, b=b: g.vector.memset(T.pa[:, a:b], 0))}, (), PA[k:k + 1])
    for k in range(4):
        add("fill", {"s": (cv(320), lambda g, k=k: g.scalar.activation(T.pa[:, 1952 + 320 * k:2272 + 320 * k], T.pa[:, 0:320], ACT.Copy))}, PA[0:1], PA[2 + k:3 + k])
    iota("fill6", T.pa[:, 3232:Z0 + V], [[0, 880]], 0, 0, 880, PA[6:7], True)
    nx = dma("ld_nx", "y", T.pa[rows, Z0:Z0 + V], T.nx[:], 131072, (), PA)
    c1 = dma("ld_c1", "y", T.ca[:, Z0 + 2048:Z0 + V], T.cards[:, 2048:V], 600000, (), ["ca1"], after=ops[nx]["deps"])
    dma("ld_cur", "y", T.curi[:, :], T.cur[:], 40960, (), ["curi"])
    c0 = dma("ld_c0", "y", T.ca[:, Z0:Z0 + 2048], T.cards[:, 0:2048], 900000, (), ["ca0"])
    dma("ld_wt", "y", T.wti[:, 0:1], T.wt[:], 10000, (), ["wti"])
    dma("ld_z", "y", T.z[:, :], T.z0[:], 500000, (), ["z%d" % k for k in range(len(CH))])
    dma("ld_cb", "y", T.cb[:, Z0:Z0 + V], T.cards[:, :], 1048576, (), ["cb0"], after=[c0, c1])

    iota("pm", T.pm[:, :], [[-1, 144]], 0, 1, 144, ["pm"])
    iota("ip", T.ip[:, 0:2], [[16, 2]], 0, 1, 2, ["ip"], True)
    iota("pg", T.pg[:, :], [[-16, 8], [0, 16]], 0, 1, 128, ["pg"])
    iota("iom", T.iom[:, :], [[1, 128]], 0, 0, 128, ["iom"])
    ts("idp", T.idp[:, :], T.pm[:, :], 0.0, None, ALU.is_equal, None, 144, ["pm"], ["idp"])
    for nms, base, step in ((["NM1"], -int(M1 + ZH), 0), (["NQH", "PZH"], int(2 * ZH) - 1, 1 - int(ZH)), (["P2K", "N2K"], 2048, -4096), (["P2Z"], 2048 + Z0, 0), (["YB0", "YB1"], Z0 - 2048, -4096), (["NQ", "TH2", "TH3", "TH4"], -1, 2)):
        k = names.index(nms[0])
        iota(nms[0], T.col[:, k:k + len(nms)], [[step, len(nms)]], base, 0, len(nms), nms)
    lin("gp0", T.gp[:, :], T.pm[:, :], 0.0, 0.0, 144, ["pm"], ["gp"])
    ts("gp", T.gp[:, 15:143:16], T.pg[:, 0:128:16], 0.0, None, ALU.is_equal, None, 8, ["pg"], ["gp"])
    ts("ir", T.iq[:, 1:2], T.ip[:, 0:1], 15, None, ALU.bitwise_and, None, 1, ["ip"], ["iq1"])
    ts("ig", T.iq[:, 0:1], T.ip[:, 0:1], 4, None, ALU.arith_shift_right, None, 1, ["ip"], ["iq0"])
    ts("ish", T.iq[:, 3:4], T.ip[:, 1:2], 127, None, ALU.bitwise_and, None, 1, ["ip"], ["iq3"])
    ts("ipar", T.iq[:, 4:5], T.ip[:, 0:1], 1, None, ALU.bitwise_and, None, 1, ["ip"], ["iq4"])
    cp("gf", col("GF"), T.iq[:, 0:1], 1, ["iq0"], ["GF"])
    cp("pf", col("PF"), T.ip[:, 0:1], 1, ["ip"], ["PF"])
    cp("shf", T.col[:, names.index("SHF"):names.index("SHF") + 2], T.iq[:, 3:5], 2, ["iq3", "iq4"], ["SHF", "PARF"])
    cp("w4", col("W4"), T.wti[:, 0:1], 1, ["wti"], ["W4"])
    ts("gsel", T.gsel[:, :], T.iom[:, 0:8], col("GF"), None, ALU.is_equal, None, 8, ["iom", "GF"], ["gsel"])
    ms("gm", T.gm[:, :], 0.0, 288, ["gm0", "gm1"])
    lin("gw", T.gm[:, GW * 144 + 15:GW * 144 + 143:16], T.gsel[:, :], col("W4"), 0.0, 8, ["gsel", "W4"], ["gm%d" % GW])
    lin("gc", T.gm[:, GC * 144 + 15:GC * 144 + 143:16], T.gsel[:, :], -BIG, 0.0, 8, ["gsel"], ["gm%d" % GC])
    for nm, sc in (("ihh", 0.5), ("ih", 0.5), ("inh", -0.5), ("ione", 1.0), ("ineg", -1.0), ("i4k", -4096.0)):
        lin(nm, T[nm][:, :], idf, sc, 0.0, 128, ["idp"], [nm], f=0.5)
    for k in range(3):
        ts("r%d" % k, col("R1%d" % (3 + k)), T.iq[:, 1:2], 13.0 + k, None, ALU.is_equal, None, 1, ["iq1"], ["R1%d" % (3 + k)])
    ts("c14", col("C14"), col("R13"), col("R14"), 0.125, ALU.subtract, ALU.mult, 1, ["R13", "R14"], ["C14"])
    ts("c15", col("C15"), col("R15"), -0.125, 1.0, ALU.mult, ALU.add, 1, ["R15"], ["C15"])
    for a in range(NB):
        ts("bkp%d" % a, T.bkp[:, 128 * a:128 * a + 128], T.pg[:, :], float(a), col("C14"), ALU.is_equal, ALU.add, 128, ["pg", "C14"], ["bkp%d" % a], f=0.5)
        ts("bkn%d" % a, T.bkn[:, 128 * a:128 * a + 128], T.pg[:, :], float(a), col("C15"), ALU.not_equal, ALU.subtract, 128, ["pg", "C15"], ["bkn%d" % a], f=0.5)
    lin("offa", col("K0"), col("R14"), 0.25, 0.0, 1, ["R14"], ["K0"])
    lin("offb", col("K1"), col("R13"), ZH / 2, col("K0"), 1, ["R13", "K0"], ["K1"])
    lin("offb", col("K2"), col("R15"), M1, col("K1"), 1, ["R15", "K1"], ["K2"])
    ts("offc", col("TC"), T.iq[:, 1:2], 13.0, BIG, ALU.is_lt, ALU.mult, 1, ["iq1"], ["TC"])
    for k in range(3):
        for e, off in (("s", 1.0), ("v", 17.0)):
            lin("off", col("OFF%d%s" % (k, e)), col("TC"), off, col("K%d" % k), 1, ["K%d" % k, "TC"], ["OFF%d%s" % (k, e)])
    ms("st", T.st[:, :], 0.0, 128, ["st"])
    ts("bw", T.bw[:, :], T.pg[:, :], 0.0, None, ALU.is_equal, None, 128, ["pg"], ["bw"], f=0.5)
    ts("swa", col("TD"), col("PARF"), -2.0, 1.0, ALU.mult, ALU.add, 1, ["PARF"], ["TD"])
    lin("swf", col("SWF"), col("TD"), 1.0, col("PF"), 1, ["TD", "PF"], ["SWF"])
    ts("swm", T.sw[:, :], T.iom[:, :], col("SWF"), None, ALU.is_equal, None, 128, ["iom", "SWF"], ["sw"])
    ts("kp", col("KP"), col("PARF"), -2.0, None, ALU.add, None, 1, ["PARF"], ["KP"])
    ts("kt", col("KT"), col("PARF"), -258.0, None, ALU.add, None, 1, ["PARF"], ["KT"])
    ts("ku", col("KU"), col("PARF"), -0.5, 1153.0, ALU.mult, ALU.add, 1, ["PARF"], ["KU"])
    iota("pcf", T.pcf[:, :], [[2, 128]], int(NC), 0, 128, ["pcf"])
    cp("pcn", T.pcn[:, :], T.pcf[:, :], 128, ["pcf"], ["pcn"])
    iota("kh0", T.kh[:, :], [[16, 8]], 0, 1, 8, ["kh"])
    ts("kh1", col("TD"), col("GF"), -8.0, None, ALU.mult, None, 1, ["GF", "SWF"], ["TD"])
    lin("kh2", T.kh[:, :], T.kh[:, :], 0.5, col("TD"), 8, ["kh", "TD"], ["kh"])
    for e in range(3):
        red("m3%d" % e, col("M3%d" % e), T.gsel[:, e:8:3], ["gsel"], ["M3%d" % e])
        ts("sh%d" % e, T.sh[:, 128 * e:128 * e + 128], T.iom[:, :], col("SHF"), col("M3%d" % e), ALU.is_equal, ALU.mult, 128, ["iom", "SHF", "M3%d" % e], ["sh%d" % e])
    for nm in ("ca", "cb"):
        ms(nm + "z", T[nm][:, 0:Z0], 0.0, Z0, [nm + "z"])
        ms(nm + "y", T[nm][:, Z0 + V:Z0 + CG], 0.0, CG - V, [nm + "y"])
    ms("pay0", T.pay0[:, 16:16 + S], 0.0, S, ["pay0"])
    for k in range(8):
        iota("junk", T.pb[:, 514 * k:514 * k + 514], [[0, 514]], 0, 0, 514, ["pb%d" % k], True)
    for t in range(RO - 1):
        iota("tc%d" % t, T.tc[:, TS_ * t:TS_ * t + S], [[2, S]], V, 0, S, ["tc%d" % t])

    dma("ld_pb", "y", T.pb[rows, Z0:Z0 + V], T.nx[:], 131072, (), ["pb"] + ["pb%d" % k for k in range(8)])
    Pt, PK = [T.pa, T.pb, T.pa, T.pc], [PA, ["pb"], PA, ["pc"]]
    CA = ["ca0", "ca1", "caz", "cay"]
    Ct, CK = [T.ca, T.cb, T.ca], [CA, ["cb0", "cbz", "cby"], CA]
    cp("x0", T.x0[:, 0:80], T.curi[:, :], 80, ["curi"], keys("x0_0", 0, L))

    rts = routes(T, topo)

    def parts(t):
        return [(0, L)] if CFG["parts"][t] == 1 else [(0, CH[0][1]), (CH[0][1], L)]

    def part_of(t, lo):
        return [p for p in parts(t) if p[0] <= lo < p[1]][0]

    def xl(t, k, lo, hi):
        if k == 0:
            ap = T.x0[:, 80 * t + lo // 16:80 * t + hi // 16]
        elif k < 5:
            p0, p1 = part_of(t, lo)
            b = 320 * t + p0 // 4 + (k - 1) * (p1 - p0) // 16 - p0 // 16
            ap = T.xs[:, b + lo // 16:b + hi // 16]
        elif k == 5:
            ap = T.xu[:, 320 * t + lo // 16:320 * t + hi // 16]
        else:
            p0, p1 = part_of(t, lo)
            b = 320 * t + 80 + 3 * p0 // 16 + (k - 6) * (p1 - p0) // 16 - p0 // 16
            ap = T.xu[:, b + lo // 16:b + hi // 16]
        return ap, keys("x%d_%d" % (k, t), lo, hi)

    def fo(s, lo, hi, step=1):
        b = (s - 1) * L
        return T.fo[:, b + lo:b + hi:step] if step > 1 else T.fo[:, b + lo:b + hi]

    def list_set(name, out, src, n, r, w, bank, fam=None, more=(), two=False):
        if two:
            mm(name + "a", [(T.ma[0:n, 384 + a:512:16], src(a), T.gp[:, 15:143:16], True, True, -n) for a in range(16)], r + ["gp"], ["Bma4"], "ma")
            cp("tw", T.tw[0:n, :], T.ma[0:n, 384:512], 128, ["Bma4"], ["tw"], "ma")
            items, r = [(out, T.tw[0:n, :], T.idp[0:n, 0:n], True, not more, n)], ["tw", "idp"]
        else:
            st = gp if fam is None else (lambda a: gm(fam, a))
            items, r = [(out, st(a), src(a), a == 0, a == 15 and not more, n) for a in range(16)], r + ["gp" if fam is None else "gm%d" % fam]
        return mm(name, items + [m[0] for m in more], r + [k for m in more for k in m[1]], w, bank)

    def folded(t, lo):
        return CFG["fold"][t][parts(t).index(part_of(t, lo))]

    over = {}

    def walk_lists(t, j, first):
        lo, hi = parts(t)[j]
        n, o = (hi - lo) // 16, lo // 16
        one = len(parts(t)) == 1
        b1, b2 = ("ma", "mb") if one else (("ma", "ma") if j == 0 else ("mb", "mb"))
        k1, k2, u = b1, b2, 0
        if len(CH) > 4 and j == 0:
            b1, b2, u = "mb", "mb", 64
        pcl, pcy = T[b1][:, u:u + n], T[b1][:, u + n:u + 4 * n]
        q = 0 if one else u + 4 * n
        psel, pus = T[b2][:, q:q + 4 * n], (T[b2][:, 4 * n:5 * n] if one else pcl)
        kus = "B%s2" % k2 if one else "B%s0" % k1
        zk = ["z%d" % k for k, c in enumerate(CH) if lo <= c[0] < hi]
        xk = lambda k: xl(t, k, lo, hi)
        e = CFG["inv"][t][j]
        ib = 400 * t + 5 * o
        iv = lambda s0, s1: T.inv[:, ib + (s0 - 1) * n:ib + s1 * n]
        ik = "inv%d%d" % (t, j)
        iks = [ik + x for x in ("e1", "2", "3", "4", "e5")]
        yb = col("YB1" if e == "v" else "YB0")
        if first:
            over[t, lo] = (iv, ik, yb)
            list_set("cl%d%d" % (t, j), pcl, lambda a: T.z[:, lo + a:hi:16], n, zk, ["B%s%d" % (b, k) for b in (k1, k2) for k in range(4)], b1, GW)
            cp("cli", T.li[:, o:o + n], pcl, n, ["B%s0" % k1], keys("li", lo, hi), b1)
            lj = T.lj[:, o:o + n]
            ts("clj", lj, T.li[:, o:o + n], 3, None, ALU.bitwise_and, None, n, keys("li", lo, hi), keys("lj", lo, hi))
            for s, c in ((1, -1.0), (5, 1.0)):
                ms("inve", iv(s, s), c - (e == "v"), n, [ik + "e%d" % s])
            for s in range(2, 5):
                if e == "s":
                    fn = lambda g, s=s: g.scalar.activation(iv(s, s), lj, ACT.Sign, bias=col("TH%d" % s), scale=-2.0)
                else:
                    fn = lambda g, s=s: g.vector.tensor_scalar(iv(s, s), lj, s - 1.5, -2.0, ALU.is_gt, ALU.mult)
                add("inv", {e: (cv(n), fn)}, keys("lj", lo, hi) + ["TH%d" % s], [ik + str(s)])
            mm("sel%d%d" % (t, j), [(psel, T.ih[:, :], iv(2, 5), True, False, 4 * n), (psel, T.inh[:, :], iv(1, 4), False, True, 4 * n)],
               iks + ["ih", "inh"], ["B%s3" % k2], b2)
            return
        xf, xm = T.xf[:, 4 * o:4 * o + 4 * n], T.xm[:, 4 * o:4 * o + 4 * n]
        src = T.xs[:, 320 * t + 4 * o:320 * t + 4 * o + 4 * n]
        ts("xf", xf, src, -2048.0 - Z0 * folded(t, lo), None, ALU.add, None, 4 * n, sum((xk(s)[1] for s in range(1, 5)), []), keys("xf", lo, hi), f=0.5)
        if not folded(t, lo):
            mm("cy%d%d" % (t, j), [(pcy, idf, T.xf[:, 4 * o + n:4 * o + 4 * n], True, False, 3 * n), (pcy, T.i4k[:, :], iv(2, 4), False, True, 3 * n)],
               iks + ["idp", "i4k"] + keys("xf", lo, hi), ["B%s1" % k1], b1)
            b = 320 * t + 80 + 3 * o
            relu("yl", T.xu[:, b:b + 3 * n], pcy, lambda: yb, 3 * n, ["B%s1" % k1, "YB0", "YB1"], sum((xk(k)[1] for k in range(6, 9)), []), b1)
        tt("xm", xm, psel, xf, ALU.mult, 4 * n, ["B%s3" % k2] + keys("xf", lo, hi), keys("xm", lo, hi), b2)
        mm("us%d%d" % (t, j), [(pus, idf, T.xm[:, 4 * o + s * n:4 * o + s * n + n], s == 0, s == 3, n) for s in range(4)],
           ["idp"] + keys("xm", lo, hi), [kus], b2)
        lin("ul", xk(5)[0], pus, 1.0, col("P2K"), n, [kus, "P2K"], xk(5)[1], b2)

    def z_chain(t, ch):
        lo, hi = CH[ch]
        n = hi - lo
        nb = n // 64
        dk, zk, hk = ("d0", "d1", "d2", "d3", "ma")[ch], "z%d" % ch, "dh%d" % ch
        D, C = T[dk][:, 0:n], T[dk][:, 448:512]
        zz, dh, sgv, ml = T.z[:, lo:hi], T.dh[:, lo:hi], T.sg[:, lo:hi], T.ml[:, 64 * ch:64 * ch + 64]
        zh, cv5, fold = T.zh[:, lo:hi], T.cv[:, lo:hi], folded(t, lo)
        for s in range(1, 5):
            off, ok = xl(t, s if fold or s == 1 else s + 4, lo, hi)
            win = Ct[t][:, Z0:Z0 + V] if s == 1 and not fold else Ct[t][:, 0:Z0 + V]
            zin, zr, one, nq, th = (zz, zk, T.ione[:, :], "NQ", 0.0) if s == 1 else (zh, "h" + zk, idf, "NQH", -ZH)
            gather_tt("gs%d%d%d" % (t, ch, s), dh, win, off, zin, ALU.subtract, n, CK[t] + ok + [zr], [hk])
            so = add("sg%d%d%d" % (t, ch, s), {"s": (cv(n), lambda g, nq=nq: g.scalar.activation(sgv, dh, ACT.Sign, bias=col(nq), scale=2.0)),
                                               "v": (cv(n, 0.5), lambda g, th=th: g.vector.tensor_scalar(sgv, dh, th, 2.0, ALU.is_gt, ALU.mult))},
                     [hk, nq], ["sg%d" % ch])
            mm("cnt%d%d%d" % (t, ch, s), [(C, gm(GC, a), T.sg[:, lo + 64 * a:lo + 64 * a + 64], a == 0, a == nb - 1, 64) for a in range(nb)],
               ["sg%d" % ch, "gm%d" % GC], ["pcn%d" % ch], dk)
            kind = "OFF%d" % (0, 1, 1, 2)[s - 1]
            relu("ml%d%d%d" % (t, ch, s), ml, C, lambda so=so, kind=kind: col(kind + ops[so]["e"]), 64,
                 ["pcn%d" % ch, kind + "v", kind + "s"], ["ml%d" % ch], dk)
            items = [(D, T.ihh[:, :], dh, True, False, n)]
            for bk in (T.bkp, T.bkn):
                items += [(T[dk][:, 64 * a:64 * a + 64], bk[:, 128 * a:128 * a + 128], ml, False, False, 64) for a in range(nb)]
            items.append((D, one, zin, False, s < 4, n))
            up = mm("upd%d%d%d" % (t, ch, s), items, ["ml%d" % ch, "ihh", "ione", hk, zr] + ["bk%s%d" % (x, a) for a in range(nb) for x in "pn"], [dk], dk)
            if s == 1:
                lin("zo%d%d%d" % (t, ch, s), zh, D, 1.0, col("PZH"), n, [dk, "PZH"], ["h" + zk], dk)
            elif s < 4:
                i = add("zo%d%d%d" % (t, ch, s), {"v": (cv(n), lambda g: g.vector.tensor_tensor(zh, D, zh, ALU.add)),
                                                  "s": (cv(n), lambda g: g.scalar.activation(zh, D, ACT.Copy))}, [dk], ["h" + zk], dk)
                ops[i]["link"], ops[up]["short"] = (up, n), i
            else:
                if (t, ch) not in shown:
                    off, ok = xl(t + 1, 0, lo, hi)
                    src = Ct[t][:, Z0:Z0 + V].indirect(off)
                    i = add("cv%d%d" % (t, ch), {"v": ((55, 0, n, 0, 0), lambda g: g.vector.tensor_tensor(cv5, src, zh, ALU.subtract)),
                                                 "s": ((70, 0, n, 0, 0), lambda g: g.scalar.activation(cv5, src, ACT.Copy))},
                            CK[t] + ok + [zr], ["cv%d" % ch])
                    ops[i]["link"], ops[up]["short"] = (up, n), i
                mm("rv%d%d" % (t, ch), [(D, T.ineg[:, :], cv5, False, True, n)], ["ineg", "cv%d" % ch], [dk], dk)
        add("abs%d%d" % (t, ch), {"s": (cv(n), lambda g: g.scalar.activation(zz, D, ACT.Abs, bias=col("NM1")))}, [dk, "NM1"], [zk], dk)
        if t == RO - 1:
            dma("st_z%d" % ch, "y", T.yz[:, lo:hi], zz, n * 256, [zk], ["yz%d" % ch])

    shown = [(0, 0)] if CFG["spay"] else []

    def send(g, t):
        near = T.cores[[r for r, h in rts[rank] if h is None][0]]
        trs, k = [], 0
        for e, (r, h) in enumerate(rts[rank]):
            d = T.cores[r] if h is None else h
            rid, pid = topo.addr(d, core)
            if h is None:
                engs, sem = topo.engines(core, d)[0:HE], T.sem["arr%d" % t]
            else:
                engs, sem = [x for x in topo.engines(core, h) if x not in topo.engines(core, near)][HE * k:HE * k + HE], T.sem["hin%d" % t]
                k += 1
            s = (3 * t + e) * PW
            trs.append(RemoteDMATransfer(dst_ids=[DstId(rid=rid, pnc=pid)], dma_engine_mask=as_mask(engs), remote_sem=sem,
                                         src=T["pay%d" % t][:, 8:8 + PW], dst=T.land[:, s:s + PW]))
        g.remote_dma_fused(trs, local_sem=T.sem["sent%d" % t])

    for t in range(RO):
        one = len(parts(t)) == 1
        pieces = [(a, b) for a, b in zip(CFG["pieces"], CFG["pieces"][1:])] if one else CH
        if not one and CFG["cutb"]:
            w = (L - CH[0][1]) // CFG["cutb"]
            pieces = ([(0, CH[0][1] // 2), (CH[0][1] // 2, CH[0][1])] if CFG["cuta"][t] else [CH[0]]) + [(CH[0][1] + w * k, CH[0][1] + w * k + w) for k in range(CFG["cutb"])]

        def ptr(s, lo, hi):
            off, ok = xl(t, s - 1 if s < 5 else 5, lo, hi)
            win = Pt[t][:, 0:Z0 + V] if 1 < s < 5 and folded(t, lo) else Pt[t][:, Z0:Z0 + V]
            gather("p%d%d_%d" % (t, s, lo), fo(s, lo, hi), win, off, hi - lo, PK[t] + ok + ["N2K"], keys("fo%d" % s, lo, hi), col("N2K"))

        def lists(s, lo, hi):
            q = 80 * (s % 2) + 160 * (s == 5)
            ps, pk = T.lb[:, q + lo // 16:q + hi // 16], keys("Blb%d" % q, lo, hi)
            mine = [p for p in parts(t) if lo <= p[0] < hi]
            more = [p for p in mine if 1 < s < 5 and folded(t, p[0])]
            items = [((T.lb[:, q + p[0] // 16:q + p[1] // 16], T.i4k[:, :], over[t, p[0]][0](s, s), False, p == more[-1], (p[1] - p[0]) // 16),
                      ["i4k", over[t, p[0]][1] + str(s)]) for p in more]
            list_set("ls%d%d_%d" % (t, s, lo), ps, lambda a: fo(s, lo + a, hi, 16), (hi - lo) // 16, keys("fo%d" % s, lo, hi), pk, "lb",
                     more=items, two=hi - lo <= 512 and CFG["two"][t][0])
            for p0, p1 in mine:
                out, ok = xl(t, s, p0, p1) if s < 5 else xl(t + 1, 0, p0, p1)
                src, n, rk = T.lb[:, q + p0 // 16:q + p1 // 16], (p1 - p0) // 16, keys("Blb%d" % q, p0, p1)
                if s == 5 and p0 == 0:
                    cp("vl", T.vl[:, :], T.lb[:, q:q + 16], 16, keys("Blb%d" % q, 0, A), ["vl"], "lb")
                if (p0, p1) in more:
                    relu("xl", out, src, lambda p0=p0, t=t: over[t, p0][2], n, rk + ["YB0", "YB1"], ok, "lb")
                else:
                    bi = "P2Z" if s < 5 and folded(t, p0) else "P2K"
                    lin("xl", out, src, 1.0, col(bi), n, rk + [bi], ok, "lb")

        for j in range(len(parts(t))):
            walk_lists(t, j, True)
        for s in range(1, 5):
            for lo, hi in pieces:
                ptr(s, lo, hi)
            for lo, hi in ([(0, L)] if CFG["joint"][t] else parts(t)):
                lists(s, lo, hi)
        walk_lists(t, 0, False)
        p1 = parts(t)[0][1]
        for lo, hi in pieces:
            if hi <= p1:
                ptr(5, lo, hi)
        n0 = p1 // 16
        up = mm("upart", [(T.xk[:, 400:416], T.sw[:, :], T.xm[:, n0 * s:n0 * s + 16], s == 0, s == 3, 16) for s in range(4)],
                ["sw", "Bxk"] + keys("xm", 0, p1), ["pup"], "xk")
        uh = lin("uph", T.uph[:, :], T.xk[:, 400:416], 0.5, col("KU"), 16, ["pup", "KU"], ["uph"], "xk")
        mm("vwide", [(T[vb][:, 0:256], T.bw[:, :], fo(5, 0, A), True, True, 256)], ["bw", "B" + vb] + keys("fo5", 0, A), ["pvw"], vb)
        lists(5, 0, p1)
        if (t, 0) in shown:
            off, ok = xl(t + 1, 0, *CH[0])
            gather("cv00", T.cv[:, 0:CH[0][1]], Ct[t][:, Z0:Z0 + V], off, CH[0][1], CK[t] + ok, ["cv0"])
        cp("vw", T.vw[:, :], T[vb][:, 0:256], 256, ["pvw"], ["vw"], vb)
        lin("vt", T.vt[:, :], T[vb][:, 0:256], 1.0, col("P2K"), 256, ["pvw", "P2K"], ["vt"], vb)
        PS, PR, PT = T.xk[:, 256:384], T.xk[:, 384:400], T.xk[:, 416:424]
        for k in range(16):
            ts("eq%d" % k, T.eq[:, 256 * k:256 * k + 256], T.vw[:, :], T.vl[:, k:k + 1], 1.0 / 256, ALU.is_equal, ALU.subtract, 256, ["vw", "vl"], ["eq%d" % k], f=0.5)
            if k % 2 == 1:
                items = [(T.xk[:, 424:432], T.eq[:, 256 * kk + h:256 * kk + 256:2], T.gm[:, GC * 144 + 15:GC * 144 + 143:16],
                          kk == 0 and h == 0, kk == 15 and h == 1, 8) for kk in (k - 1, k) for h in range(2)]
                mm("S%d" % k, items, ["gm%d" % GC, "eq%d" % (k - 1), "eq%d" % k, "pT", "pC"], ["pS0"], "xk", after=[up, uh])
        cp("st", T.st[:, 0:128:16], T.xk[:, 424:432], 8, ["pS0"], ["st"], "xk")
        mm("S", [(PS, T.st[:, :], T.i4k[:, :], True, True, 128)], ["st", "i4k"], ["pS"], "xk")
        ts("cutp", T.cutp[:, :], PS, 0.0, None, ALU.is_equal, None, 128, ["pS"], ["cutp"], "xk")
        tt("cutr", T.cutr[:, :], PS, T.pcn[:, :], ALU.min, 128, ["pS", "pcn"], ["cutr"], "xk")
        add("cum", {"v": (cv(64), lambda g: g.vector.tensor_tensor_scan(T.cum[:, :], T.cutp[:, :], T.cutp[:, :], 0.0, ALU.add, ALU.max))}, ["cutp"], ["cum"])
        tt("rr", T.rr[:, :], T.cutr[:, :], T.cum[:, :], ALU.max, 128, ["cutr", "cum"], ["rr"])
        list_set("R%d" % t, PR, lambda a: T.rr[:, a // 2:128:8], 16, ["rr"], ["pR"], "xk", two=CFG["two"][t][1])
        if t < RO - 1:
            lin("ipay", T.ipay[:, :], PR, 2.0, col("KP"), 16, ["pR", "KP"], ["ipay"], "xk")
        tt("k3", T.k3[:, :], PR, T.uph[:, :], ALU.max, 16, ["pR", "uph"], ["k3"], "xk")
        lin("itg", T.itg[:, :], T.k3[:, :], 2.0, col("KT"), 16, ["k3", "KT"], ["itg"])
        if t < RO - 1:
            tc = T.tc[:, TS_ * t:TS_ * t + TS_]
            pay = T["pay%d" % t]
            if t == 0 and CFG["spay"]:
                scatter("spay", pay[:, 16:16 + TS_], T.ipay[:, :], T.cv[:, 0:A], A, ["ipay", "cv0"], ["pay0"])
            scatter("stc%d" % t, tc, T.ipay[:, :], T.vt[:, :], A, ["ipay", "vt"], ["tc%d" % t])
            lin("tch", T.tch[:, :], T.tc[:, TS_ * t:TS_ * t + S], 1.0, col("N2K"), S, ["tc%d" % t, "N2K"], ["tch"])
            list_set("TL%d" % t, PT, lambda a: T.tch[:, a:S:16], 8, ["tch"], ["pT"], "xk", two=CFG["two"][t][1])
            pl = T.pl[:, 8 * t:8 * t + 8]
            cp("t16", T.t16[:, 8 * t:8 * t + 8], PT, 8, ["pT"], ["t16%d" % t], "xk")
            mm("cb", [(T.xk[:, 432:433], T.bw[:, :], T.cum[:, 127:128], True, True, 1)], ["bw", "cum"], ["pC"], "xk")
            ts("mark", pay[:, 8:16], T.kh[:, :], T.xk[:, 432:433], 2.0 * V, ALU.is_ge, ALU.mult, 8, ["kh", "pC"], ["mark%d" % t], "xk")
            if t > 0 or not CFG["spay"]:
                lin("pl", pl, PT, 1.0, col("P2K"), 8, ["pT", "P2K"], ["pl%d" % t], "xk")
                gather("pay%d" % t, pay[:, 16:16 + S], Ct[t][:, Z0:Z0 + CG], pl, S, CK[t] + ["pl%d" % t], ["pay%d" % t])
            add("send%d" % t, {"g": ((600.0, 0, 0, 0, 0), lambda g, t=t: send(g, t))}, ["pay%d" % t, "mark%d" % t], ["land%d" % t],
                lat=8000.0 if t == 0 else 6000.0, ext="send")
        scatter("sbn%d" % t, Pt[t + 1][:, Z0:Z0 + PS_], T.itg[:, :], T.vt[:, :], A, ["itg", "vt"], PK[t + 1])
        if not one:
            z_chain(t, 0)
            walk_lists(t, 1, False)
            for lo, hi in pieces:
                if hi > p1:
                    ptr(5, lo, hi)
            lists(5, p1, L)
        if t == 0:
            dma("cp_p2", "y", Pt[2][rows, Z0:Z0 + V], Pt[1][rows, Z0:Z0 + V], 131072, PK[1], PK[2])
        if t == 1:
            dma("cp_p3a", "y", T.nxi[:, :], Pt[2][rows, Z0:Z0 + V], 131072, PK[2], ["nxi"])
            cp("nxf", T.nxf[:, :], T.nxi[:, :], 256, ["nxi"], ["nxf"])
            dma("cp_p3", "y", Pt[3][rows, Z0:Z0 + V], T.nxf[:, :], 131072, ["nxf"], PK[3])
        for ch in range(0 if one else 1, len(CH)):
            z_chain(t, ch)
        if t < RO - 1:
            narr, PM = 0, T[mb][:, 320:320 + PW]
            items = []
            for e in range(3):
                h = rts[(rank - 1 - e) % 4][e][1]
                narr += HE if h is None else len(topo.engines(h, core))
                s, m = (3 * t + e) * PW, (e - t) % 3
                items.append((PM, T.sh[:, 128 * m:128 * m + 128], T.land[:, s:s + PW], e == 0, False, PW))
            items.append((T[mb][:, 320:328], idf, T.t16[:, 8 * t:8 * t + 8], False, True, 8))
            i = mm("merge%d" % t, items, ["land%d" % t, "sh0", "sh1", "sh2", "idp", "t16%d" % t, "B" + mb], ["pmg"], mb)
            ops[i]["ext"] = ("arr%d" % t, narr)
            arr, dl = T.arr[:, S * t:S * t + S], T.dl[:, 8 * t:8 * t + 8]
            cp("arr", arr, T[mb][:, 328:328 + S], S, ["pmg"], ["arr%d" % t], mb)
            lin("dl", dl, T[mb][:, 320:328], 1.0, col("P2K"), 8, ["pmg", "P2K"], ["dl%d" % t], mb)
            for u in range(t + 1, RO):
                scatter("sw%d%d" % (t, u), Ct[u][:, Z0:Z0 + CS], dl, arr, S, ["dl%d" % t, "arr%d" % t], CK[u])
    dma("st_n", "y", T.yn[:], T.pc[rows, Z0:Z0 + V], 131072, PK[3], ["yn"])
    if CFG["ycd"]:
        dma("cp_c", "y", T.ych[:, :], T.fo[rows, 4 * L:5 * L], 20480, keys("fo5", 0, L), ["ych"])
        lin("ycs", T.ycs[:, :], T.ych[:, :], 1.0, col("P2K"), 80, ["ych", "P2K"], ["ycs"])
    else:
        list_set("yc", T[mb][:, 320:400], lambda a: fo(5, 80 * a, 80 * a + 80), 80, keys("fo5", 0, L), ["pmg"], mb)
        lin("ycs", T.ycs[:, :], T[mb][:, 320:400], 1.0, col("P2K"), 80, ["pmg", "P2K"], ["ycs"], mb)
    dma("st_c", "y", T.yc[:], T.ycs[:, :], 40960, ["ycs"], ["yc"])
    return ops


def after(xs, x):
    lo, hi = 0, len(xs)
    while lo < hi:
        m = (lo + hi) // 2
        if xs[m] > x:
            hi = m
        else:
            lo = m + 1
    return lo


def lay(pred, succ, bank, head, hop, prio, pick):
    n = len(pred)
    left = [len(p) for p in pred]
    ready = sorted((prio[i], i) for i in range(n) if not left[i])
    start, end, eng = [0.0] * n, [0.0] * n, [None] * n
    busy, used = {e: ([], []) for e in "vstgy"}, {}
    while ready:
        _p, i = ready.pop(0)
        t0 = max([head[i]] + [end[d] + lag for d, lag in pred[i]])
        best = None
        for e, c, h in pick[i]:
            s, f = busy[e]
            t, moved = t0, True
            while moved:
                k = after(f, t)
                while k < len(s) and s[k] < t + c:
                    t = f[k] if f[k] > t else t
                    k += 1
                moved = False
                if bank[i]:
                    u = used.setdefault(bank[i], [])
                    m = after(u, (t - hop,))
                    while m < len(u) and u[m][1] - hop < t + c:
                        if u[m][2] != e and u[m][0] + hop > t:
                            t, moved = u[m][0] + hop, True
                        m += 1
            if best is None or t + c + h < best[0]:
                best = (t + c + h, t, e, c, k)
        _x, t, e, c, k = best
        busy[e][0].insert(k, t)
        busy[e][1].insert(k, t + c)
        if bank[i]:
            u.insert(after(u, (t + c,)), (t + c, t, e))
        start[i], end[i], eng[i] = t, t + c, e
        for j in succ[i]:
            left[j] -= 1
            if not left[j]:
                ready.insert(after(ready, (prio[j], j)), (prio[j], j))
    return start, end, eng


def replay(ops, order, eng, cost, hop, lf, a=0, old=None):
    free, bank, last, end, why = dict.fromkeys("vstgy", 0.0), {}, {}, [0.0] * len(ops), [None] * len(ops)
    if old:
        end, why = list(old[1]), list(old[2])
        for i in order[:a]:
            last[eng[i]] = bank[ops[i]["bank"]] = i
        for e, i in last.items():
            free[e] = end[i] - ops[i]["lat"] * lf
    for i in order[a:]:
        far, near, b, lat = ops[i]["plan"]
        e = eng[i]
        t, y, q = -hop, None, 0
        for d in far:
            if end[d] > t:
                t, y = end[d], d
        if b:
            p = bank.get(b)
            if p is not None and end[p] > t and eng[p] != e:
                t, y, q = end[p], p, 1
            bank[b] = i
        t += hop
        for d in near:
            if end[d] > t:
                t, y, q = end[d], d, 0
        if free[e] > t:
            t, y, q = free[e], last[e], 1
        t += cost[i][e]
        free[e], last[e], end[i] = t, i, t + lat * lf
        why[i] = None if y is None else (y, q)
    return max(end), end, why


PLAN = {}


def schedule(ops):
    for o in ops:
        near = [d for d in o["deps"] if "t" in o["alts"] and "t" in ops[d]["alts"]]
        o["plan"] = ([d for d in o["deps"] if d not in near], near, o["bank"], o["lat"])
    if "order" not in PLAN:
        costs = [[{e: sum(a * b for a, b in zip(c, m[0])) for e, (c, _f) in o["alts"].items()} for o in ops] for m in PLANS]
        rng = np.random.default_rng(CFG["seed"])
        n, hop = len(ops), PLANS[0][1]
        lat, bank = [o["lat"] * PLANS[0][2] for o in ops], [o["bank"] for o in ops]
        gap = lambda a, b: lat[a] + (0.0 if "t" in ops[a]["alts"] and "t" in ops[b]["alts"] else hop)
        fp, bs = [[(d, gap(d, o["i"])) for d in o["deps"]] for o in ops], [o["deps"] for o in ops]
        fs, bp = [[] for _ in ops], [[] for _ in ops]
        for o in ops:
            for d in o["deps"]:
                fs[d].append(o["i"])
                bp[d].append((o["i"], gap(d, o["i"])))

        def judge(order, eng, most=1e30, few=False, a=0, old=(None, None, None)):
            r = [replay(ops, order, eng, costs[0], PLANS[0][1], PLANS[0][2], a, old[0])]
            if r[0][0] > most or few:
                return (1e30 if r[0][0] > most else r[0][0]), r
            r += [replay(ops, order, eng, costs[j], PLANS[j][1], PLANS[j][2], a, old[j]) for j in (1, 2)]
            return (2 * r[0][0] + r[1][0] + r[2][0]) / 4, r

        links = [i for i in range(n) if "link" in ops[i]]
        full = {i: [c[ops[i]["link"][0]]["t"] for c in costs] for i in links}

        def relink(i, e):
            for j, c in enumerate(costs):
                c[ops[i]["link"][0]]["t"] = full[i][j] - (ops[i]["link"][1] * PLANS[j][0][4] if e == "v" else 0.0)

        def both(prio, hand):
            for i in links:
                relink(i, "v" if hand[i] < 0 else "s")
            pick = [[(e, c, hand[i] * c if e == "v" else 0.0) for e, c in costs[0][i].items() if i not in full or (e == "v") == (hand[i] < 0)]
                    for i in range(n)]
            _s, f, eng = lay(fp, fs, bank, [0.0] * n, hop, prio, pick)
            fixed = [[(eng[i], costs[0][i][eng[i]], 0.0)] for i in range(n)]
            _s, f, _e = lay(bp, bs, bank, lat, hop, [-(f[i] + lat[i]) for i in range(n)], fixed)
            s, _f, eng = lay(fp, fs, bank, [0.0] * n, hop, [-x for x in f], pick)
            return s, eng

        rank = [0.0] * n
        for i in range(n - 1, -1, -1):
            rank[i] = min(costs[0][i].values()) + max([lat[i]] + [rank[j] + lag for j, lag in bp[i]])
        prio, h0 = -np.array(rank), CFG["hand"]
        hand = np.array([-h0 if o["n"][:2] == "sg" else h0 for o in ops])
        hand[links] *= np.where(rng.random(len(links)) < CFG["byv"], -1.0, 1.0)
        best = score = None
        for it in range(CFG["iters"]):
            p, h = prio.copy(), hand.copy()
            if it:
                k = rng.random(n) < rng.choice([0.02, 0.1, 0.5])
                p[k] += rng.normal(0.0, 600.0 * rng.choice([0.3, 1.0, 3.0]), int(k.sum()))
                k = rng.random(n) < 0.005
                h[k] = rng.normal(0.0, h0, int(k.sum()))
            s, eng = both(p.tolist(), h.tolist())
            order = sorted(range(n), key=lambda i: (s[i], i))
            s2, r = judge(order, eng)
            if score is None or s2 <= score + 400.0 * (1 - it / CFG["iters"]) * rng.random() ** 2:
                score, prio, hand = s2, np.array(s), h
            if best is None or s2 < best[0]:
                best = (s2, order, eng, r)

        def waits(r):
            out = []
            for m, end, why in r:
                i = end.index(m)
                while why[i] is not None:
                    if why[i][1]:
                        out.append((i, why[i][0]))
                    i = why[i][0]
            return out

        order, eng = best[1:3]
        dear = [i for i in range(n) if len(costs[0][i]) > 1 and max(costs[0][i].values()) > min(costs[0][i].values()) + 50.0]
        dear += links
        for many, heat, few in CFG["polish"]:
            for i in links:
                relink(i, eng[i])
            score, r = judge(order, eng, few=few)
            best, cand = (score, order, eng), waits(r)
            for it, (u0, u, u2, u3) in enumerate(rng.random((many, 4)).tolist()):
                if it % 200 == 0:
                    order = sorted(order, key=lambda i: r[0][1][i] - lat[i] - costs[0][i][eng[i]])
                    score, r = judge(order, eng, few=few)
                    cand = waits(r)
                i, p = cand[int(u0 * len(cand))]
                o2, e2 = order, eng
                j = dear[int(u0 * len(dear))] if u < 0.05 else p if u < 0.2 else i
                if u < 0.3 and len(ops[j]["alts"]) > 1:
                    e2, a = list(eng), order.index(j)
                    e2[j] = [e for e in ops[j]["alts"] if e != eng[j]][0]
                    if j in full:
                        relink(j, e2[j])
                        a = min(a, order.index(ops[j]["link"][0]))
                else:
                    a, b = order.index(p), order.index(i)
                    seg, ahead = order[a:b + 1], u2 < 0.5
                    need = {i if ahead else p}
                    for x in (reversed(seg) if ahead else seg):
                        if x in need:
                            need.update(bs[x] if ahead else fs[x])
                    if p in need and i in need:
                        continue
                    o2 = order[:a] + [x for x in seg if (x in need) == ahead] + [x for x in seg if (x in need) != ahead] + order[b + 1:]
                h = heat * (1 - it / many)
                s2, r2 = judge(o2, e2, r[0][0] + 300.0 + h, few, a, r)
                if s2 + CFG["thrift"] * (costs[0][j][e2[j]] - costs[0][j][eng[j]]) <= score - 0.3 * h * math.log(u3 + 1e-12):
                    score, order, eng, r = s2, o2, e2, r2
                    cand = waits(r)
                    if score < best[0]:
                        best = (score, order, eng)
                elif j in full:
                    relink(j, eng[j])
            order, eng = best[1:3]
        for i in links:
            relink(i, eng[i])
        PLAN["order"], PLAN["eng"], PLAN["val"] = order, eng, [x[0] for x in judge(order, eng)[1]]
    for o, e in zip(ops, PLAN["eng"]):
        o["e"] = e
    return PLAN["order"]


def emit(g, T, ops, order):
    queue = {"v": g.vector, "s": g.scalar, "t": g.tensor, "g": g, "y": g.sync}
    sem = {"v": "nv", "s": "ns", "t": "nt", "g": "ng"}
    count = {"v": 0, "s": 0, "t": 0, "g": 0}
    seen = {e: {} for e in queue}
    last_bank, tail, ndma = {}, {}, [0]

    def wait(e, name, val):
        if seen[e].get(name, 0) < val:
            queue[e].wait_ge(T.sem[name], val)
            seen[e][name] = val

    for i in order:
        o = ops[i]
        e = o["e"]
        deps = list(o["deps"])
        if o["bank"]:
            if o["bank"] in last_bank and ops[last_bank[o["bank"]]]["e"] != e:
                deps.append(last_bank[o["bank"]])
            last_bank[o["bank"]] = i
        need = {}
        for d in deps:
            p = ops[d]
            if p["ext"] == "send" or (e == "t" and p["e"] == "t"):
                continue
            name, val = p["tok"]
            need[name] = max(need.get(name, 0), val)
        for name in sorted(need):
            wait(e, name, need[name])
        if o["ext"] and o["ext"] != "send":
            wait(e, o["ext"][0], o["ext"][1])
        ins = o["alts"][e][1](g)
        if o["ext"] == "send":
            continue
        if o["dma"]:
            name = "dq%d" % ndma[0]
            ndma[0] += 1
            ins.then_inc(T.sem[name], 16)
            o["tok"] = (name, 16)
        else:
            count[e] += 1
            ins.then_inc(T.sem[sem[e]], 1)
            o["tok"] = (sem[e], count[e])
        tail[o["tok"][0]] = o["tok"][1]
    for t in range(RO - 1):
        wait("g", "sent%d" % t, 3 * HE)
    for name in sorted(tail):
        if max(seen[e].get(name, 0) for e in queue) < tail[name]:
            wait("y", name, tail[name])


def rank_program(g, core, T, topo):
    rank = T.rank_of(core)
    if rank is None:
        for row in routes(T, topo):
            for e, (r, h) in enumerate(row):
                if h == core:
                    helper_program(g, core, T, topo, e, r)
        return
    ops = build(T, topo, core, rank)
    emit(g, T, ops, schedule(ops))
